import numpy as np, ml_dtypes
CORES = [25,29,65,69,153,157,193,197]
N = 8
BF = ml_dtypes.bfloat16
def gentries(a):
    return np.ascontiguousarray(a.reshape(8, 16, -1).transpose(0, 2, 1)).reshape(8, -1)
def gtable(e):
    e = np.asarray(e); return np.ascontiguousarray(e.reshape(8, -1, 16).transpose(0, 2, 1)).reshape(128, -1).astype(np.int32)
NL, H, L, K, S, RO = 2048, 1024, 64, 16, 3, 5
MT = [12, 18, 14, 22, 16]
AT = [10, 8, 9, 6, 8]
def own(rng, c):
    return np.take_along_axis(c, rng.integers(0, K, (N, 8, 1, L)), 2)[:, :, 0]
def parts(rng):
    v = rng.integers(0, 256, (N, 8, 16, NL))
    g = 2 * np.argsort(rng.random((N, 8, 16, H)), axis=-1) + rng.integers(0, 2, (N, 8, 16, H))
    c = rng.integers(0, NL, (N, 8, K, L)); d = rng.integers(0, NL, (N, 8, K, L))
    return v, g, c, d, own(rng, c)
def pack(v, g, c, d, l):
    return {"val": np.ascontiguousarray(v.reshape(N, 128, NL)).astype(np.float32).astype(BF), "gen": np.ascontiguousarray(g.reshape(N, 128, H)).astype(np.int32),
            "cla": np.stack([gtable(a.reshape(8, -1)) for a in c]), "par": np.stack([gtable(a.reshape(8, -1)) for a in d]), "lit": np.stack([gtable(a) for a in l])}
def setup_inputs(rng):
    return pack(*parts(rng))
def setup_inputs_corners(rng):
    v, g, c, d, l = parts(rng)
    top = rng.random((N, 8, 1, NL)) < 1.0 / K
    v = np.where(top, rng.choice(np.array([222, 223, 224, 240, 255]), v.shape), rng.choice(np.array([0, 1, 31, 32, 33, 100]), v.shape))
    v[0, 6] = 0; v[1, 6] = 255
    g[:, 0, 3] = 2 * np.arange(H); g[:, 0, 15] = 2 * np.arange(H) + 1
    g[:, 1] = g[:, 1, :1].copy(); g[:, 2, ::4] = 0; g[:, 2, 1::4] = NL - 1
    c[..., 0::5] = d[..., 0::5]
    c[..., 1::5] = c[:, :, :1, 1::5].copy()
    c[:, :, 1::2, 2::5] = c[:, :, 0::2, 2::5] ^ 1
    e = c[..., 3::5]; c[..., 3::5] = rng.choice(np.array([0, 1, NL - 2, NL - 1]), e.shape)
    l[..., 0::3] = 0; l[..., 1::3] = NL - 1; l[..., 2::3] = c[:, :, K - 1, 2::3]
    return pack(v, g, c, d, l)
def setup_inputs_crowd(rng):
    v, g, c, d, l = parts(rng)
    for q in range(N):
        for s in range(8):
            w = 2 * rng.permutation(H)[:2 * K] + rng.integers(0, 2, 2 * K); c[q, s] = w[:K, None]; d[q, s] = w[K:, None]
            j = 15 if s == 7 else int(rng.integers(0, 16)); k = K - 1 if s == 0 else int(rng.integers(0, K))
            im = g[q, s, j, w[:K] >> 1] ^ (w[:K] & 1); both = np.concatenate([im, im ^ 1])
            v[q, s][:, both] = np.minimum(v[q, s][:, both], 100); v[q, s][:, im[k]] = 255; l[q, s] = im[k]
            if s in (2, 5):
                turn = rng.random(L) < 0.5; c[q, s] = np.where(turn, c[q, s] ^ 1, c[q, s]); v[q, s][:, im[k] ^ 1] = 255
            if s & 1:
                o = 0 if s == 1 else L - 1 if s == 7 else int(rng.integers(0, L))
                c[q, s, :, o] = int(c[q, s, 0, o]); d[q, s, :, o] = int(d[q, s, 0, o])
    return pack(v, g, c, d, l)
def endclauses(rng):
    E = np.array([0, NL - 1]); sh = (N, 8, 1, L); b = rng.integers(0, 2, sh); x = E[b]; y = E[1 - b]; kind = rng.integers(0, 4, sh)
    k1 = rng.integers(0, K, sh); k2 = (k1 + rng.integers(1, K, sh)) % K; k = np.arange(K).reshape(1, 1, K, 1)
    c = np.where(k == k1, y, x); c = np.where((kind == 2) & (k == k2), x ^ 1, c)
    return np.where(kind == 3, E[rng.integers(0, 2, (N, 8, K, L))], c)
def setup_inputs_ends(rng):
    E = np.array([0, NL - 1]); v = 255 * rng.integers(0, 2, (N, 8, 16, NL)); g = E[rng.integers(0, 2, (N, 8, 16, H))]
    c = endclauses(rng); d = endclauses(rng); l = E[rng.integers(0, 2, (N, 8, L))]
    for o, k in ((0, 0), (L - 1, K - 1)):
        c[:, :, :, o] = NL - 1; c[:, :, k, o] = 0
    h = (np.arange(16) < 8).astype(np.int64); on = np.ones(16, np.int64); no = 0 * on
    for q in range(N):
        for s in range(8):
            ty = (3 * q + s) % 6
            if q == N - 1 and s == 7: ty = 0
            if q in (0, 2) and s == 6: ty = 6
            four = [[on, no, no, on], [no, on, on, no], [h, no, no, 1 - h], [no, h, 1 - h, no], list(rng.integers(0, 2, (4, 16))), [on, no, no, on], [on, no, no, no]][ty]
            four = np.stack(four)
            if ty == 5: four[:, 13:] = rng.integers(0, 2, (4, 3))
            if ty == 6: g[q, s, :2, 0] = NL - 1; g[q, s, 2:, 0] = 0
            v[q, s][:, [0, 1, NL - 2, NL - 1]] = 255 * four.T
    return pack(v, g, c, d, l)
def setup_inputs_spread(rng):
    v, g, c, d, l = parts(rng)
    v = np.minimum((1.1 * np.exp2(8 * rng.random((N, 8, 1, NL))) * rng.random((N, 8, 16, NL))).astype(np.int64), 255)
    v[:, 1::2] = np.minimum((256 * rng.random((N, 4, 16, NL)) ** np.exp2(rng.integers(-1, 3, (N, 4, 16, 1)))).astype(np.int64), 255)
    g[:, :, ::2] = 2 * np.minimum((H * rng.random((N, 8, 8, H)) ** 3).astype(np.int64), H - 1) + rng.integers(0, 2, (N, 8, 8, H))
    p = rng.choice(np.array([1, 2, 4]), (N, 8, 1, 1))
    c = np.minimum((NL * rng.random((N, 8, K, L)) ** p).astype(np.int64), NL - 1); d = NL - 1 - np.minimum((NL * rng.random((N, 8, K, L)) ** p).astype(np.int64), NL - 1)
    l = np.where(rng.random((N, 8, L)) < 0.5, own(rng, c), own(rng, d))
    return pack(v, g, c, d, l)
def apart(rng, v, g, c, d, l, s, one):
    w = rng.permutation(H); z = 2 * w[:L] + rng.integers(0, 2, L); r = w[L:]; m = np.zeros(H, np.int64)
    m[z >> 1] = np.roll(z, -1) ^ (z & 1); m[r] = 2 * rng.permutation(r) + rng.integers(0, 2, H - L); g[:, s, 0] = m
    v[:, s] = np.minimum(v[:, s], 100); v[:, s][:, :, z] = 255; v[:, s][:, :, z ^ 1] = rng.integers(200, 256, (N, 16, L))
    c[:, s] = 2 * r[rng.integers(0, H - L, (N, K, L))] + rng.integers(0, 2, (N, K, L))
    for q in range(N):
        y = rng.permutation(z); c[q, s, rng.integers(0, K, L), np.arange(L)] = y; l[q, s] = y
        if one:
            o = L - 1 if q == N - 1 else int(rng.integers(0, L))
            c[q, s, :, o] = int(c[q, s, 0, o]); d[q, s, :, o] = int(d[q, s, 0, o])
def setup_inputs_ties(rng):
    v, g, c, d, l = parts(rng); m = np.array(MT)[np.arange(8) % RO].reshape(1, 8, 1, 1); u = K * rng.random((N, 8, 1, NL))
    low = (rng.random(v.shape) * (255 - m)).astype(np.int64)
    w = np.where(u < 1, 255, np.where(u < 1.3, 255 - m, np.where(u < 4, 254 - m, low)))
    v = np.where(rng.random(v.shape) < 0.02, v, w)
    h = (np.arange(16) < 8).astype(np.int64).reshape(16, 1); x = u[:, [2, 5]]
    v[:, [2, 5]] = np.where(x < 1, 255 * h, np.where(x < 2, 255 * (1 - h), np.minimum(low[:, [2, 5]], 100)))
    eq = rng.random((N, 8, 1, H)) < 0.25; v[..., 1::2] = np.where(eq, v[..., 0::2], v[..., 1::2])
    apart(rng, v, g, c, d, l, 6, False); apart(rng, v, g, c, d, l, 7, True)
    return pack(v, g, c, d, l)
def check_inputs(d):
    bad = []
    for k, lo, hi in (("val", 0, 255), ("gen", 0, NL - 1), ("cla", 0, NL - 1), ("par", 0, NL - 1), ("lit", 0, NL - 1)):
        a = np.asarray(d[k]).astype(np.float64)
        if not (np.min(a) >= lo and np.max(a) <= hi): bad.append("range of " + k)
        elif np.any(a != np.floor(a)): bad.append("whole numbers of " + k)
    return bad
def reference(val, gen, cla, par, lit):
    V = val.astype(np.float32).astype(np.int16).reshape(N, 8, 16, NL)
    e = gen.astype(np.int64).reshape(N, 8, 16, H); P = np.stack([e, e ^ 1], axis=-1).reshape(N, 8, 16, NL)
    C = np.stack([gentries(a) for a in cla]).astype(np.int64).reshape(N, 8, K, L); D = np.stack([gentries(a) for a in par]).astype(np.int64).reshape(N, 8, K, L)
    l = np.stack([gentries(a) for a in lit]).astype(np.int64); A = np.zeros((N, 8), np.int64)
    for t in range(RO):
        if t: C = np.roll(C, S, axis=0); D = np.roll(D, S, axis=0); l = np.roll(l, S, axis=0)
        for a in range(N):
            v = V[a]; x = l[a][:, None, :]
            less = np.take_along_axis(v, x, 2) < np.take_along_axis(v, x ^ 1, 2)
            c = np.where((np.add.reduce(less.astype(np.int64), axis=1) >= 9)[:, None, :], D[a], C[a])
            img = np.take_along_axis(P[a], c.reshape(8, 1, K * L), 2)
            w = np.take_along_axis(v, img.reshape(8, 1, 16 * K * L), 2).reshape(8, 16, 16, K, L)
            near = w >= np.max(w, axis=3)[:, :, :, None] - MT[t]
            unit = np.add.reduce(near, axis=3, dtype=np.int16) == 1
            votes = np.add.reduce(unit.astype(np.int64), axis=1); js = np.argmax(votes, axis=1)
            pro = np.max(votes, axis=1) >= (AT[t] + (A[a] & 1))[:, None]
            new = np.take_along_axis(img.reshape(8, 16, K, L), js[:, None, None, :], 1)[:, 0]
            un = np.take_along_axis(unit, js[:, None, None, :], 2)[:, :, 0]
            vn = np.take_along_axis(v, new.reshape(8, 1, K * L), 2).reshape(8, 16, K, L).astype(np.int64)
            ks = np.argmax(np.add.reduce(np.where(un[:, :, None, :], vn, 0), axis=1), axis=1)
            nl = np.take_along_axis(new, ks[:, None, :], 1)[:, 0]
            C[a] = np.where(pro[:, None, :], new, D[a]); D[a] = c; l[a] = np.where(pro, nl, l[a])
            for g in range(8):
                z = nl[g, np.flatnonzero(pro[g])]
                z = z[np.unique(z >> 1, return_index=True)[1]]
                up = np.minimum(v[g][:, z] + 32, 255); down = np.maximum(v[g][:, z ^ 1] - 32, 0)
                v[g][:, z] = up; v[g][:, z ^ 1] = down
            A[a] = np.add.reduce(pro.astype(np.int64), axis=1)
    return {"yv": V.reshape(N, 128, NL).astype(np.float32).astype(BF), "yc": np.stack([gtable(a.reshape(8, -1)) for a in C]).astype(np.float32),
            "yd": np.stack([gtable(a.reshape(8, -1)) for a in D]).astype(np.float32), "yl": np.stack([gtable(a) for a in l]).astype(np.float32)}

@@ -1,0 +1,578 @@
+from concourse.mybir import dt, AluOpType, AxisListType, ActivationFunctionType
+
+A_ = AluOpType
+F = ActivationFunctionType
+X_ = AxisListType.X
+NR_ = 5
+BAT = {"A": (0, 32), "B": (32, 32)}
+NV = 8
+PRE = 8
+MAGIC = 12582912.0
+
+_SIZE = {"float32": 4, "int32": 4, "uint16": 2, "float16": 2, "bfloat16": 2}
+SCRATCH = {}
+for _d, _names in (("int32", "GEN 1024 CW0 64 CW 64 PI 8 XC 64 XD 64 XL 4 LT0 4 LT1 4 TI 2"),
+                   ("float32", "GM 1024 PM 1024 PT 2048 IFB 512 K1 1024 K2 1024 B64 64 PENC 64 LMT 192 PC 16 DC 64 Z 128 ZT 128 "
+                               "Z2 128 ZT2 128 FX 64 FX2 64 YC 64 YD 64 YL 4 PREP 64 THR 4"),
+                   ("bfloat16", "VAL 2176 W 16384 U 1024 UX 1024 PR 1024 MSK 256 MKK 512 ONE 128 BO 128 B1 128 BOV 128 BOS 128 IDN 128 "
+                                "E0 128 SL0 2048 JT 512 A16 512 OHT 512 PRO 64 NP 64"),
+                   ("float16", "IFA 512 MK 1024 BOH 128 IDH 128 SEL 2048"), ("uint16", "IMG 1024")):
+    _w = _names.split()
+    for _i in range(0, len(_w), 2):
+        SCRATCH[_w[_i]] = ("sbuf", [128, int(_w[_i + 1])], _d)
+for _i in (0, 1):
+    SCRATCH["SB%d" % _i] = ("sbuf", [128, 257, 16], "bfloat16")
+    SCRATCH["YB%d" % _i] = ("sbuf", [128, 256, 16], "bfloat16")
+for _n in "psD0 psD1 psV0 psV1 psS psN psR".split():
+    SCRATCH[_n] = ("psum", [128, 512], "float32")
+SEMAPHORES = "vc sc tc gc ls ld0 ld1 ld2 ld3 ld4 st0 st1 st2 st3".split()
+_POS = {}
+
+
+def _declare():
+    tot = {}
+    for b, (a0, n) in BAT.items():
+        nq = n // 16
+        for t in range(NR_):
+            SCRATCH["i%s%d" % (b, t)] = ("sbuf", [128, 2 * n + 2 * nq], "float16")
+            SCRATCH["o%s%d" % (b, t)] = ("sbuf", [128, 2 * n + 2 * nq], "float16")
+            if t:
+                SEMAPHORES.append("a%s%d" % (b, t))
+        for d, names in (("uint16", (("LL", 2 * nq), ("CU", n), ("LU", n), ("LW", n), ("EL", 2 * nq))),
+                         ("bfloat16", (("XV", 2 * n), ("LE", n), ("ZE", 2 * n))),
+                         ("int32", (("KI", n), ("QI", n), ("WI", n), ("K2I", n), ("KR", n))),
+                         ("float16", (("PEN", n), ("NCG", n), ("XX", n))),
+                         ("float32", (("DMC", n), ("FL", n), ("T2", n), ("NM", nq), ("DN", n), ("OHK", n), ("DM", n), ("NL", 2 * nq),
+                                      ("PCL", nq), ("EQ", 64 * nq), ("EM", 64 * nq), ("DV", 2 * nq), ("FP", nq),
+                                      ("OL", 2 * nq), ("YE", 2 * n), ("KP", 2 * nq), ("DL", 2 * nq), ("DK", 2 * nq)))):
+            for nm, w in names:
+                al = 64 // _SIZE[d]
+                _POS[nm + b] = ("pk_" + d, tot.get(d, 0), w)
+                tot[d] = tot.get(d, 0) + (w + al - 1) // al * al
+    for d in tot:
+        SCRATCH["pk_" + d] = ("sbuf", [128, tot[d]], d)
+
+
+_declare()
+
+
+def _route(r, T, topo):
+    s, d = T.cores[r], T.cores[(r + 3) % len(T.cores)]
+    if topo.may_write(s, d):
+        return s, None, d
+    own = [c for c in topo.cores_of(s) if c not in T.cores and topo.may_write(c, d)]
+    own.sort(key=lambda c: (topo.die(c) != topo.die(s), c))
+    return s, own[0], d
+
+
+def _mask(src, dst, topo):
+    e = topo.engines(src, dst)[:8]
+    return sum(1 << x for x in e), len(e)
+
+
+def _send(g, T, topo, core, dst, src_ap, name, sem):
+    rid, pid = topo.addr(dst, core)
+    m, k = _mask(core, dst, topo)
+    g.remote_dma(T[name][:], src_ap, T.sem[sem], T.sem["ls"], pid, rid, m)
+    return k
+
+
+def _relay(g, core, T, topo):
+    for r in range(len(T.cores)):
+        s, h, d = _route(r, T, topo)
+        if h != core:
+            continue
+        tot = 0
+        for t in range(1, NR_):
+            for b in BAT:
+                nm, sem = "i%s%d" % (b, t), "a%s%d" % (b, t)
+                g.wait_ge(T.sem[sem], _mask(s, h, topo)[1])
+                tot += _send(g, T, topo, core, d, T[nm][:], nm, sem)
+        g.wait_ge(T.sem["ls"], tot)
+
+
+def _weave(a, c, x0=0.0):
+    L, k = [], 0
+    for i, f in enumerate(a):
+        L.append(f)
+        want = int(max(((i + 1) / len(a) - x0) / (1.0 - x0), 0.0) * len(c) + 1e-6)
+        L += c[k:want]
+        k = max(k, want)
+    return L + c[k:]
+
+
+def _go(L):
+    for f in L:
+        f()
+
+
+def rank_program(g, core, T, topo):
+    rank = T.rank_of(core)
+    if rank is None:
+        return _relay(g, core, T, topo)
+    MT, AT = (12, 18, 14, 22, 16), (10, 8, 9, 6, 8)
+    eng = {"v": g.vector, "s": g.scalar, "t": g.tensor, "g": g, "y": g.sync}
+    cnt, total, hist = {}, {}, {}
+    known = {q: {} for q in eng}
+    V, S, TE = g.vector, g.scalar, g.tensor
+
+    def need(q, reads, writes):
+        w = {}
+        for keys, wr in ((reads, False), (writes, True)):
+            for (key, c0, c1) in keys:
+                for h in hist.get(key, ()):
+                    if h[0] >= c1 or c0 >= h[1] or h[3] == q == "t":
+                        continue
+                    if not (wr or h[2] or (key[:2] == "ps" and h[3] != q)):
+                        continue
+                    s, n = h[4]
+                    w[s] = max(w.get(s, 0), n)
+        for s in w:
+            if known[q].get(s, 0) < w[s]:
+                eng[q].wait_ge(T.sem[s], w[s])
+                known[q][s] = w[s]
+
+    def note(q, reads, writes, ev):
+        for keys, wr in ((reads, False), (writes, True)):
+            for (key, c0, c1) in keys:
+                L = hist.setdefault(key, [])
+                if wr:
+                    L[:] = [h for h in L if not (c0 <= h[0] and h[1] <= c1)]
+                else:
+                    L[:] = [h for h in L if h[2] or h[3] != q or not (c0 <= h[0] and h[1] <= c1)]
+                L.append((c0, c1, wr, q, ev))
+
+    def op(q, fn, reads, writes):
+        need(q, reads, writes)
+        sem = q + "c"
+        total[sem] = cnt[q] = cnt.get(q, 0) + 1
+        fn().then_inc(T.sem[sem], 1)
+        note(q, reads, writes, (sem, cnt[q]))
+
+    def dma(q, o, i, reads, writes, sem):
+        need(q, reads, writes)
+        eng[q].dma_start(o, i).then_inc(T.sem[sem], 16)
+        total[sem] = 16
+        note("dma" + sem, reads, writes, (sem, 16))
+
+    def B(name, c0=0, c1=None, st=1):
+        base, off, w = _POS[name] if name in _POS else (name, 0, SCRATCH[name][1][1])
+        c1 = w if c1 is None else c1
+        ap = T[base][:, off + c0:off + c1] if st == 1 else T[base][:, off + c0:off + c1:st]
+        return ap, ((base, 0, 512) if base[:2] == "ps" else (base, off + c0, off + c1))
+
+    def vcopy(o, i):
+        op("v", lambda: V.tensor_copy(o[0], i[0]), [i[1]], [o[1]])
+
+    def vgat(o, win, off):
+        op("v", lambda: V.tensor_copy(o[0], win[0].indirect(off[0])), [win[1], off[1]], [o[1]])
+
+    def sgat(o, win, off):
+        op("s", lambda: S.activation(o[0], win[0].indirect(off[0]), F.Copy), [win[1], off[1]], [o[1]])
+
+    def act(o, i, scale, bias, f=F.Copy):
+        op("s", lambda: S.activation(o[0], i[0], f, bias=bias, scale=scale), [i[1]], [o[1]])
+
+    def tt(o, a, b, f):
+        op("v", lambda: V.tensor_tensor(o[0], a[0], b[0], f), [a[1], b[1]], [o[1]])
+
+    def ttg(o, win, off, b, f):
+        op("v", lambda: V.tensor_tensor(o[0], win[0].indirect(off[0]), b[0], f), [win[1], off[1], b[1]], [o[1]])
+
+    def ts(o, a, s1, f1, s2=None, f2=None):
+        rd = [a[1]] + [s[1] for s in (s1, s2) if isinstance(s, tuple)]
+        x1 = s1[0] if isinstance(s1, tuple) else s1
+        x2 = s2[0] if isinstance(s2, tuple) else s2
+        if f2 is None:
+            op("v", lambda: V.tensor_scalar(o[0], a[0], x1, None, f1), rd, [o[1]])
+        else:
+            op("v", lambda: V.tensor_scalar(o[0], a[0], x1, x2, f1, f2), rd, [o[1]])
+
+    def lin(b, o, i, scale, bias):
+        if b == "B":
+            act(o, i, scale, bias)
+        else:
+            ts(o, i, scale, A_.mult, bias, A_.add)
+
+    def red(o, a, f):
+        op("v", lambda: V.tensor_reduce(o[0], a[0], X_, f), [a[1]], [o[1]])
+
+    def ms(o, c):
+        op("v", lambda: V.memset(o[0], c), [], [o[1]])
+
+    def mm(o, l, r, st, sp):
+        op("t", lambda: TE.matmul(o[0], l[0], r[0], st, sp), [l[1], r[1]], [o[1]])
+
+    def iota(o, pat, base, ch, whole=False):
+        if whole:
+            op("g", lambda: g.iota(o[0], pat, base, ch), [], [o[1]])
+        else:
+            op("g", lambda: g.iota(o[0], pat, base, ch, allow_small_or_imprecise_dtypes=True), [], [o[1]])
+
+    def asel(o, i, pat, f, base, ch):
+        op("g", lambda: g.affine_select(o[0], i[0], pat, f, 0.0, base, ch), [i[1]], [o[1]])
+
+    for q, nm, c1, src, sem in (("s", "GEN", 1024, T.gen, "ld3"), ("y", "XC", 64, T.cla, "ld0"), ("y", "XD", 64, T.par, "ld1"),
+                                ("y", "XL", 4, T.lit, "ld2"), ("y", "VAL", 2048, T.val, "ld4")):
+        o = B(nm, 0, c1)
+        dma(q, o[0], src[:], [], [o[1]], sem)
+
+    iota(B("PI", 0, 1), [[1, 1]], 0, 1, True)
+    ms(B("ONE"), 1.0)
+    asel(B("B1"), B("ONE"), [[-16, 8], [0, 16]], A_.is_ge, 0, 1)
+    asel(B("BO"), B("B1"), [[16, 8], [0, 16]], A_.is_ge, 15, -1)
+    asel(B("IDN"), B("ONE"), [[-1, 128]], A_.is_equal, 0, 1)
+    asel(B("E0"), B("ONE"), [[0, 128]], A_.is_equal, 0, 1)
+    iota(B("JT"), [[0, 32], [1, 16]], 0, 0)
+    iota(B("A16"), [[16, 32], [0, 16]], 0, 0)
+    iota(B("CW0"), [[240, 64]], 0, 0, True)
+    iota(B("B64"), [[1, 64]], 0, 0)
+    iota(B("PENC"), [[2, 64]], 2048, 0)
+    ms(B("VAL", 2048, 2176), 0.0)
+    ts(B("PI", 1, 2), B("PI", 0, 1), 15, A_.bitwise_and)
+    ts(B("PI", 2, 3), B("PI", 0, 1), 16, A_.bitwise_and)
+    ms(B("DC", 0, 32), 32.0)
+    vcopy(B("PC", 0, 1), B("PI", 1, 2))
+    ts(B("PC", 1, 2), B("PI", 2, 3), 0.0, A_.is_equal)
+    ts(B("PC", 2, 3), B("PI", 2, 3), 16.0, A_.is_equal)
+    ts(B("PC", 3, 4), B("PC", 0, 1), 16.0, A_.mult)
+    for q in range(4):
+        ts(B("PC", 4 + q, 5 + q), B("PC", 0, 1), 16.0 * q, A_.add)
+    for q in range(4):
+        ts(B("PC", 8 + q, 9 + q), B("PC", 4 + q, 5 + q), 2.0, A_.mult, 2048.0, A_.add)
+    for p in (0, 1):
+        op("v", lambda p=p: V.memset(T["SB%d" % p][:, 0, :], 0.0), [], [("SB%d.%d" % (p, j), 0, 1) for j in range(16)])
+    ms(B("DC", 32, 64), -32.0)
+    ms(B("THR", 2, 3), -1024000.0 * (AT[0] - 1) - 500.0)
+    ms(B("THR", 3, 4), 1024000.0 * (AT[0] - 1) + 500.0)
+    ms(B("MSK"), 1.0)
+    ms(B("MKK"), 1.0)
+
+    def flip(q_, Z, ZT, src, dst):
+        def blocks():
+            for q in range(4):
+                for h in range(2):
+                    o, i, m = B(Z, 32 * q + 16 * h, 32 * q + 16 * h + 16), src(q), B("PC", 1 + h, 2 + h)
+                    if q_ == "s":
+                        op("s", lambda: S.activation(o[0], i[0], F.Copy, scale=m[0]), [i[1], m[1]], [o[1]])
+                    else:
+                        ts(o, i, m, A_.mult)
+
+        def turn():
+            a, b = B(Z), B(ZT)
+            op("v", lambda: V.transpose(b[0], a[0]), [a[1]], [b[1]])
+        return [blocks, turn] + [lambda q=q: tt(dst(q), B(ZT, 32 * q, 32 * q + 16), B(ZT, 32 * q + 16, 32 * q + 32), A_.add)
+                                 for q in range(4)]
+
+    def lane16(pre, t, part):
+        def f(q):
+            b = "A" if 16 * q < BAT["B"][0] else "B"
+            c = part * BAT[b][1] + 16 * q - BAT[b][0]
+            return B("%s%s%d" % (pre, b, t), c, c + 16)
+        return f
+
+    vcopy(B("FX"), B("XC"))
+    fc = flip("s", "Z", "ZT", lambda q: B("FX", q, 64, 4), lane16("i", 0, 0))
+    fd = flip("v", "Z2", "ZT2", lambda q: B("FX2", q, 64, 4), lane16("i", 0, 1))
+    fc[0]()
+    vcopy(B("FX2"), B("XD"))
+    HF = ((0, 512), (512, 1024))
+    for c0, c1 in HF:
+        vcopy(B("PT", 2 * c0, 2 * c1, 2), B("GEN", c0, c1))
+    for i, (c0, c1) in enumerate(HF):
+        act(B("PM", c0, c1), B("PT", 2 * c0, 2 * c1, 2), 0.49994, MAGIC)
+        act(B("psD%d" % i), B("PM", c0, c1), 4.0, -4.0 * MAGIC)
+    _go(fc[1:2])
+    ts(B("GM", 0, 512), B("GEN", 0, 512), 1.0, A_.subtract)
+    _go(fc[2:])
+    ts(B("GM", 512, 1024), B("GEN", 512, 1024), 1.0, A_.subtract)
+    _go(fd)
+    ts(B("LT0"), B("XL"), 1, A_.bitwise_and)
+    for b in BAT:
+        a0, n = BAT[b]
+        vcopy(B("i%s0" % b, 2 * n, 2 * n + n // 16), B("XL", a0 // 16, (a0 + n) // 16))
+    ts(B("LT1"), B("LT0"), -2.0, A_.mult, 1.0, A_.add)
+    tt(B("PT", 1, 1024, 2), B("psD0"), B("GM", 0, 512), A_.subtract)
+    for b in BAT:
+        a0, n = BAT[b]
+        q0, nq = a0 // 16, n // 16
+        tt(B("i%s0" % b, 2 * n + nq, 2 * n + 2 * nq), B("XL", q0, q0 + nq), B("LT1", q0, q0 + nq), A_.add)
+    tt(B("PT", 1025, 2048, 2), B("psD1"), B("GM", 512, 1024), A_.subtract)
+
+    def late_constants():
+        ms(B("SL0"), 1.0)
+        asel(B("SL0"), B("SL0"), [[1, 16], [0, 8], [-1, 16]], A_.is_equal, 0, 0)
+        asel(B("SL0"), B("SL0"), [[0, 16], [-16, 8], [0, 16]], A_.is_ge, 0, 1)
+        asel(B("SL0"), B("SL0"), [[0, 16], [16, 8], [0, 16]], A_.is_ge, 15, -1)
+        ms(B("MSK", 15, 256, 16), -1.0)
+        ms(B("MKK", 0, 512, 16), 0.0)
+        ts(B("BOV"), B("BO"), -1024.0, A_.mult)
+        ts(B("BOS"), B("BO"), -16.0, A_.mult)
+        vcopy(B("BOH"), B("BO"))
+        vcopy(B("IDH"), B("IDN"))
+        ts(B("OHT"), B("JT"), B("PC", 0, 1), A_.is_equal)
+        ts(B("CW"), B("CW0"), B("PC", 3, 4), A_.add)
+        for q, c0, w in ((0, 0, 32), (1, 32, 32), (2, 64, 64), (3, 128, 64)):
+            ts(B("LMT", c0, c0 + w), B("B64", 0, w), B("PC", 4 + q, 5 + q), A_.is_lt, B("PC", 8 + q, 9 + q), A_.mult)
+
+    def step1(t, b):
+        a0, n = BAT[b]
+        nq = n // 16
+        I, O = "i%s%d" % (b, t), "o%s%d" % (b, t)
+        return [
+            lambda: vcopy(B("LL" + b), B(I, 2 * n, 2 * n + 2 * nq)),
+            lambda: vgat(B("XV" + b), B("VAL", 0, 2048), B("LL" + b)),
+            lambda: tt(B("LE" + b), B("XV" + b, 0, n), B("XV" + b, n, 2 * n), A_.is_lt),
+            lambda: mm(B("psR", 0, n), B("BO"), B("LE" + b), True, True),
+            lambda: tt(B("DMC" + b), B(I, n, 2 * n), B(I, 0, n), A_.subtract),
+            lambda: ts(B("FL" + b), B("psR", 0, n), 8.5, A_.is_ge),
+            lambda: tt(B("T2" + b), B("FL" + b), B("DMC" + b), A_.mult),
+            lambda: tt(B(O, n, 2 * n), B("T2" + b), B(I, 0, n), A_.add),
+            lambda: vcopy(B("CU" + b), B(O, n, 2 * n)),
+        ]
+
+    def image(b, x0, x1):
+        a0 = BAT[b][0]
+        vgat(B("IMG", 16 * x0, 16 * x1), B("PT"), B("CU" + b, x0 - a0, x1 - a0))
+
+    def imf(b):
+        a0, n = BAT[b]
+        if b == "A":
+            vcopy(B("IFA"), B("IMG", 16 * a0, 16 * (a0 + n)))
+        else:
+            sgat(B("IFB"), B("PT"), B("CU" + b))
+
+    def values(f, x0, x1):
+        f(B("W", 256 * x0, 256 * x1), B("VAL", 0, 2048), B("IMG", 16 * x0, 16 * x1))
+
+    def scans(c):
+        p = c & 1
+        sb, yb = T["SB%d" % p], T["YB%d" % p]
+        wr = ("W", 4096 * c, 4096 * (c + 1))
+
+        def one(j):
+            op("v", lambda: V.tensor_tensor_scan(sb[:, 1:257, j], T.W[:, 4096 * c + j:4096 * (c + 1):16], T.MSK[:], 0.0, A_.max, A_.mult),
+               [wr, ("MSK", 0, 256)], [("SB%d.%d" % (p, j), 1, 257)])
+
+        def two(j):
+            op("v", lambda: V.tensor_tensor_scan(yb[:, :, j], T.W[:, 4096 * c + j:4096 * (c + 1):16], sb[:, 0:256, j], 0.0, A_.max, A_.min),
+               [wr, ("SB%d.%d" % (p, j), 0, 256)], [("YB%d.%d" % (p, j), 0, 256)])
+        out = [lambda: one(0)]
+        for j in range(1, 16):
+            out.append(lambda j=j: one(j))
+            out.append(lambda j=j: two(j - 1))
+        out.append(lambda: two(15))
+        return out
+
+    def diff(c):
+        p = c & 1
+        o = B("psD%d" % p, 0, 256)
+        op("t", lambda: TE.matmul(o[0], T.IDN[:], T["SB%d" % p][:, 16:257:16, :], True, False),
+           [("IDN", 0, 128)] + [("SB%d.%d" % (p, j), 16, 257) for j in range(16)], [o[1]])
+        op("t", lambda: TE.matmul(o[0], T.IDN[:], T["YB%d" % p][:, 15:256:16, :], False, True),
+           [("IDN", 0, 128)] + [("YB%d.%d" % (p, j), 15, 256) for j in range(16)], [o[1]])
+
+    def unit(t, c, q):
+        i, o = B("psD%d" % (c & 1), 0, 256), B("U", 256 * c, 256 * c + 256)
+        if q == "v":
+            ts(o, i, -float(MT[t]), A_.is_lt)
+        else:
+            act(o, i, -1000.0, -1000.0 * (MT[t] + 0.5), F.Sigmoid)
+
+    def votes(c):
+        o, c0 = B("psV%d" % (c & 1), 0, 256), 256 * (c % 2)
+        mm(o, B("E0"), B("A16", c0, c0 + 256), True, False)
+        mm(o, B("E0"), B("JT", 0, 256), False, False)
+        mm(o, B("BOV"), B("U", 256 * c, 256 * c + 256), False, True)
+
+    def scanmin(o, i):
+        n = o[1][2] - o[1][1]
+        m = B("MKK", 0, n)
+        op("v", lambda: V.tensor_tensor_scan(o[0], m[0], i[0], 0.0, A_.mult, A_.min), [m[1], i[1]], [o[1]])
+
+    def best(c):
+        scanmin(B("K1", 256 * c, 256 * c + 256), B("psV%d" % (c & 1), 0, 256))
+
+    def post(t, b, x0, x1):
+        a0, n = BAT[b]
+        nq, e0, e1, w, m0 = n // 16, 16 * a0, 16 * (a0 + n), a0 + n, 2 * a0
+        I, O = "i%s%d" % (b, t), "o%s%d" % (b, t)
+        km = lambda: B("K1", e0 + 15, e1, 16)
+
+        def promoted():
+            for o, f, c in (("PRO", -1000.0, 2), ("NP", 1000.0, 3)):
+                x, y, z = B(o, a0, a0 + n), km(), B("THR", c, c + 1)
+                op("s", lambda: S.activation(x[0], y[0], F.Sigmoid, bias=z[0], scale=f), [y[1], z[1]], [x[1]])
+
+        def newc():
+            for k in range(16):
+                mm(B("psN", 0, n), B("SEL", 128 * k, 128 * k + 128), B("MK", e0 + k, e1, 16), k == 0, k == 15)
+
+        def sums():
+            mm(B("psS"), B("E0"), B("JT"), True, False)
+            mm(B("psS"), B("BOS"), B("PR", e0, e1), False, True)
+
+        def marks():
+            mm(B("psR", 0, n), B("IDH"), B("PEN" + b), True, False)
+            mm(B("psR", 0, n), B("BOH"), B("XX" + b), False, True)
+
+        def put():
+            x, e, z = B("VAL"), B("EL" + b), B("ZE" + b)
+            op("v", lambda: V.tensor_copy(x[0].indirect(e[0]), z[0]), [e[1], z[1]], [x[1]])
+        L = [
+            lambda: vcopy(B("KI" + b), km()),
+            lambda: ts(B("QI" + b), B("KI" + b), 1023, A_.bitwise_and),
+            lambda: vcopy(B("LU" + b), B("QI" + b)),
+            lambda: sgat(B("UX", e0, e1), B("U", e0, e1), B("LU" + b)),
+            lambda: tt(B("WI" + b), B("QI" + b), B("CW", 0, n), A_.add),
+            promoted,
+            lambda: vcopy(B("LW" + b), B("WI" + b)),
+            lambda: ttg(B("MK", e0, e1), B("OHT"), B("LU" + b), B("IF" + b), A_.mult),
+            newc,
+            lambda: ttg(B("PR", e0, e1), B("W", 16 * e0, 16 * e1), B("LW" + b), B("UX", e0, e1), A_.mult),
+            sums,
+            lambda: tt(B("PEN" + b), B("NP", a0, a0 + n), B("PENC", a0, a0 + n), A_.mult),
+            lambda: tt(B("DN" + b), B(I, n, 2 * n), B("NP", a0, a0 + n), A_.mult),
+            lambda: tt(B("NCG" + b), B("psN", 0, n), B("PRO", a0, a0 + n), A_.mult),
+            lambda: tt(B(O, 0, n), B("NCG" + b), B("DN" + b), A_.add),
+        ]
+        M = [
+            lambda: scanmin(B("K2", e0, e1), B("psS")),
+            lambda: vcopy(B("K2I" + b), B("K2", e0 + 15, e1, 16)),
+            lambda: ts(B("KR" + b), B("K2I" + b), 15, A_.bitwise_and),
+            lambda: ts(B("OHK" + b), B("KR" + b), B("PC", 0, 1), A_.is_equal),
+            lambda: tt(B("XX" + b), B("OHK" + b), B("NCG" + b), A_.mult),
+            marks,
+            lambda: tt(B("DM" + b), B("psR", 0, n), B("OHT", 0, n), A_.mult),
+            lambda: lin(b, B("PREP", a0, a0 + n), B("psR", 0, n), 0.49994, MAGIC),
+        ]
+        M += [lambda q=q: red(B("NL" + b, q, q + 1), B("DM" + b, 16 * q, 16 * q + 16), A_.add) for q in range(nq)]
+        M += [
+            lambda: ts(B("PCL" + b), B("NL" + b, 0, nq), 0.49994, A_.mult, MAGIC, A_.add),
+            lambda: lin(b, B("NM" + b), B("NL" + b, 0, nq), -1.0, 1.0),
+        ]
+        M += [lambda q=q: ts(B("EQ" + b, w * q, w * q + w), B("PREP", 0, w), B("PCL" + b, q, q + 1), A_.is_equal) for q in range(nq)]
+        M += [lambda: lin(b, B("FP" + b), B("PCL" + b), 4.0, -4.0 * MAGIC)]
+        N = [
+            lambda: tt(B("EM" + b, 0, nq * w), B("EQ" + b, 0, nq * w), B("LMT", m0, m0 + nq * w), A_.mult),
+            lambda: tt(B("NL" + b, nq, 2 * nq), B("FP" + b), B("NM" + b), A_.add),
+        ]
+        N += [lambda q=q: red(B("DV" + b, q, q + 1), B("EM" + b, w * q, w * q + w), A_.max) for q in range(nq)]
+        N += [
+            lambda: ts(B("DV" + b, nq, 2 * nq), B("DV" + b, 0, nq), 1.0 + 2.0 ** -11, A_.mult),
+            lambda: tt(B("OL" + b), B("NL" + b), B("DV" + b), A_.max),
+            lambda: vcopy(B("EL" + b), B("OL" + b)),
+        ]
+        E = [
+            lambda: ttg(B("YE" + b), B("VAL"), B("EL" + b), B("DC"), A_.add),
+            lambda: ts(B("ZE" + b), B("YE" + b), 255.0, A_.min, 0.0, A_.max),
+            put,
+        ]
+        return L + _weave(M, x0) + N[:2] + _weave(N[2:], x1), E
+
+    def newmarks(t, b):
+        n = BAT[b][1]
+        I, O = "i%s%d" % (b, t), "o%s%d" % (b, t)
+        old = lambda: B(I, 2 * n, 2 * n + n // 8)
+        return [
+            lambda: ts(B("KP" + b), B("NL" + b), 2047.5, A_.is_lt),
+            lambda: tt(B("DL" + b), B("NL" + b), old(), A_.subtract),
+            lambda: tt(B("DK" + b), B("DL" + b), B("KP" + b), A_.mult),
+            lambda: tt(B(O, 2 * n, 2 * n + n // 8), B("DK" + b), old(), A_.add),
+        ]
+
+    def parity(t):
+        return [
+            lambda: red(B("THR", 1, 2), B("PRO"), A_.add),
+            lambda: vcopy(B("TI", 0, 1), B("THR", 1, 2)),
+            lambda: ts(B("TI", 1, 2), B("TI", 0, 1), 1, A_.bitwise_and),
+            lambda: ts(B("THR", 2, 3), B("TI", 1, 2), -1024000.0, A_.mult, -1024000.0 * (AT[t] - 1) - 500.0, A_.add),
+            lambda: ts(B("THR", 3, 4), B("TI", 1, 2), 1024000.0, A_.mult, 1024000.0 * (AT[t] - 1) + 500.0, A_.add),
+        ]
+
+    src, hand, dst = _route(rank, T, topo)
+    sent = [0]
+
+    def send(t, b):
+        if t == NR_ - 1:
+            return
+        o = B("o%s%d" % (b, t))
+        need("g", [o[1]], [])
+        to = hand if hand is not None else dst
+        sent[0] += _send(g, T, topo, core, to, o[0], "i%s%d" % (b, t + 1), "a%s%d" % (b, t + 1))
+
+    into = _route((rank - 3) % len(T.cores), T, topo)
+    arr = _mask(into[1] if into[1] is not None else into[0], core, topo)[1]
+
+    def arrive(t):
+        for b in BAT:
+            i, sem = B("i%s%d" % (b, t)), "a%s%d" % (b, t)
+            total[sem] = arr
+            note("rem" + sem, [], [i[1]], (sem, arr))
+
+    def store(q, y, nm, sem, c1):
+        o = B(nm, 0, c1)
+        dma(q, y[:], o[0], [o[1]], [], sem)
+
+    def outputs(q, part, fx, z, zt, y, yd, sem):
+        t = NR_ - 1
+        L = [lambda b=b: vcopy(B(fx, BAT[b][0], sum(BAT[b])), B("o%s%d" % (b, t), part * BAT[b][1], (part + 1) * BAT[b][1])) for b in BAT]
+        return L + flip("s", z, zt, lambda x: B(fx, 16 * x, 16 * x + 16), lambda x: B(y, x, 64, 4)) + [lambda: store(q, yd, y, sem, 64)]
+
+    for t in range(NR_):
+        last = t == NR_ - 1
+        if t:
+            arrive(t)
+        _go(step1(t, "A"))
+        image("A", 0, 16)
+        values(sgat, 0, 16 - NV)
+        image("A", 16, 32)
+        if t == 0:
+            late_constants()
+        values(vgat, 16 - NV, 16)
+        values(sgat, 16, 32)
+        imf("A")
+        _go(_weave(scans(0), (parity(t) if t else []) + step1(t, "B") + [lambda: image("B", 32, 48)], 0.3))
+        values(sgat, 32, 40)
+        diff(0)
+        unit(t, 0, "s")
+        votes(0)
+        values(sgat, 40, 48)
+        _go(_weave(scans(1), [lambda: image("B", 48, 64), lambda: best(0)], 0.1))
+        diff(1)
+        unit(t, 1, "v")
+        votes(1)
+        if t == 0:
+            vcopy(B("SEL"), B("SL0"))
+        best(1)
+        chain, late = post(t, "A", [], newmarks(t, "A"))
+        _go(chain[:6])
+        values(sgat, 48, 64)
+        imf("B")
+        _go(chain[6:PRE])
+        _go(_weave(scans(2), chain[PRE:] + [lambda: send(t, "A")]))
+        diff(2)
+        unit(t, 2, "s")
+        votes(2)
+        _go(_weave(scans(3), [lambda: best(2)], 0.2))
+        diff(3)
+        late[0]()
+        unit(t, 3, "v")
+        votes(3)
+        _go(late[1:])
+        best(3)
+        x0 = outputs("s", 1, "FX2", "Z2", "ZT2", "YD", T.yd, "st2") + outputs("y", 0, "FX", "Z", "ZT", "YC", T.yc, "st1") if last else []
+        chain, late = post(t, "B", x0, newmarks(t, "B"))
+        _go(chain)
+        send(t, "B")
+        _go(late)
+
+    store("y", T.yv, "VAL", "st0", 2048)
+    for b in BAT:
+        a0, n = BAT[b]
+        vcopy(B("YL", a0 // 16, (a0 + n) // 16), B("o%s%d" % (b, NR_ - 1), 2 * n, 2 * n + n // 16))
+    store("s", T.yl, "YL", "st3", 4)
+    total["ls"] = sent[0]
+    for s in total:
+        if total[s]:
+            g.wait_ge(T.sem[s], total[s])

@@ -4,56 +4,32 @@ A_ = AluOpType
 F = ActivationFunctionType
 X_ = AxisListType.X
 NR_ = 5
-BAT = {"A": (0, 32), "B": (32, 32)}
-NV = 8
-PRE = 8
+PAR = dict(ch=(2, 2, 2, 2, 2, 2, 2, 1, 1), sunit=0, img="s", ux="s", prs=0, par="v", down="v", ic=(4, 12), vg=(),
+           cyc=1.0, gat=1.5, put=3.5, fix=40, wake=70, hop=4500, dma=4000, slack=100)
+VW = 2320
+BIG = 1.0e9
 MAGIC = 12582912.0
 
-_SIZE = {"float32": 4, "int32": 4, "uint16": 2, "float16": 2, "bfloat16": 2}
 SCRATCH = {}
-for _d, _names in (("int32", "GEN 1024 CW0 64 CW 64 PI 8 XC 64 XD 64 XL 4 LT0 4 LT1 4 TI 2"),
-                   ("float32", "GM 1024 PM 1024 PT 2048 IFB 512 K1 1024 K2 1024 B64 64 PENC 64 LMT 192 PC 16 DC 64 Z 128 ZT 128 "
-                               "Z2 128 ZT2 128 FX 64 FX2 64 YC 64 YD 64 YL 4 PREP 64 THR 4"),
-                   ("bfloat16", "VAL 2176 W 16384 U 1024 UX 1024 PR 1024 MSK 256 MKK 512 ONE 128 BO 128 B1 128 BOV 128 BOS 128 IDN 128 "
-                                "E0 128 SL0 2048 JT 512 A16 512 OHT 512 PRO 64 NP 64"),
-                   ("float16", "IFA 512 MK 1024 BOH 128 IDH 128 SEL 2048"), ("uint16", "IMG 1024")):
+for _d, _names in (("int32", "GEN 1024 XCD 128 XL 4 PI 4 LC0 8 TI 2 PR2 4"),
+                   ("float32", "PT0 2048 PT1 2048 IMG 512 IMT0 544 IMT1 544 PC 16 B64 64 IX0 32 KB 12 THK0 32 THK1 32 TH2 32 K1 32 RR 2 "
+                               "KT 64 K2 32 XD 32 XX 34 U4 4 PK 2 TB 4 GT 128 GU 128 YCD 128 YL 4"),
+                   ("bfloat16", "VAL0 %d VAL1 %d W0 8704 W1 8704 SB 8208 YB 8192 U0 544 U1 544 UX 512 WS 512 PR 512 MSK 2048 ONE 160 NEG 144 B1 160 "
+                                "BW 160 BP0 160 BP1 160 BN0 160 BN1 160 IW 160 IW0 160 IW1 160 SL1 144 SL2 144 SEL 144 R0 128 R1 128 RM0 128 RM1 128 "
+                                "B2 128 B32 128 OH 32 KC 32 FAR 128 XV 64 LE 32 ZE 128 ZC 64 MK2 130" % (VW, VW)),
+                   ("float16", "G16 1024 A16 1024 FX 128 FT 128 ML 8 IDX 32 AA 2 XH 64 EE 4 EQ 130 DV 260 CD 64"),
+                   ("uint16", "LC 8 LL 4 CU 32 LI0 512 LI1 512 LW 32 LU 32 EL 8")):
     _w = _names.split()
     for _i in range(0, len(_w), 2):
         SCRATCH[_w[_i]] = ("sbuf", [128, int(_w[_i + 1])], _d)
-for _i in (0, 1):
-    SCRATCH["SB%d" % _i] = ("sbuf", [128, 257, 16], "bfloat16")
-    SCRATCH["YB%d" % _i] = ("sbuf", [128, 256, 16], "bfloat16")
-for _n in "psD0 psD1 psV0 psV1 psS psN psR".split():
+for _n in "psD0 psD1 psK0 psK1 psS psR psP psE".split():
     SCRATCH[_n] = ("psum", [128, 512], "float32")
-SEMAPHORES = "vc sc tc gc ls ld0 ld1 ld2 ld3 ld4 st0 st1 st2 st3".split()
-_POS = {}
-
-
-def _declare():
-    tot = {}
-    for b, (a0, n) in BAT.items():
-        nq = n // 16
-        for t in range(NR_):
-            SCRATCH["i%s%d" % (b, t)] = ("sbuf", [128, 2 * n + 2 * nq], "float16")
-            SCRATCH["o%s%d" % (b, t)] = ("sbuf", [128, 2 * n + 2 * nq], "float16")
-            if t:
-                SEMAPHORES.append("a%s%d" % (b, t))
-        for d, names in (("uint16", (("LL", 2 * nq), ("CU", n), ("LU", n), ("LW", n), ("EL", 2 * nq))),
-                         ("bfloat16", (("XV", 2 * n), ("LE", n), ("ZE", 2 * n))),
-                         ("int32", (("KI", n), ("QI", n), ("WI", n), ("K2I", n), ("KR", n))),
-                         ("float16", (("PEN", n), ("NCG", n), ("XX", n))),
-                         ("float32", (("DMC", n), ("FL", n), ("T2", n), ("NM", nq), ("DN", n), ("OHK", n), ("DM", n), ("NL", 2 * nq),
-                                      ("PCL", nq), ("EQ", 64 * nq), ("EM", 64 * nq), ("DV", 2 * nq), ("FP", nq),
-                                      ("OL", 2 * nq), ("YE", 2 * n), ("KP", 2 * nq), ("DL", 2 * nq), ("DK", 2 * nq)))):
-            for nm, w in names:
-                al = 64 // _SIZE[d]
-                _POS[nm + b] = ("pk_" + d, tot.get(d, 0), w)
-                tot[d] = tot.get(d, 0) + (w + al - 1) // al * al
-    for d in tot:
-        SCRATCH["pk_" + d] = ("sbuf", [128, tot[d]], d)
-
-
-_declare()
+SEMAPHORES = "vc sc tc gc ls ldg ldc ldl ldv0 ldv1 stv0 stv1 stw1 stc std stl".split()
+for _n in range(2 * NR_):
+    SCRATCH["i%d" % _n] = ("sbuf", [128, 68], "float16")
+    SCRATCH["o%d" % _n] = ("sbuf", [128, 68], "float16")
+    if _n > 1:
+        SEMAPHORES.append("a%d" % _n)
 
 
 def _route(r, T, topo):
@@ -83,27 +59,52 @@ def _relay(g, core, T, topo):
         if h != core:
             continue
         tot = 0
-        for t in range(1, NR_):
-            for b in BAT:
-                nm, sem = "i%s%d" % (b, t), "a%s%d" % (b, t)
-                g.wait_ge(T.sem[sem], _mask(s, h, topo)[1])
-                tot += _send(g, T, topo, core, d, T[nm][:], nm, sem)
+        for n in range(2, 2 * NR_):
+            g.wait_ge(T.sem["a%d" % n], _mask(s, h, topo)[1])
+            tot += _send(g, T, topo, core, d, T["i%d" % n][:], "i%d" % n, "a%d" % n)
         g.wait_ge(T.sem["ls"], tot)
 
 
-def _weave(a, c, x0=0.0):
-    L, k = [], 0
-    for i, f in enumerate(a):
-        L.append(f)
-        want = int(max(((i + 1) / len(a) - x0) / (1.0 - x0), 0.0) * len(c) + 1e-6)
-        L += c[k:want]
-        k = max(k, want)
-    return L + c[k:]
+def _meet(a, b):
+    if a[0] > b[-1] or b[0] > a[-1]:
+        return False
+    return (a.step == 1 and b.step == 1) or any(x in b for x in a)
 
 
-def _go(L):
-    for f in L:
-        f()
+def _inside(a, b):
+    return a == b or (b.step == 1 and b[0] <= a[0] and a[-1] <= b[-1])
+
+
+def _order(calls):
+    P = PAR
+    users = [[] for c in calls]
+    for i, c in enumerate(calls):
+        for d in c["deps"]:
+            users[d].append(i)
+    way = [0.0] * len(calls)
+    for i in reversed(range(len(calls))):
+        way[i] = calls[i]["busy"] + calls[i]["late"] + max([way[u] + P["wake"] for u in users[i]], default=0.0)
+    left = [len(c["deps"]) for c in calls]
+    at = [0.0] * len(calls)
+    ready = {}
+    for i, c in enumerate(calls):
+        ready.setdefault(c["q"], [])
+        if not left[i]:
+            ready[c["q"]].append(i)
+    free = {q: 0.0 for q in ready}
+    out = []
+    while len(out) < len(calls):
+        now, q = min((max(free[q], min(at[i] for i in ready[q])), q) for q in ready if ready[q])
+        i = max((i for i in ready[q] if at[i] <= now + P["slack"]), key=lambda i: (way[i], -i))
+        ready[q].remove(i)
+        out.append(i)
+        free[q] = max(now, at[i]) + calls[i]["busy"]
+        for u in users[i]:
+            at[u] = max(at[u], free[q] + calls[i]["late"] + (0.0 if calls[u]["q"] == q == "t" else P["wake"]))
+            left[u] -= 1
+            if not left[u]:
+                ready[calls[u]["q"]].append(u)
+    return out
 
 
 def rank_program(g, core, T, topo):
@@ -111,468 +112,369 @@ def rank_program(g, core, T, topo):
     if rank is None:
         return _relay(g, core, T, topo)
     MT, AT = (12, 18, 14, 22, 16), (10, 8, 9, 6, 8)
+    P = PAR
     eng = {"v": g.vector, "s": g.scalar, "t": g.tensor, "g": g, "y": g.sync}
-    cnt, total, hist = {}, {}, {}
-    known = {q: {} for q in eng}
     V, S, TE = g.vector, g.scalar, g.tensor
+    calls, hist = [], {}
 
-    def need(q, reads, writes):
-        w = {}
+    def op(q, fn, reads, writes, busy, late=0.0, ev=None, after=()):
+        me, deps = len(calls), set(after)
         for keys, wr in ((reads, False), (writes, True)):
-            for (key, c0, c1) in keys:
+            for key, r in keys:
                 for h in hist.get(key, ()):
-                    if h[0] >= c1 or c0 >= h[1] or h[3] == q == "t":
-                        continue
-                    if not (wr or h[2] or (key[:2] == "ps" and h[3] != q)):
-                        continue
-                    s, n = h[4]
-                    w[s] = max(w.get(s, 0), n)
-        for s in w:
-            if known[q].get(s, 0) < w[s]:
-                eng[q].wait_ge(T.sem[s], w[s])
-                known[q][s] = w[s]
-
-    def note(q, reads, writes, ev):
+                    if (wr or h[1] or key[:2] == "ps") and _meet(r, h[0]):
+                        deps.add(h[2])
         for keys, wr in ((reads, False), (writes, True)):
-            for (key, c0, c1) in keys:
+            for key, r in keys:
                 L = hist.setdefault(key, [])
-                if wr:
-                    L[:] = [h for h in L if not (c0 <= h[0] and h[1] <= c1)]
+                if wr or key[:2] == "ps":
+                    L[:] = [h for h in L if not _inside(h[0], r)]
+                L.append((r, wr, me))
+        deps.discard(me)
+        calls.append(dict(q=q, fn=fn, deps=deps, free=set(after), busy=busy, late=late, ev=ev))
+        return me
+
+    def issue():
+        cnt, total, known, clock = {}, {}, {q: {} for q in eng}, {}
+        for i in _order(calls):
+            c = calls[i]
+            q = c["q"]
+            if q in eng:
+                for d in sorted(c["deps"], key=lambda d: -calls[d]["at"]):
+                    if calls[d]["q"] == q == "t" or d in c["free"]:
+                        continue
+                    s, n = calls[d]["ev"]
+                    if known[q].get(s, 0) < n:
+                        eng[q].wait_ge(T.sem[s], n)
+                        for x, m in list(clock[d].items()) + [(s, n)]:
+                            known[q][x] = max(known[q].get(x, 0), m)
+                clock[i] = dict(known[q])
+                if c["ev"] is None:
+                    cnt[q] = cnt.get(q, 0) + 1
+                    c["ev"] = (q + "c", cnt[q])
+                    c["fn"]().then_inc(T.sem[q + "c"], 1)
                 else:
-                    L[:] = [h for h in L if h[2] or h[3] != q or not (c0 <= h[0] and h[1] <= c1)]
-                L.append((c0, c1, wr, q, ev))
+                    c["fn"]()
+            else:
+                clock[i] = {}
+            c["at"] = len(clock)
+            total[c["ev"][0]] = max(total.get(c["ev"][0], 0), c["ev"][1])
+        for s in total:
+            g.wait_ge(T.sem[s], total[s])
 
-    def op(q, fn, reads, writes):
-        need(q, reads, writes)
-        sem = q + "c"
-        total[sem] = cnt[q] = cnt.get(q, 0) + 1
-        fn().then_inc(T.sem[sem], 1)
-        note(q, reads, writes, (sem, cnt[q]))
-
-    def dma(q, o, i, reads, writes, sem):
-        need(q, reads, writes)
-        eng[q].dma_start(o, i).then_inc(T.sem[sem], 16)
-        total[sem] = 16
-        note("dma" + sem, reads, writes, (sem, 16))
+    def dmas(q, pairs, reads, writes, sem):
+        def fn():
+            for o, s in pairs:
+                eng[q].dma_start(o, s).then_inc(T.sem[sem], 16)
+        op(q, fn, reads, writes, 60.0 * len(pairs), P["dma"], (sem, 16 * len(pairs)))
 
     def B(name, c0=0, c1=None, st=1):
-        base, off, w = _POS[name] if name in _POS else (name, 0, SCRATCH[name][1][1])
-        c1 = w if c1 is None else c1
-        ap = T[base][:, off + c0:off + c1] if st == 1 else T[base][:, off + c0:off + c1:st]
-        return ap, ((base, 0, 512) if base[:2] == "ps" else (base, off + c0, off + c1))
+        c1 = SCRATCH[name][1][1] if c1 is None else c1
+        ap = T[name][:, c0:c1] if st == 1 else T[name][:, c0:c1:st]
+        r = range(c0, c1, st)
+        return ap, (name, range(512) if name[:2] == "ps" else r), len(r), 2 if "16" in SCRATCH[name][2] else 4
+
+    def col(name, c):
+        return B(name, c, c + 1)
+
+    def cost(o, *ins):
+        return P["fix"] + P["cyc"] * max(64, o[2] * (0.5 if max(x[3] for x in (o,) + ins) == 2 else 1.0))
+
+    def picked(n, rate="gat"):
+        return 60 + P["cyc"] * n * P[rate]
 
     def vcopy(o, i):
-        op("v", lambda: V.tensor_copy(o[0], i[0]), [i[1]], [o[1]])
+        op("v", lambda: V.tensor_copy(o[0], i[0]), [i[1]], [o[1]], cost(o, i))
 
-    def vgat(o, win, off):
-        op("v", lambda: V.tensor_copy(o[0], win[0].indirect(off[0])), [win[1], off[1]], [o[1]])
+    def gat(q, o, win, off, f=F.Copy, scale=1.0, bias=0.0, after=()):
+        if q == "s":
+            return op("s", lambda: S.activation(o[0], win[0].indirect(off[0]), f, bias=bias, scale=scale), [win[1], off[1]], [o[1]],
+                      picked(o[2]), after=after)
+        elif scale != 1.0:
+            ts(o, win, scale, A_.mult, off=off)
+        else:
+            op("v", lambda: V.tensor_copy(o[0], win[0].indirect(off[0])), [win[1], off[1]], [o[1]], picked(o[2]))
 
-    def sgat(o, win, off):
-        op("s", lambda: S.activation(o[0], win[0].indirect(off[0]), F.Copy), [win[1], off[1]], [o[1]])
+    def vput(win, off, i):
+        op("v", lambda: V.tensor_copy(win[0].indirect(off[0]), i[0]), [off[1], i[1]], [win[1]], picked(i[2], "put"))
 
     def act(o, i, scale, bias, f=F.Copy):
-        op("s", lambda: S.activation(o[0], i[0], f, bias=bias, scale=scale), [i[1]], [o[1]])
+        c = isinstance(bias, tuple)
+        op("s", lambda: S.activation(o[0], i[0], f, bias=bias[0] if c else bias, scale=scale), [i[1]] + ([bias[1]] if c else []), [o[1]],
+           P["fix"] + P["cyc"] * max(64, o[2]))
 
     def tt(o, a, b, f):
-        op("v", lambda: V.tensor_tensor(o[0], a[0], b[0], f), [a[1], b[1]], [o[1]])
+        op("v", lambda: V.tensor_tensor(o[0], a[0], b[0], f), [a[1], b[1]], [o[1]], P["fix"] + P["cyc"] * max(64, 2 * o[2]))
 
     def ttg(o, win, off, b, f):
-        op("v", lambda: V.tensor_tensor(o[0], win[0].indirect(off[0]), b[0], f), [win[1], off[1], b[1]], [o[1]])
+        op("v", lambda: V.tensor_tensor(o[0], win[0].indirect(off[0]), b[0], f), [win[1], off[1], b[1]], [o[1]], picked(o[2]))
 
-    def ts(o, a, s1, f1, s2=None, f2=None):
-        rd = [a[1]] + [s[1] for s in (s1, s2) if isinstance(s, tuple)]
+    def ts(o, a, s1, f1, s2=None, f2=None, off=None):
+        rd = [a[1]] + [s[1] for s in (s1, s2, off) if isinstance(s, tuple)]
         x1 = s1[0] if isinstance(s1, tuple) else s1
         x2 = s2[0] if isinstance(s2, tuple) else s2
-        if f2 is None:
-            op("v", lambda: V.tensor_scalar(o[0], a[0], x1, None, f1), rd, [o[1]])
-        else:
-            op("v", lambda: V.tensor_scalar(o[0], a[0], x1, x2, f1, f2), rd, [o[1]])
-
-    def lin(b, o, i, scale, bias):
-        if b == "B":
-            act(o, i, scale, bias)
-        else:
-            ts(o, i, scale, A_.mult, bias, A_.add)
+        args = (x1, None, f1) if f2 is None else (x1, x2, f1, f2)
+        op("v", lambda: V.tensor_scalar(o[0], a[0].indirect(off[0]) if off else a[0], *args), rd, [o[1]], picked(o[2]) if off else cost(o, a))
 
     def red(o, a, f):
-        op("v", lambda: V.tensor_reduce(o[0], a[0], X_, f), [a[1]], [o[1]])
+        op("v", lambda: V.tensor_reduce(o[0], a[0], X_, f), [a[1]], [o[1]], cost(o))
+
+    def scan(o, a, b, init, f0, f1):
+        op("v", lambda: V.tensor_tensor_scan(o[0], a[0], b[0], init, f0, f1), [a[1], b[1]], [o[1]], cost(o, a, b))
+
+    def turn(o, i):
+        op("v", lambda: V.transpose(o[0], i[0]), [i[1]], [o[1]], cost(o))
 
     def ms(o, c):
-        op("v", lambda: V.memset(o[0], c), [], [o[1]])
+        op("v", lambda: V.memset(o[0], c), [], [o[1]], cost(o))
 
     def mm(o, l, r, st, sp):
-        op("t", lambda: TE.matmul(o[0], l[0], r[0], st, sp), [l[1], r[1]], [o[1]])
+        op("t", lambda: TE.matmul(o[0], l[0], r[0], st, sp), [l[1], r[1]], [o[1]], P["cyc"] * max(64, r[2]), P["wake"])
+
+    def mms(o, pairs):
+        for i, (l, r) in enumerate(pairs):
+            mm(o, l, r, i == 0, i == len(pairs) - 1)
 
     def iota(o, pat, base, ch, whole=False):
-        if whole:
-            op("g", lambda: g.iota(o[0], pat, base, ch), [], [o[1]])
-        else:
-            op("g", lambda: g.iota(o[0], pat, base, ch, allow_small_or_imprecise_dtypes=True), [], [o[1]])
+        kw = {} if whole else dict(allow_small_or_imprecise_dtypes=True)
+        op("g", lambda: g.iota(o[0], pat, base, ch, **kw), [], [o[1]], 150 + 2 * P["cyc"] * o[2])
 
     def asel(o, i, pat, f, base, ch):
-        op("g", lambda: g.affine_select(o[0], i[0], pat, f, 0.0, base, ch), [i[1]], [o[1]])
+        op("g", lambda: g.affine_select(o[0], i[0], pat, f, 0.0, base, ch), [i[1]], [o[1]], 200 + 2 * P["cyc"] * o[2])
 
-    for q, nm, c1, src, sem in (("s", "GEN", 1024, T.gen, "ld3"), ("y", "XC", 64, T.cla, "ld0"), ("y", "XD", 64, T.par, "ld1"),
-                                ("y", "XL", 4, T.lit, "ld2"), ("y", "VAL", 2048, T.val, "ld4")):
-        o = B(nm, 0, c1)
-        dma(q, o[0], src[:], [], [o[1]], sem)
+    def move(w, h, l):
+        c = 16 + 16 * (h - l)
+        return B("%s%d" % (w, h), c, c + 128)
 
-    iota(B("PI", 0, 1), [[1, 1]], 0, 1, True)
+    IDN = B("IW", 16, 144)
+
+    def sel(p):
+        return B("SEL", 15 - p, 143 - p)
+
+    dmas("s", [(T.GEN[:], T.gen[:])], [], [B("GEN")[1]], "ldg")
+    dmas("y", [(T.XCD[:, 0:64], T.cla[:]), (T.XCD[:, 64:128], T.par[:])], [], [B("XCD")[1]], "ldc")
+    dmas("y", [(T.XL[:], T.lit[:])], [], [B("XL")[1]], "ldl")
+    for s in (0, 1):
+        dmas("y", [(T["VAL%d" % s][16 * x:16 * x + 16, 0:2048], T.val[32 * (x // 2) + 16 * s:32 * (x // 2) + 16 * s + 16, :]) for x in range(8)],
+             [], [B("VAL%d" % s, 0, 2048)[1]], "ldv%d" % s)
+
+    iota(col("PI", 0), [[1, 1]], 0, 1, True)
     ms(B("ONE"), 1.0)
-    asel(B("B1"), B("ONE"), [[-16, 8], [0, 16]], A_.is_ge, 0, 1)
-    asel(B("BO"), B("B1"), [[16, 8], [0, 16]], A_.is_ge, 15, -1)
-    asel(B("IDN"), B("ONE"), [[-1, 128]], A_.is_equal, 0, 1)
-    asel(B("E0"), B("ONE"), [[0, 128]], A_.is_equal, 0, 1)
-    iota(B("JT"), [[0, 32], [1, 16]], 0, 0)
-    iota(B("A16"), [[16, 32], [0, 16]], 0, 0)
-    iota(B("CW0"), [[240, 64]], 0, 0, True)
+    asel(B("IW"), B("ONE"), [[-1, 160]], A_.is_equal, 16, 1)
+    iota(B("LC0"), [[64, 2], [1, 2], [2, 2]], 0, 0, True)
+    asel(B("B1"), B("ONE"), [[-16, 10], [0, 16]], A_.is_ge, 16, 1)
+    asel(B("BW"), B("B1"), [[16, 10], [0, 16]], A_.is_ge, -1, -1)
+    ms(B("NEG"), -32768.0)
+    for c, m in ((1, 15), (2, 16), (3, 31)):
+        ts(col("PI", c), col("PI", 0), m, A_.bitwise_and)
+    for h in (0, 1):
+        ts(col("PC", 1 + h), col("PI", 2), 16.0 * h, A_.is_equal)
+        ts(col("PC", 3 + h), col("PI", 3), 32.0 * h, A_.add)
+    ts(B("PC", 5, 7), B("PC", 3, 5), 2.0, A_.mult, 2048.0, A_.add)
+    for c, m in ((7, 4.0), (8, 512.0), (9, 16.0), (10, -2048.0)):
+        ts(col("PC", c), col("PI", 1), m, A_.mult)
+    ts(B("LC"), B("LC0"), col("PC", 7), A_.add)
+    for h in (0, 1):
+        ts(B("IW%d" % h), B("IW"), col("PC", 1 + h), A_.mult)
+        tt(B("R%d" % h), move("IW", h, 0), move("IW", h, 1), A_.add)
+        ts(B("RM%d" % h), B("R%d" % h), -0.25, A_.mult)
+        ts(B("BP%d" % h), B("BW"), col("PC", 1 + h), A_.mult, 4096.0, A_.mult)
+        ts(B("BN%d" % h), B("BW"), col("PC", 1 + h), A_.mult, -4096.0, A_.mult)
+        ms(B("ZC", 32 * h, 32 * h + 32), 8.5 * 4096.0 * (1 - 2 * h))
     iota(B("B64"), [[1, 64]], 0, 0)
-    iota(B("PENC"), [[2, 64]], 2048, 0)
-    ms(B("VAL", 2048, 2176), 0.0)
-    ts(B("PI", 1, 2), B("PI", 0, 1), 15, A_.bitwise_and)
-    ts(B("PI", 2, 3), B("PI", 0, 1), 16, A_.bitwise_and)
-    ms(B("DC", 0, 32), 32.0)
-    vcopy(B("PC", 0, 1), B("PI", 1, 2))
-    ts(B("PC", 1, 2), B("PI", 2, 3), 0.0, A_.is_equal)
-    ts(B("PC", 2, 3), B("PI", 2, 3), 16.0, A_.is_equal)
-    ts(B("PC", 3, 4), B("PC", 0, 1), 16.0, A_.mult)
-    for q in range(4):
-        ts(B("PC", 4 + q, 5 + q), B("PC", 0, 1), 16.0 * q, A_.add)
-    for q in range(4):
-        ts(B("PC", 8 + q, 9 + q), B("PC", 4 + q, 5 + q), 2.0, A_.mult, 2048.0, A_.add)
-    for p in (0, 1):
-        op("v", lambda p=p: V.memset(T["SB%d" % p][:, 0, :], 0.0), [], [("SB%d.%d" % (p, j), 0, 1) for j in range(16)])
-    ms(B("DC", 32, 64), -32.0)
-    ms(B("THR", 2, 3), -1024000.0 * (AT[0] - 1) - 500.0)
-    ms(B("THR", 3, 4), 1024000.0 * (AT[0] - 1) + 500.0)
-    ms(B("MSK"), 1.0)
-    ms(B("MKK"), 1.0)
+    iota(B("IX0"), [[16, 32]], 0, 0)
+    asel(B("SL1"), B("NEG"), [[-16, 9], [0, 16]], A_.is_ge, 0, 1)
+    asel(B("SL2"), B("SL1"), [[16, 9], [0, 16]], A_.is_ge, 15, -1)
+    asel(B("SEL"), B("SL2"), [[0, 9], [1, 16]], A_.is_equal, -15, 0)
+    asel(B("B2"), B("ONE", 0, 128), [[-32, 4], [0, 32]], A_.is_ge, 0, 1)
+    asel(B("B32"), B("B2"), [[32, 4], [0, 32]], A_.is_ge, 31, -1)
+    wide = 512 * max(P["ch"])
+    ms(B("MSK", 0, wide), 1.0)
+    ms(B("MSK", 15, wide, 16), -1.0)
+    ms(B("SB", 0, 1), 0.0)
+    ms(B("TH2"), BIG)
+    ms(B("TH2", 0, 32, 16), 4096.0)
+    ms(B("MK2"), 1.0)
+    ms(B("MK2", 0, 130, 65), 0.0)
+    ms(B("YCD"), 0.0)
+    ts(B("IDX"), B("IX0"), col("PC", 8), A_.add)
+    ts(B("KB", 0, 2), B("IX0", 0, 32, 16), 8192.0, A_.add, col("PC", 9), A_.add)
+    ts(B("KC"), B("ONE", 0, 32), col("PC", 10), A_.mult)
+    ts(B("OH"), B("B64", 0, 32), col("PC", 3), A_.is_equal)
+    for s in (0, 1):
+        ms(B("VAL%d" % s, 2048, VW), 0.0)
+        ms(B("W%d" % s, 8192, 8704), 0.0)
+        ms(B("U%d" % s, 512, 544), 0.0)
+        ms(B("THK%d" % s), -BIG)
+        ts(B("FAR", 64 * s, 64 * s + 64), B("B64"), col("PC", 3 + s), A_.is_ge, 4096.0, A_.mult)
+        ts(B("THK%d" % s, 0, 32, 16), B("KB", 0, 2), -32768.0 * AT[0], A_.add)
+    if P["par"] == "s":
+        for t in range(1, NR_):
+            act(B("KB", 2 * t, 2 * t + 2), B("KB", 0, 2), 1.0, -32768.0 * AT[t])
 
-    def flip(q_, Z, ZT, src, dst):
-        def blocks():
-            for q in range(4):
-                for h in range(2):
-                    o, i, m = B(Z, 32 * q + 16 * h, 32 * q + 16 * h + 16), src(q), B("PC", 1 + h, 2 + h)
-                    if q_ == "s":
-                        op("s", lambda: S.activation(o[0], i[0], F.Copy, scale=m[0]), [i[1], m[1]], [o[1]])
-                    else:
-                        ts(o, i, m, A_.mult)
+    def pair_of(l, lp, n):
+        ts(B("PR2", 0, n), l, 0.5, A_.mult, -0.25, A_.add)
+        ts(B("U4", 0, n), B("PR2", 0, n), 4.0, A_.mult, 1.0, A_.add)
+        tt(lp, B("U4", 0, n), l, A_.subtract)
 
-        def turn():
-            a, b = B(Z), B(ZT)
-            op("v", lambda: V.transpose(b[0], a[0]), [a[1]], [b[1]])
-        return [blocks, turn] + [lambda q=q: tt(dst(q), B(ZT, 32 * q, 32 * q + 16), B(ZT, 32 * q + 16, 32 * q + 32), A_.add)
-                                 for q in range(4)]
-
-    def lane16(pre, t, part):
-        def f(q):
-            b = "A" if 16 * q < BAT["B"][0] else "B"
-            c = part * BAT[b][1] + 16 * q - BAT[b][0]
-            return B("%s%s%d" % (pre, b, t), c, c + 16)
-        return f
-
-    vcopy(B("FX"), B("XC"))
-    fc = flip("s", "Z", "ZT", lambda q: B("FX", q, 64, 4), lane16("i", 0, 0))
-    fd = flip("v", "Z2", "ZT2", lambda q: B("FX2", q, 64, 4), lane16("i", 0, 1))
-    fc[0]()
-    vcopy(B("FX2"), B("XD"))
-    HF = ((0, 512), (512, 1024))
-    for c0, c1 in HF:
-        vcopy(B("PT", 2 * c0, 2 * c1, 2), B("GEN", c0, c1))
-    for i, (c0, c1) in enumerate(HF):
-        act(B("PM", c0, c1), B("PT", 2 * c0, 2 * c1, 2), 0.49994, MAGIC)
-        act(B("psD%d" % i), B("PM", c0, c1), 4.0, -4.0 * MAGIC)
-    _go(fc[1:2])
-    ts(B("GM", 0, 512), B("GEN", 0, 512), 1.0, A_.subtract)
-    _go(fc[2:])
-    ts(B("GM", 512, 1024), B("GEN", 512, 1024), 1.0, A_.subtract)
-    _go(fd)
-    ts(B("LT0"), B("XL"), 1, A_.bitwise_and)
-    for b in BAT:
-        a0, n = BAT[b]
-        vcopy(B("i%s0" % b, 2 * n, 2 * n + n // 16), B("XL", a0 // 16, (a0 + n) // 16))
-    ts(B("LT1"), B("LT0"), -2.0, A_.mult, 1.0, A_.add)
-    tt(B("PT", 1, 1024, 2), B("psD0"), B("GM", 0, 512), A_.subtract)
-    for b in BAT:
-        a0, n = BAT[b]
-        q0, nq = a0 // 16, n // 16
-        tt(B("i%s0" % b, 2 * n + nq, 2 * n + 2 * nq), B("XL", q0, q0 + nq), B("LT1", q0, q0 + nq), A_.add)
-    tt(B("PT", 1025, 2048, 2), B("psD1"), B("GM", 512, 1024), A_.subtract)
-
-    def late_constants():
-        ms(B("SL0"), 1.0)
-        asel(B("SL0"), B("SL0"), [[1, 16], [0, 8], [-1, 16]], A_.is_equal, 0, 0)
-        asel(B("SL0"), B("SL0"), [[0, 16], [-16, 8], [0, 16]], A_.is_ge, 0, 1)
-        asel(B("SL0"), B("SL0"), [[0, 16], [16, 8], [0, 16]], A_.is_ge, 15, -1)
-        ms(B("MSK", 15, 256, 16), -1.0)
-        ms(B("MKK", 0, 512, 16), 0.0)
-        ts(B("BOV"), B("BO"), -1024.0, A_.mult)
-        ts(B("BOS"), B("BO"), -16.0, A_.mult)
-        vcopy(B("BOH"), B("BO"))
-        vcopy(B("IDH"), B("IDN"))
-        ts(B("OHT"), B("JT"), B("PC", 0, 1), A_.is_equal)
-        ts(B("CW"), B("CW0"), B("PC", 3, 4), A_.add)
-        for q, c0, w in ((0, 0, 32), (1, 32, 32), (2, 64, 64), (3, 128, 64)):
-            ts(B("LMT", c0, c0 + w), B("B64", 0, w), B("PC", 4 + q, 5 + q), A_.is_lt, B("PC", 8 + q, 9 + q), A_.mult)
-
-    def step1(t, b):
-        a0, n = BAT[b]
-        nq = n // 16
-        I, O = "i%s%d" % (b, t), "o%s%d" % (b, t)
-        return [
-            lambda: vcopy(B("LL" + b), B(I, 2 * n, 2 * n + 2 * nq)),
-            lambda: vgat(B("XV" + b), B("VAL", 0, 2048), B("LL" + b)),
-            lambda: tt(B("LE" + b), B("XV" + b, 0, n), B("XV" + b, n, 2 * n), A_.is_lt),
-            lambda: mm(B("psR", 0, n), B("BO"), B("LE" + b), True, True),
-            lambda: tt(B("DMC" + b), B(I, n, 2 * n), B(I, 0, n), A_.subtract),
-            lambda: ts(B("FL" + b), B("psR", 0, n), 8.5, A_.is_ge),
-            lambda: tt(B("T2" + b), B("FL" + b), B("DMC" + b), A_.mult),
-            lambda: tt(B(O, n, 2 * n), B("T2" + b), B(I, 0, n), A_.add),
-            lambda: vcopy(B("CU" + b), B(O, n, 2 * n)),
-        ]
-
-    def image(b, x0, x1):
-        a0 = BAT[b][0]
-        vgat(B("IMG", 16 * x0, 16 * x1), B("PT"), B("CU" + b, x0 - a0, x1 - a0))
-
-    def imf(b):
-        a0, n = BAT[b]
-        if b == "A":
-            vcopy(B("IFA"), B("IMG", 16 * a0, 16 * (a0 + n)))
-        else:
-            sgat(B("IFB"), B("PT"), B("CU" + b))
-
-    def values(f, x0, x1):
-        f(B("W", 256 * x0, 256 * x1), B("VAL", 0, 2048), B("IMG", 16 * x0, 16 * x1))
-
-    def scans(c):
-        p = c & 1
-        sb, yb = T["SB%d" % p], T["YB%d" % p]
-        wr = ("W", 4096 * c, 4096 * (c + 1))
-
-        def one(j):
-            op("v", lambda: V.tensor_tensor_scan(sb[:, 1:257, j], T.W[:, 4096 * c + j:4096 * (c + 1):16], T.MSK[:], 0.0, A_.max, A_.mult),
-               [wr, ("MSK", 0, 256)], [("SB%d.%d" % (p, j), 1, 257)])
-
-        def two(j):
-            op("v", lambda: V.tensor_tensor_scan(yb[:, :, j], T.W[:, 4096 * c + j:4096 * (c + 1):16], sb[:, 0:256, j], 0.0, A_.max, A_.min),
-               [wr, ("SB%d.%d" % (p, j), 0, 256)], [("YB%d.%d" % (p, j), 0, 256)])
-        out = [lambda: one(0)]
-        for j in range(1, 16):
-            out.append(lambda j=j: one(j))
-            out.append(lambda j=j: two(j - 1))
-        out.append(lambda: two(15))
-        return out
-
-    def diff(c):
-        p = c & 1
-        o = B("psD%d" % p, 0, 256)
-        op("t", lambda: TE.matmul(o[0], T.IDN[:], T["SB%d" % p][:, 16:257:16, :], True, False),
-           [("IDN", 0, 128)] + [("SB%d.%d" % (p, j), 16, 257) for j in range(16)], [o[1]])
-        op("t", lambda: TE.matmul(o[0], T.IDN[:], T["YB%d" % p][:, 15:256:16, :], False, True),
-           [("IDN", 0, 128)] + [("YB%d.%d" % (p, j), 15, 256) for j in range(16)], [o[1]])
-
-    def unit(t, c, q):
-        i, o = B("psD%d" % (c & 1), 0, 256), B("U", 256 * c, 256 * c + 256)
-        if q == "v":
-            ts(o, i, -float(MT[t]), A_.is_lt)
-        else:
-            act(o, i, -1000.0, -1000.0 * (MT[t] + 0.5), F.Sigmoid)
-
-    def votes(c):
-        o, c0 = B("psV%d" % (c & 1), 0, 256), 256 * (c % 2)
-        mm(o, B("E0"), B("A16", c0, c0 + 256), True, False)
-        mm(o, B("E0"), B("JT", 0, 256), False, False)
-        mm(o, B("BOV"), B("U", 256 * c, 256 * c + 256), False, True)
-
-    def scanmin(o, i):
-        n = o[1][2] - o[1][1]
-        m = B("MKK", 0, n)
-        op("v", lambda: V.tensor_tensor_scan(o[0], m[0], i[0], 0.0, A_.mult, A_.min), [m[1], i[1]], [o[1]])
-
-    def best(c):
-        scanmin(B("K1", 256 * c, 256 * c + 256), B("psV%d" % (c & 1), 0, 256))
-
-    def post(t, b, x0, x1):
-        a0, n = BAT[b]
-        nq, e0, e1, w, m0 = n // 16, 16 * a0, 16 * (a0 + n), a0 + n, 2 * a0
-        I, O = "i%s%d" % (b, t), "o%s%d" % (b, t)
-        km = lambda: B("K1", e0 + 15, e1, 16)
-
-        def promoted():
-            for o, f, c in (("PRO", -1000.0, 2), ("NP", 1000.0, 3)):
-                x, y, z = B(o, a0, a0 + n), km(), B("THR", c, c + 1)
-                op("s", lambda: S.activation(x[0], y[0], F.Sigmoid, bias=z[0], scale=f), [y[1], z[1]], [x[1]])
-
-        def newc():
-            for k in range(16):
-                mm(B("psN", 0, n), B("SEL", 128 * k, 128 * k + 128), B("MK", e0 + k, e1, 16), k == 0, k == 15)
-
-        def sums():
-            mm(B("psS"), B("E0"), B("JT"), True, False)
-            mm(B("psS"), B("BOS"), B("PR", e0, e1), False, True)
-
-        def marks():
-            mm(B("psR", 0, n), B("IDH"), B("PEN" + b), True, False)
-            mm(B("psR", 0, n), B("BOH"), B("XX" + b), False, True)
-
-        def put():
-            x, e, z = B("VAL"), B("EL" + b), B("ZE" + b)
-            op("v", lambda: V.tensor_copy(x[0].indirect(e[0]), z[0]), [e[1], z[1]], [x[1]])
-        L = [
-            lambda: vcopy(B("KI" + b), km()),
-            lambda: ts(B("QI" + b), B("KI" + b), 1023, A_.bitwise_and),
-            lambda: vcopy(B("LU" + b), B("QI" + b)),
-            lambda: sgat(B("UX", e0, e1), B("U", e0, e1), B("LU" + b)),
-            lambda: tt(B("WI" + b), B("QI" + b), B("CW", 0, n), A_.add),
-            promoted,
-            lambda: vcopy(B("LW" + b), B("WI" + b)),
-            lambda: ttg(B("MK", e0, e1), B("OHT"), B("LU" + b), B("IF" + b), A_.mult),
-            newc,
-            lambda: ttg(B("PR", e0, e1), B("W", 16 * e0, 16 * e1), B("LW" + b), B("UX", e0, e1), A_.mult),
-            sums,
-            lambda: tt(B("PEN" + b), B("NP", a0, a0 + n), B("PENC", a0, a0 + n), A_.mult),
-            lambda: tt(B("DN" + b), B(I, n, 2 * n), B("NP", a0, a0 + n), A_.mult),
-            lambda: tt(B("NCG" + b), B("psN", 0, n), B("PRO", a0, a0 + n), A_.mult),
-            lambda: tt(B(O, 0, n), B("NCG" + b), B("DN" + b), A_.add),
-        ]
-        M = [
-            lambda: scanmin(B("K2", e0, e1), B("psS")),
-            lambda: vcopy(B("K2I" + b), B("K2", e0 + 15, e1, 16)),
-            lambda: ts(B("KR" + b), B("K2I" + b), 15, A_.bitwise_and),
-            lambda: ts(B("OHK" + b), B("KR" + b), B("PC", 0, 1), A_.is_equal),
-            lambda: tt(B("XX" + b), B("OHK" + b), B("NCG" + b), A_.mult),
-            marks,
-            lambda: tt(B("DM" + b), B("psR", 0, n), B("OHT", 0, n), A_.mult),
-            lambda: lin(b, B("PREP", a0, a0 + n), B("psR", 0, n), 0.49994, MAGIC),
-        ]
-        M += [lambda q=q: red(B("NL" + b, q, q + 1), B("DM" + b, 16 * q, 16 * q + 16), A_.add) for q in range(nq)]
-        M += [
-            lambda: ts(B("PCL" + b), B("NL" + b, 0, nq), 0.49994, A_.mult, MAGIC, A_.add),
-            lambda: lin(b, B("NM" + b), B("NL" + b, 0, nq), -1.0, 1.0),
-        ]
-        M += [lambda q=q: ts(B("EQ" + b, w * q, w * q + w), B("PREP", 0, w), B("PCL" + b, q, q + 1), A_.is_equal) for q in range(nq)]
-        M += [lambda: lin(b, B("FP" + b), B("PCL" + b), 4.0, -4.0 * MAGIC)]
-        N = [
-            lambda: tt(B("EM" + b, 0, nq * w), B("EQ" + b, 0, nq * w), B("LMT", m0, m0 + nq * w), A_.mult),
-            lambda: tt(B("NL" + b, nq, 2 * nq), B("FP" + b), B("NM" + b), A_.add),
-        ]
-        N += [lambda q=q: red(B("DV" + b, q, q + 1), B("EM" + b, w * q, w * q + w), A_.max) for q in range(nq)]
-        N += [
-            lambda: ts(B("DV" + b, nq, 2 * nq), B("DV" + b, 0, nq), 1.0 + 2.0 ** -11, A_.mult),
-            lambda: tt(B("OL" + b), B("NL" + b), B("DV" + b), A_.max),
-            lambda: vcopy(B("EL" + b), B("OL" + b)),
-        ]
-        E = [
-            lambda: ttg(B("YE" + b), B("VAL"), B("EL" + b), B("DC"), A_.add),
-            lambda: ts(B("ZE" + b), B("YE" + b), 255.0, A_.min, 0.0, A_.max),
-            put,
-        ]
-        return L + _weave(M, x0) + N[:2] + _weave(N[2:], x1), E
-
-    def newmarks(t, b):
-        n = BAT[b][1]
-        I, O = "i%s%d" % (b, t), "o%s%d" % (b, t)
-        old = lambda: B(I, 2 * n, 2 * n + n // 8)
-        return [
-            lambda: ts(B("KP" + b), B("NL" + b), 2047.5, A_.is_lt),
-            lambda: tt(B("DL" + b), B("NL" + b), old(), A_.subtract),
-            lambda: tt(B("DK" + b), B("DL" + b), B("KP" + b), A_.mult),
-            lambda: tt(B(O, 2 * n, 2 * n + n // 8), B("DK" + b), old(), A_.add),
-        ]
-
-    def parity(t):
-        return [
-            lambda: red(B("THR", 1, 2), B("PRO"), A_.add),
-            lambda: vcopy(B("TI", 0, 1), B("THR", 1, 2)),
-            lambda: ts(B("TI", 1, 2), B("TI", 0, 1), 1, A_.bitwise_and),
-            lambda: ts(B("THR", 2, 3), B("TI", 1, 2), -1024000.0, A_.mult, -1024000.0 * (AT[t] - 1) - 500.0, A_.add),
-            lambda: ts(B("THR", 3, 4), B("TI", 1, 2), 1024000.0, A_.mult, 1024000.0 * (AT[t] - 1) + 500.0, A_.add),
-        ]
+    gat("v", B("FX"), B("XCD"), B("LC"))
+    turn(B("FT"), B("FX"))
+    vcopy(B("ML", 0, 4), B("XL"))
+    pair_of(B("ML", 0, 4), B("ML", 4, 8), 4)
+    for s in (0, 1):
+        mms(B("psE", 4 * s, 4 * s + 4), [(move("IW", s, q), B("ML", q, 8, 2)) for q in (0, 1)])
+    for s in (0, 1):
+        vcopy(B("i%d" % s, 64, 68), B("psE", 4 * s, 4 * s + 4))
+        for x in range(4):
+            vcopy(B("i%d" % s, 16 * x, 16 * x + 16), B("FT", 32 * x + 16 * s, 32 * x + 16 * s + 16))
+    for c in (0, 512):
+        vcopy(B("G16", c, c + 512), B("GEN", c, c + 512))
+        ts(B("A16", c, c + 512), B("G16", c, c + 512), 0.5, A_.mult, 1023.8, A_.add)
+    for s in (0, 1):
+        for c in (0, 1):
+            c0, c1, ev, od = 512 * c, 512 * c + 512, B(("psS", "psE")[c]), B(("psP", "psK1")[c])
+            mm(ev, B("R%d" % s), B("G16", c0, c1), True, True)
+            mms(od, [(B("R%d" % s), B("A16", c0, c1)), (B("RM%d" % s), B("G16", c0, c1))])
+            act(B("PT%d" % s, 2 * c0, 2 * c1, 2), ev, 1.0, 0.0)
+            if s == 0:
+                ts(B("PT%d" % s, 2 * c0 + 1, 2 * c1, 2), od, 4.0, A_.mult, -4095.0, A_.add)
+            else:
+                act(B("PT%d" % s, 2 * c0 + 1, 2 * c1, 2), od, 4.0, -4095.0)
 
     src, hand, dst = _route(rank, T, topo)
-    sent = [0]
-
-    def send(t, b):
-        if t == NR_ - 1:
-            return
-        o = B("o%s%d" % (b, t))
-        need("g", [o[1]], [])
-        to = hand if hand is not None else dst
-        sent[0] += _send(g, T, topo, core, to, o[0], "i%s%d" % (b, t + 1), "a%s%d" % (b, t + 1))
-
+    to = hand if hand is not None else dst
     into = _route((rank - 3) % len(T.cores), T, topo)
     arr = _mask(into[1] if into[1] is not None else into[0], core, topo)[1]
+    edge = [sum(P["ch"][:c]) for c in range(len(P["ch"]) + 1)]
 
-    def arrive(t):
-        for b in BAT:
-            i, sem = B("i%s%d" % (b, t)), "a%s%d" % (b, t)
-            total[sem] = arr
-            note("rem" + sem, [], [i[1]], (sem, arr))
+    before = []
+    for n in range(2 * NR_):
+        s, t, I, O = n % 2, n // 2, "i%d" % n, "o%d" % n
+        val, W, U, IMT, LI = B("VAL%d" % s), "W%d" % s, "U%d" % s, "IMT%d" % s, "LI%d" % s
 
-    def store(q, y, nm, sem, c1):
-        o = B(nm, 0, c1)
-        dma(q, y[:], o[0], [o[1]], [], sem)
+        vcopy(B("LL"), B(I, 64, 68))
+        gat("v", B("XV"), val, B("LL"))
+        tt(B("LE"), B("XV", 0, 32), B("XV", 32, 64), A_.is_lt)
+        mm(B("psR", 0, 64), IDN, B("ZC"), True, False)
+        for x in range(8):
+            c, h = 16 * (x // 2), x % 2
+            mm(B("psR", c, c + 16), move(("BN", "BP")[x // 4], x // 2 % 2, h), B("LE", 16 * h, 16 * h + 16), False, x == 7)
+        tt(B("CD"), B(I, 0, 64), B("psR", 0, 64), A_.min)
+        tt(B(O, 32, 64), B("CD", 0, 32), B("CD", 32, 64), A_.max)
+        for l in (0, 1):
+            mms(B("psR", l, 32, 2), [(move("IW", l, h), B(O, 32 + 16 * h, 48 + 16 * h)) for h in (0, 1)])
+        vcopy(B("CU"), B("psR", 0, 32))
+        mm(B("psR", 0, 32), IDN, B(I, 32, 64), True, True)
+        act(B(IMT, 512, 544), B("psR", 0, 32), 1.0, 0.0)
+        p0 = 0
+        for w in P["ic"]:
+            c0, c1 = 32 * p0, 32 * (p0 + w)
+            gat(P["img"], B("IMG", c0, c1), B("PT%d" % s), B("CU", 2 * p0, 2 * (p0 + w)))
+            turn(B(IMT, c0, c1), B("IMG", c0, c1))
+            vcopy(B(LI, c0, c1), B(IMT, c0, c1))
+            p0 += w
 
-    def outputs(q, part, fx, z, zt, y, yd, sem):
-        t = NR_ - 1
-        L = [lambda b=b: vcopy(B(fx, BAT[b][0], sum(BAT[b])), B("o%s%d" % (b, t), part * BAT[b][1], (part + 1) * BAT[b][1])) for b in BAT]
-        return L + flip("s", z, zt, lambda x: B(fx, 16 * x, 16 * x + 16), lambda x: B(y, x, 64, 4)) + [lambda: store(q, yd, y, sem, 64)]
+        K = B("psK%d" % s, 0, 32)
+        mm(K, IDN, B("IDX"), True, False)
+        for c in range(len(P["ch"])):
+            p0, p1 = edge[c], edge[c + 1]
+            c0, c1, d = 512 * p0, 512 * p1, B("psD%d" % (c & 1), 0, 32 * (p1 - p0))
+            x = gat("v" if (n, c) in P["vg"] or c in P["vg"] else "s", B(W, c0, c1), val, B(LI, 32 * p0, 32 * p1), after=before)
+            before = before if x is None else [x]
+            scan(B("SB", c0 + 1, c1 + 1), B(W, c0, c1), B("MSK", 0, c1 - c0), 0.0, A_.max, A_.mult)
+            scan(B("YB", c0, c1), B(W, c0, c1), B("SB", c0, c1), 0.0, A_.max, A_.min)
+            mms(d, [(IDN, B("SB", c0 + 16, c1 + 1, 16)), (IDN, B("YB", c0 + 15, c1, 16))])
+            if c < P["sunit"]:
+                act(B(U, 32 * p0, 32 * p1), d, -1000.0, -1000.0 * (MT[t] + 0.5), F.Sigmoid)
+            else:
+                ts(B(U, 32 * p0, 32 * p1), d, -float(MT[t]), A_.is_lt)
+            for p in range(p0, p1):
+                mm(K, sel(p), B(U, 32 * p, 32 * p + 32), False, p == 15)
 
-    for t in range(NR_):
-        last = t == NR_ - 1
-        if t:
-            arrive(t)
-        _go(step1(t, "A"))
-        image("A", 0, 16)
-        values(sgat, 0, 16 - NV)
-        image("A", 16, 32)
-        if t == 0:
-            late_constants()
-        values(vgat, 16 - NV, 16)
-        values(sgat, 16, 32)
-        imf("A")
-        _go(_weave(scans(0), (parity(t) if t else []) + step1(t, "B") + [lambda: image("B", 32, 48)], 0.3))
-        values(sgat, 32, 40)
-        diff(0)
-        unit(t, 0, "s")
-        votes(0)
-        values(sgat, 40, 48)
-        _go(_weave(scans(1), [lambda: image("B", 48, 64), lambda: best(0)], 0.1))
-        diff(1)
-        unit(t, 1, "v")
-        votes(1)
-        if t == 0:
-            vcopy(B("SEL"), B("SL0"))
-        best(1)
-        chain, late = post(t, "A", [], newmarks(t, "A"))
-        _go(chain[:6])
-        values(sgat, 48, 64)
-        imf("B")
-        _go(chain[6:PRE])
-        _go(_weave(scans(2), chain[PRE:] + [lambda: send(t, "A")]))
-        diff(2)
-        unit(t, 2, "s")
-        votes(2)
-        _go(_weave(scans(3), [lambda: best(2)], 0.2))
-        diff(3)
-        late[0]()
-        unit(t, 3, "v")
-        votes(3)
-        _go(late[1:])
-        best(3)
-        x0 = outputs("s", 1, "FX2", "Z2", "ZT2", "YD", T.yd, "st2") + outputs("y", 0, "FX", "Z", "ZT", "YC", T.yc, "st1") if last else []
-        chain, late = post(t, "B", x0, newmarks(t, "B"))
-        _go(chain)
-        send(t, "B")
-        _go(late)
+        M2 = 32768.0 * MAGIC
+        scan(B("K1"), B("THK%d" % s), K, -BIG, A_.max, A_.min)
+        ts(B("RR"), B("K1", 15, 32, 16), M2, A_.add, M2, A_.subtract)
+        for q in (0, 1):
+            ts(B("LW", q, 32, 2), B("B64", 0, 16), col("K1", 16 * q + 15), A_.add, col("RR", q), A_.subtract)
+        ts(B("LU"), B("LW"), 1.0 / 16, A_.mult, -0.47, A_.add)
 
-    store("y", T.yv, "VAL", "st0", 2048)
-    for b in BAT:
-        a0, n = BAT[b]
-        vcopy(B("YL", a0 // 16, (a0 + n) // 16), B("o%s%d" % (b, NR_ - 1), 2 * n, 2 * n + n // 16))
-    store("s", T.yl, "YL", "st3", 4)
-    total["ls"] = sent[0]
-    for s in total:
-        if total[s]:
-            g.wait_ge(T.sem[s], total[s])
+        gat("v", B(O, 0, 32), B(IMT), B("LU", 0, 2))
+        mm(B("psS", 32, 64), IDN, B(O, 0, 32), True, True)
+        mm(B("psS", 0, 32), IDN, B("KC"), True, False)
+        for x in (0, 1):
+            c0, c1 = 256 * x, 256 * x + 256
+            gat(P["ux"], B("UX", c0, c1), B(U), B("LU", 16 * x, 16 * x + 16), scale=-1.0)
+            if P["prs"]:
+                gat("s", B("WS", c0, c1), B(W), B("LW", 16 * x, 16 * x + 16))
+                scan(B("PR", c0, c1), B("WS", c0, c1), B("UX", c0, c1), 0.0, A_.max, A_.mult)
+            else:
+                ttg(B("PR", c0, c1), B(W), B("LW", 16 * x, 16 * x + 16), B("UX", c0, c1), A_.mult)
+            for k in range(8 * x, 8 * x + 8):
+                mm(B("psS", 0, 32), sel(k), B("PR", 32 * k, 32 * k + 32), False, k == 15)
+        turn(B("KT"), B("psS", 0, 64))
+        scan(B("K2"), B("TH2"), B("KT", 0, 32), BIG, A_.min, A_.max)
+        for h in (0, 1):
+            ts(B("XD", 16 * h, 16 * h + 16), B("KT", 16 * h, 16 * h + 16), col("K2", 16 * h + 15), A_.subtract)
+        ts(B("AA"), B("K2", 15, 32, 16), 5000.0, A_.is_gt, -4096.0, A_.mult)
+        tt(B("XX", 1, 33), B("XD"), B("KT", 32, 64), A_.add)
+        tt(B("XX", 0, 34, 33), B(I, 64, 66), B("AA"), A_.add)
+        for h in (0, 1):
+            red(col(O, 64 + h), B("XX", 17 * h, 17 * h + 17), A_.max)
+        pair_of(B(O, 64, 66), B(O, 66, 68), 2)
+        if t < NR_ - 1:
+            sent = op("g", lambda n=n: _send(g, T, topo, core, to, T["o%d" % n][:], "i%d" % (n + 2), "a%d" % (n + 2)), [B(O)[1]], [], 300.0,
+                      ev=("ls", (n + 1) * _mask(core, to, topo)[1]))
+            op("in%d" % n, None, [], [B("i%d" % (n + 2))[1]], 0.0, P["hop"], ("a%d" % (n + 2), arr), [sent])
+
+        tt(B("EQ", 0, 130, 129), B("AA"), B("PC", 5, 7), A_.add)
+        tt(B("PK"), B("PR2", 0, 2), B("EQ", 0, 130, 129), A_.max)
+        for h in (0, 1):
+            ts(B("XH", 32 * h, 32 * h + 32), B("OH"), col("PK", h), A_.mult)
+        for h in (0, 1):
+            mms(B("psP", 64 * h, 64 * h + 64), [(IDN, B("FAR", 64 * h, 64 * h + 64)), (B("B32"), B("XH"))])
+        for h in (0, 1):
+            ts(B("EQ", 64 * h + 1, 64 * h + 65), B("psP", 64 * h, 64 * h + 64), col("PK", h), A_.is_equal, col("PC", 5 + h), A_.mult)
+        scan(B("DV", 0, 130), B("MK2"), B("EQ"), 0.0, A_.mult, A_.max)
+        ts(B("DV", 194, 260, 65), B("DV", 64, 130, 65), 1.0625, A_.mult)
+        tt(B("EE"), B(O, 64, 68), B("DV", 64, 260, 65), A_.max)
+        for x in range(4):
+            mm(B("psE", 2 * x, 2 * x + 2), B("R%d" % (x % 2)), B("EE", x // 2 * 2, x // 2 * 2 + 2), True, True)
+        vcopy(B("EL"), B("psE", 0, 8))
+        ts(B("ZE", 0, 64), val, 32.0, A_.add, 255.0, A_.min, B("EL", 0, 4))
+        if P["down"] == "s" and n < 9:
+            gat("s", B("ZE", 64, 128), val, B("EL", 4, 8), F.Relu, 1.0, -32.0)
+        else:
+            ts(B("ZE", 64, 128), val, -32.0, A_.add, 0.0, A_.max, B("EL", 4, 8))
+        vput(val, B("EL"), B("ZE"))
+
+        if t < NR_ - 1:
+            c = col("psE", 0)
+            mms(c, [(B("B32"), col("AA", h)) for h in (0, 1)])
+            if P["par"] == "s":
+                act(col("TB", 0), c, -0.49994 / 4096, MAGIC)
+                act(col("TB", 1), col("TB", 0), 65536.0, -65536.0 * MAGIC)
+                act(col("TB", 2), c, 8.0, col("TB", 1), F.Identity)
+                act(B("THK%d" % s, 0, 32, 16), B("KB", 2 * t + 2, 2 * t + 4), 1.0, col("TB", 2), F.Identity)
+            else:
+                ts(col("TI", 0), c, -1.0 / 4096, A_.mult)
+                ts(col("TI", 1), col("TI", 0), 1, A_.bitwise_and)
+                ts(col("TB", 0), col("TI", 1), float(AT[t + 1]), A_.add, -32768.0, A_.mult)
+                ts(B("THK%d" % s, 0, 32, 16), B("KB", 0, 2), col("TB", 0), A_.add)
+        else:
+            rows = [(T.yv[32 * a + 16 * s:32 * a + 16 * s + 16, :], T["VAL%d" % s][32 * a:32 * a + 16, 0:2048]) for a in range(4)]
+            dmas("y", rows[:4 - 2 * s], [val[1]], [], "stv%d" % s)
+            if s:
+                dmas("s", rows[2:], [val[1]], [], "stw1")
+            for x in range(4):
+                vcopy(B("GT", 32 * x + 16 * s, 32 * x + 16 * s + 16), B(O, 16 * x, 16 * x + 16))
+
+    turn(B("GU"), B("GT"))
+    vput(B("YCD"), B("LC"), B("GU"))
+    dmas("y", [(T.yc[:], T.YCD[:, 0:64])], [B("YCD")[1]], [], "stc")
+    dmas("s", [(T.yd[:], T.YCD[:, 64:128])], [B("YCD")[1]], [], "std")
+    for q in (0, 1):
+        mms(B("psR", 2 * q, 2 * q + 2), [(move("IW", q, s), B("o%d" % (8 + s), 64, 66)) for s in (0, 1)])
+    for q in (0, 1):
+        vcopy(B("YL", q, 4, 2), B("psR", 2 * q, 2 * q + 2))
+    dmas("y", [(T.yl[:], T.YL[:])], [B("YL")[1]], [], "stl")
+    issue()

@@ -4,27 +4,27 @@ A_ = AluOpType
 F = ActivationFunctionType
 X_ = AxisListType.X
 NR_ = 5
-PAR = dict(ch=(2, 2, 2, 2, 2, 2, 2, 1, 1), sunit=0, img="s", ux="s", prs=0, par="v", down="v", ic=(4, 12), vg=(),
-           cyc=1.0, gat=1.5, put=3.5, fix=40, wake=70, hop=4500, dma=4000, slack=100)
+PAR = dict(ch=(2, 2, 2, 2, 2, 2, 2, 1, 1), sunit=0, img="s", ws="vv", pt="ssssvvvv", pe=60, par="s", down="s", ic=(4, 12), vg=(), sc=512, i16=0,
+           cyc=1.0, gat=1.5, put=3.5, fix=10, wake=100, hop=4500, dma=4000, slack=30)
 VW = 2320
 BIG = 1.0e9
 MAGIC = 12582912.0
 
 SCRATCH = {}
-for _d, _names in (("int32", "GEN 1024 XCD 128 XL 4 PI 4 LC0 8 TI 2 PR2 4"),
+for _d, _names in (("int32", "GEN 1024 XCD 128 XL 4 PI 4 LC0 8 LZ0 2 TI 2 PR2 4"),
                    ("float32", "PT0 2048 PT1 2048 IMG 512 IMT0 544 IMT1 544 PC 16 B64 64 IX0 32 KB 12 THK0 32 THK1 32 TH2 32 K1 32 RR 2 "
-                               "KT 64 K2 32 XD 32 XX 34 U4 4 PK 2 TB 4 GT 128 GU 128 YCD 128 YL 4"),
-                   ("bfloat16", "VAL0 %d VAL1 %d W0 8704 W1 8704 SB 8208 YB 8192 U0 544 U1 544 UX 512 WS 512 PR 512 MSK 2048 ONE 160 NEG 144 B1 160 "
-                                "BW 160 BP0 160 BP1 160 BN0 160 BN1 160 IW 160 IW0 160 IW1 160 SL1 144 SL2 144 SEL 144 R0 128 R1 128 RM0 128 RM1 128 "
+                               "NCT 32 LN 64 K2 32 XD 32 XX 34 U4 4 PK 2 TB 4 GT 128 GU 128 YCD 128 YL 4"),
+                   ("bfloat16", "VAL0 %d VAL1 %d W0 8704 W1 8704 SB 8208 YB 8192 U0 544 U1 544 UC 32 WS 512 ZU 4096 MSK 2048 ONE 160 NEG 144 B1 128 "
+                                "BW 128 BP 128 BN 128 IW 160 IW0 160 IW1 160 SL1 144 SL2 144 SEL 144 R0 128 R1 128 RM0 128 RM1 128 "
                                 "B2 128 B32 128 OH 32 KC 32 FAR 128 XV 64 LE 32 ZE 128 ZC 64 MK2 130" % (VW, VW)),
-                   ("float16", "G16 1024 A16 1024 FX 128 FT 128 ML 8 IDX 32 AA 2 XH 64 EE 4 EQ 130 DV 260 CD 64"),
-                   ("uint16", "LC 8 LL 4 CU 32 LI0 512 LI1 512 LW 32 LU 32 EL 8")):
+                   ("float16", "G16 1024 A16 1024 FX 128 FT 128 ML 8 IDX 32 AA 2 XH 64 EE 4 EQ 130 DV 260 CD 64 IH 512 IT 512"),
+                   ("uint16", "LC 8 LL 4 CU 32 LI0 512 LI1 512 LW 32 LU 2 LZ 2 EL 8")):
     _w = _names.split()
     for _i in range(0, len(_w), 2):
         SCRATCH[_w[_i]] = ("sbuf", [128, int(_w[_i + 1])], _d)
 for _n in "psD0 psD1 psK0 psK1 psS psR psP psE".split():
     SCRATCH[_n] = ("psum", [128, 512], "float32")
-SEMAPHORES = "vc sc tc gc ls ldg ldc ldl ldv0 ldv1 stv0 stv1 stw1 stc std stl".split()
+SEMAPHORES = "vc sc tc gc ls ldg0 ldg1 ldc ldl ldv0 ldv1 stv0 stv1 stw1 stc std stl".split()
 for _n in range(2 * NR_):
     SCRATCH["i%d" % _n] = ("sbuf", [128, 68], "float16")
     SCRATCH["o%d" % _n] = ("sbuf", [128, 68], "float16")
@@ -75,15 +75,24 @@ def _inside(a, b):
     return a == b or (b.step == 1 and b[0] <= a[0] and a[-1] <= b[-1])
 
 
+_DONE = {}
+
+
 def _order(calls):
+    if len(calls) in _DONE:
+        return _DONE[len(calls)]
     P = PAR
     users = [[] for c in calls]
     for i, c in enumerate(calls):
         for d in c["deps"]:
             users[d].append(i)
+
+    def gap(i, u):
+        same = calls[i]["q"] == calls[u]["q"] and (calls[i]["q"] == "t" or i in calls[u]["free"])
+        return 0.0 if same else calls[i]["late"] + P["wake"]
     way = [0.0] * len(calls)
     for i in reversed(range(len(calls))):
-        way[i] = calls[i]["busy"] + calls[i]["late"] + max([way[u] + P["wake"] for u in users[i]], default=0.0)
+        way[i] = calls[i]["busy"] + max([way[u] + gap(i, u) for u in users[i]], default=calls[i]["late"])
     left = [len(c["deps"]) for c in calls]
     at = [0.0] * len(calls)
     ready = {}
@@ -100,10 +109,11 @@ def _order(calls):
         out.append(i)
         free[q] = max(now, at[i]) + calls[i]["busy"]
         for u in users[i]:
-            at[u] = max(at[u], free[q] + calls[i]["late"] + (0.0 if calls[u]["q"] == q == "t" else P["wake"]))
+            at[u] = max(at[u], free[q] + gap(i, u))
             left[u] -= 1
             if not left[u]:
                 ready[calls[u]["q"]].append(u)
+    _DONE[len(calls)] = out
     return out
 
 
@@ -122,14 +132,14 @@ def rank_program(g, core, T, topo):
         for keys, wr in ((reads, False), (writes, True)):
             for key, r in keys:
                 for h in hist.get(key, ()):
-                    if (wr or h[1] or key[:2] == "ps") and _meet(r, h[0]):
+                    if (wr or h[1] or (key[:2] == "ps" and h[3] != q)) and _meet(r, h[0]):
                         deps.add(h[2])
         for keys, wr in ((reads, False), (writes, True)):
             for key, r in keys:
                 L = hist.setdefault(key, [])
-                if wr or key[:2] == "ps":
+                if wr:
                     L[:] = [h for h in L if not _inside(h[0], r)]
-                L.append((r, wr, me))
+                L.append((r, wr, me, q))
         deps.discard(me)
         calls.append(dict(q=q, fn=fn, deps=deps, free=set(after), busy=busy, late=late, ev=ev))
         return me
@@ -162,11 +172,11 @@ def rank_program(g, core, T, topo):
         for s in total:
             g.wait_ge(T.sem[s], total[s])
 
-    def dmas(q, pairs, reads, writes, sem):
+    def dmas(q, pairs, reads, writes, sem, late=None, after=()):
         def fn():
             for o, s in pairs:
                 eng[q].dma_start(o, s).then_inc(T.sem[sem], 16)
-        op(q, fn, reads, writes, 60.0 * len(pairs), P["dma"], (sem, 16 * len(pairs)))
+        return op(q, fn, reads, writes, 60.0 * len(pairs), late or P["dma"], (sem, 16 * len(pairs)), after)
 
     def B(name, c0=0, c1=None, st=1):
         c1 = SCRATCH[name][1][1] if c1 is None else c1
@@ -186,14 +196,10 @@ def rank_program(g, core, T, topo):
     def vcopy(o, i):
         op("v", lambda: V.tensor_copy(o[0], i[0]), [i[1]], [o[1]], cost(o, i))
 
-    def gat(q, o, win, off, f=F.Copy, scale=1.0, bias=0.0, after=()):
+    def gat(q, o, win, off, f=F.Copy, bias=0.0, after=()):
         if q == "s":
-            return op("s", lambda: S.activation(o[0], win[0].indirect(off[0]), f, bias=bias, scale=scale), [win[1], off[1]], [o[1]],
-                      picked(o[2]), after=after)
-        elif scale != 1.0:
-            ts(o, win, scale, A_.mult, off=off)
-        else:
-            op("v", lambda: V.tensor_copy(o[0], win[0].indirect(off[0])), [win[1], off[1]], [o[1]], picked(o[2]))
+            return op("s", lambda: S.activation(o[0], win[0].indirect(off[0]), f, bias=bias), [win[1], off[1]], [o[1]], picked(o[2]), after=after)
+        op("v", lambda: V.tensor_copy(o[0], win[0].indirect(off[0])), [win[1], off[1]], [o[1]], picked(o[2]))
 
     def vput(win, off, i):
         op("v", lambda: V.tensor_copy(win[0].indirect(off[0]), i[0]), [off[1], i[1]], [win[1]], picked(i[2], "put"))
@@ -205,9 +211,6 @@ def rank_program(g, core, T, topo):
 
     def tt(o, a, b, f):
         op("v", lambda: V.tensor_tensor(o[0], a[0], b[0], f), [a[1], b[1]], [o[1]], P["fix"] + P["cyc"] * max(64, 2 * o[2]))
-
-    def ttg(o, win, off, b, f):
-        op("v", lambda: V.tensor_tensor(o[0], win[0].indirect(off[0]), b[0], f), [win[1], off[1], b[1]], [o[1]], picked(o[2]))
 
     def ts(o, a, s1, f1, s2=None, f2=None, off=None):
         rd = [a[1]] + [s[1] for s in (s1, s2, off) if isinstance(s, tuple)]
@@ -228,8 +231,8 @@ def rank_program(g, core, T, topo):
     def ms(o, c):
         op("v", lambda: V.memset(o[0], c), [], [o[1]], cost(o))
 
-    def mm(o, l, r, st, sp):
-        op("t", lambda: TE.matmul(o[0], l[0], r[0], st, sp), [l[1], r[1]], [o[1]], P["cyc"] * max(64, r[2]), P["wake"])
+    def mm(o, l, r, st, sp, after=()):
+        op("t", lambda: TE.matmul(o[0], l[0], r[0], st, sp), [l[1], r[1]], [o[1]], P["cyc"] * max(64, r[2]), P["pe"], after=after)
 
     def mms(o, pairs):
         for i, (l, r) in enumerate(pairs):
@@ -242,71 +245,74 @@ def rank_program(g, core, T, topo):
     def asel(o, i, pat, f, base, ch):
         op("g", lambda: g.affine_select(o[0], i[0], pat, f, 0.0, base, ch), [i[1]], [o[1]], 200 + 2 * P["cyc"] * o[2])
 
-    def move(w, h, l):
+    def move(h, l):
         c = 16 + 16 * (h - l)
-        return B("%s%d" % (w, h), c, c + 128)
+        return B("IW%d" % h, c, c + 128)
 
     IDN = B("IW", 16, 144)
 
-    def sel(p):
-        return B("SEL", 15 - p, 143 - p)
-
-    dmas("s", [(T.GEN[:], T.gen[:])], [], [B("GEN")[1]], "ldg")
-    dmas("y", [(T.XCD[:, 0:64], T.cla[:]), (T.XCD[:, 64:128], T.par[:])], [], [B("XCD")[1]], "ldc")
-    dmas("y", [(T.XL[:], T.lit[:])], [], [B("XL")[1]], "ldl")
+    x = [dmas("s", [(T.GEN[:, 0:512], T.gen[:, 0:512])], [], [B("GEN", 0, 512)[1]], "ldg0", P["dma"] - 800)]
+    dmas("s", [(T.GEN[:, 512:1024], T.gen[:, 512:1024])], [], [B("GEN", 512, 1024)[1]], "ldg1", P["dma"] - 400, x)
+    x = [dmas("y", [(T.XL[:], T.lit[:])], [], [B("XL")[1]], "ldl", P["dma"] - 800)]
+    x = [dmas("y", [(T.XCD[:, 0:64], T.cla[:]), (T.XCD[:, 64:128], T.par[:])], [], [B("XCD")[1]], "ldc", P["dma"] - 400, x)]
     for s in (0, 1):
-        dmas("y", [(T["VAL%d" % s][16 * x:16 * x + 16, 0:2048], T.val[32 * (x // 2) + 16 * s:32 * (x // 2) + 16 * s + 16, :]) for x in range(8)],
-             [], [B("VAL%d" % s, 0, 2048)[1]], "ldv%d" % s)
+        x = [dmas("y", [(T["VAL%d" % s][16 * x:16 * x + 16, 0:2048], T.val[32 * (x // 2) + 16 * s:32 * (x // 2) + 16 * s + 16, :]) for x in range(8)],
+                  [], [B("VAL%d" % s, 0, 2048)[1]], "ldv%d" % s, P["dma"] + 1000 + 2000 * s, x)]
 
     iota(col("PI", 0), [[1, 1]], 0, 1, True)
     ms(B("ONE"), 1.0)
     asel(B("IW"), B("ONE"), [[-1, 160]], A_.is_equal, 16, 1)
     iota(B("LC0"), [[64, 2], [1, 2], [2, 2]], 0, 0, True)
-    asel(B("B1"), B("ONE"), [[-16, 10], [0, 16]], A_.is_ge, 16, 1)
-    asel(B("BW"), B("B1"), [[16, 10], [0, 16]], A_.is_ge, -1, -1)
+    asel(B("B1"), B("ONE", 0, 128), [[-16, 8], [0, 16]], A_.is_ge, 0, 1)
+    asel(B("BW"), B("B1"), [[16, 8], [0, 16]], A_.is_ge, 15, -1)
     ms(B("NEG"), -32768.0)
     for c, m in ((1, 15), (2, 16), (3, 31)):
         ts(col("PI", c), col("PI", 0), m, A_.bitwise_and)
+    vcopy(B("PC", 11, 13), B("PI", 2, 4))
     for h in (0, 1):
         ts(col("PC", 1 + h), col("PI", 2), 16.0 * h, A_.is_equal)
-        ts(col("PC", 3 + h), col("PI", 3), 32.0 * h, A_.add)
+        ts(col("PC", 3 + h), col("PI", 3), col("PC", 11), A_.add, 16.0 * h, A_.add)
     ts(B("PC", 5, 7), B("PC", 3, 5), 2.0, A_.mult, 2048.0, A_.add)
-    for c, m in ((7, 4.0), (8, 512.0), (9, 16.0), (10, -2048.0)):
+    for c, m in ((7, 4.0), (8, 512.0), (9, 16.0), (10, 128.0)):
         ts(col("PC", c), col("PI", 1), m, A_.mult)
     ts(B("LC"), B("LC0"), col("PC", 7), A_.add)
     for h in (0, 1):
         ts(B("IW%d" % h), B("IW"), col("PC", 1 + h), A_.mult)
-        tt(B("R%d" % h), move("IW", h, 0), move("IW", h, 1), A_.add)
+        tt(B("R%d" % h), move(h, 0), move(h, 1), A_.add)
         ts(B("RM%d" % h), B("R%d" % h), -0.25, A_.mult)
-        ts(B("BP%d" % h), B("BW"), col("PC", 1 + h), A_.mult, 4096.0, A_.mult)
-        ts(B("BN%d" % h), B("BW"), col("PC", 1 + h), A_.mult, -4096.0, A_.mult)
+        ts(B(("BP", "BN")[h]), B("BW"), 4096.0 * (1 - 2 * h), A_.mult)
         ms(B("ZC", 32 * h, 32 * h + 32), 8.5 * 4096.0 * (1 - 2 * h))
     iota(B("B64"), [[1, 64]], 0, 0)
     iota(B("IX0"), [[16, 32]], 0, 0)
+    iota(B("LN"), [[16, 2], [32, 2], [1, 16]], 0, 0)
+    iota(B("KC"), [[0, 2], [-2048, 16]], 0, 0)
+    iota(B("LZ0"), [[2048, 2]], 0, 1, True)
+    ts(B("LZ"), B("LZ0"), col("PC", 10), A_.add)
     asel(B("SL1"), B("NEG"), [[-16, 9], [0, 16]], A_.is_ge, 0, 1)
     asel(B("SL2"), B("SL1"), [[16, 9], [0, 16]], A_.is_ge, 15, -1)
     asel(B("SEL"), B("SL2"), [[0, 9], [1, 16]], A_.is_equal, -15, 0)
     asel(B("B2"), B("ONE", 0, 128), [[-32, 4], [0, 32]], A_.is_ge, 0, 1)
     asel(B("B32"), B("B2"), [[32, 4], [0, 32]], A_.is_ge, 31, -1)
-    wide = 512 * max(P["ch"])
-    ms(B("MSK", 0, wide), 1.0)
-    ms(B("MSK", 15, wide, 16), -1.0)
+    for c in range(0, 4096, 1024):
+        iota(B("ZU", c, c + 1024), [[0, 1024]], 0, 0)
+    for s in (0, 1):
+        iota(B("W%d" % s, 8192, 8704), [[0, 512]], 0, 0)
+        iota(B("U%d" % s, 512, 544), [[0, 32]], 0, 0)
+    iota(B("YCD"), [[0, 128]], 0, 0)
+    ms(B("MSK", 0, P["sc"]), 1.0)
+    ms(B("MSK", 15, P["sc"], 16), -1.0)
     ms(B("SB", 0, 1), 0.0)
     ms(B("TH2"), BIG)
     ms(B("TH2", 0, 32, 16), 4096.0)
     ms(B("MK2"), 1.0)
     ms(B("MK2", 0, 130, 65), 0.0)
-    ms(B("YCD"), 0.0)
     ts(B("IDX"), B("IX0"), col("PC", 8), A_.add)
     ts(B("KB", 0, 2), B("IX0", 0, 32, 16), 8192.0, A_.add, col("PC", 9), A_.add)
-    ts(B("KC"), B("ONE", 0, 32), col("PC", 10), A_.mult)
-    ts(B("OH"), B("B64", 0, 32), col("PC", 3), A_.is_equal)
+    ts(B("OH"), B("B64", 0, 32), col("PC", 12), A_.is_equal)
     for s in (0, 1):
         ms(B("VAL%d" % s, 2048, VW), 0.0)
-        ms(B("W%d" % s, 8192, 8704), 0.0)
-        ms(B("U%d" % s, 512, 544), 0.0)
         ms(B("THK%d" % s), -BIG)
-        ts(B("FAR", 64 * s, 64 * s + 64), B("B64"), col("PC", 3 + s), A_.is_ge, 4096.0, A_.mult)
+        ts(B("FAR", 64 * s, 64 * s + 64), B("LN"), col("PC", 3 + s), A_.is_ge, 4096.0, A_.mult)
         ts(B("THK%d" % s, 0, 32, 16), B("KB", 0, 2), -32768.0 * AT[0], A_.add)
     if P["par"] == "s":
         for t in range(1, NR_):
@@ -321,8 +327,9 @@ def rank_program(g, core, T, topo):
     turn(B("FT"), B("FX"))
     vcopy(B("ML", 0, 4), B("XL"))
     pair_of(B("ML", 0, 4), B("ML", 4, 8), 4)
-    for s in (0, 1):
-        mms(B("psE", 4 * s, 4 * s + 4), [(move("IW", s, q), B("ML", q, 8, 2)) for q in (0, 1)])
+    for x in range(4):
+        c = 4 * (x % 2)
+        mms(B("psE", 2 * x, 2 * x + 2), [(move(x // 2, h), B("ML", c + 2 * h, c + 2 * h + 2)) for h in (0, 1)])
     for s in (0, 1):
         vcopy(B("i%d" % s, 64, 68), B("psE", 4 * s, 4 * s + 4))
         for x in range(4):
@@ -330,16 +337,20 @@ def rank_program(g, core, T, topo):
     for c in (0, 512):
         vcopy(B("G16", c, c + 512), B("GEN", c, c + 512))
         ts(B("A16", c, c + 512), B("G16", c, c + 512), 0.5, A_.mult, 1023.8, A_.add)
-    for s in (0, 1):
+
+    def maps(s, banks, after):
         for c in (0, 1):
-            c0, c1, ev, od = 512 * c, 512 * c + 512, B(("psS", "psE")[c]), B(("psP", "psK1")[c])
-            mm(ev, B("R%d" % s), B("G16", c0, c1), True, True)
-            mms(od, [(B("R%d" % s), B("A16", c0, c1)), (B("RM%d" % s), B("G16", c0, c1))])
-            act(B("PT%d" % s, 2 * c0, 2 * c1, 2), ev, 1.0, 0.0)
-            if s == 0:
-                ts(B("PT%d" % s, 2 * c0 + 1, 2 * c1, 2), od, 4.0, A_.mult, -4095.0, A_.add)
-            else:
-                act(B("PT%d" % s, 2 * c0 + 1, 2 * c1, 2), od, 4.0, -4095.0)
+            c0, c1, ev, od = 512 * c, 512 * c + 512, B(banks[2 * c]), B(banks[2 * c + 1])
+            mm(ev, B("R%d" % s), B("G16", c0, c1), True, True, after)
+            mm(od, B("RM%d" % s), B("G16", c0, c1), True, False, after)
+            mm(od, B("R%d" % s), B("A16", c0, c1), False, True)
+            for x, (i, a, b) in enumerate(((ev, 1.0, 0.0), (od, 4.0, -4095.0))):
+                o = B("PT%d" % s, 2 * c0 + x, 2 * c1, 2)
+                if P["pt"][4 * s + 2 * c + x] == "v":
+                    ts(o, i, a, A_.mult, b, A_.add)
+                else:
+                    act(o, i, a, b)
+    maps(0, ("psS", "psP", "psD1", "psK1"), ())
 
     src, hand, dst = _route(rank, T, topo)
     to = hand if hand is not None else dst
@@ -356,23 +367,25 @@ def rank_program(g, core, T, topo):
         gat("v", B("XV"), val, B("LL"))
         tt(B("LE"), B("XV", 0, 32), B("XV", 32, 64), A_.is_lt)
         mm(B("psR", 0, 64), IDN, B("ZC"), True, False)
-        for x in range(8):
-            c, h = 16 * (x // 2), x % 2
-            mm(B("psR", c, c + 16), move(("BN", "BP")[x // 4], x // 2 % 2, h), B("LE", 16 * h, 16 * h + 16), False, x == 7)
+        mm(B("psR", 0, 32), B("BN"), B("LE"), False, False)
+        mm(B("psR", 32, 64), B("BP"), B("LE"), False, True)
         tt(B("CD"), B(I, 0, 64), B("psR", 0, 64), A_.min)
         tt(B(O, 32, 64), B("CD", 0, 32), B("CD", 32, 64), A_.max)
         for l in (0, 1):
-            mms(B("psR", l, 32, 2), [(move("IW", l, h), B(O, 32 + 16 * h, 48 + 16 * h)) for h in (0, 1)])
+            mms(B("psR", l, 32, 2), [(move(l, h), B(O, 32 + 16 * h, 48 + 16 * h)) for h in (0, 1)])
         vcopy(B("CU"), B("psR", 0, 32))
         mm(B("psR", 0, 32), IDN, B(I, 32, 64), True, True)
         act(B(IMT, 512, 544), B("psR", 0, 32), 1.0, 0.0)
         p0 = 0
         for w in P["ic"]:
             c0, c1 = 32 * p0, 32 * (p0 + w)
-            gat(P["img"], B("IMG", c0, c1), B("PT%d" % s), B("CU", 2 * p0, 2 * (p0 + w)))
-            turn(B(IMT, c0, c1), B("IMG", c0, c1))
-            vcopy(B(LI, c0, c1), B(IMT, c0, c1))
+            a, b = ("IH", "IT") if P["i16"] else ("IMG", IMT)
+            gat(P["img"], B(a, c0, c1), B("PT%d" % s), B("CU", 2 * p0, 2 * (p0 + w)))
+            turn(B(b, c0, c1), B(a, c0, c1))
+            vcopy(B(LI, c0, c1), B(b, c0, c1))
             p0 += w
+        if P["i16"]:
+            asel(B(IMT, 0, 512), B("IT"), [[0, 512]], A_.is_equal, 0, 0)
 
         K = B("psK%d" % s, 0, 32)
         mm(K, IDN, B("IDX"), True, False)
@@ -381,45 +394,46 @@ def rank_program(g, core, T, topo):
             c0, c1, d = 512 * p0, 512 * p1, B("psD%d" % (c & 1), 0, 32 * (p1 - p0))
             x = gat("v" if (n, c) in P["vg"] or c in P["vg"] else "s", B(W, c0, c1), val, B(LI, 32 * p0, 32 * p1), after=before)
             before = before if x is None else [x]
-            scan(B("SB", c0 + 1, c1 + 1), B(W, c0, c1), B("MSK", 0, c1 - c0), 0.0, A_.max, A_.mult)
-            scan(B("YB", c0, c1), B(W, c0, c1), B("SB", c0, c1), 0.0, A_.max, A_.min)
+            if n == c == 0:
+                maps(1, ("psS", "psP", "psE", "psK1"), before)
+            for x in range(c0, c1, P["sc"]):
+                y = min(x + P["sc"], c1)
+                scan(B("SB", x + 1, y + 1), B(W, x, y), B("MSK", 0, y - x), 0.0, A_.max, A_.mult)
+                scan(B("YB", x, y), B(W, x, y), B("SB", x, y), 0.0, A_.max, A_.min)
             mms(d, [(IDN, B("SB", c0 + 16, c1 + 1, 16)), (IDN, B("YB", c0 + 15, c1, 16))])
             if c < P["sunit"]:
                 act(B(U, 32 * p0, 32 * p1), d, -1000.0, -1000.0 * (MT[t] + 0.5), F.Sigmoid)
             else:
                 ts(B(U, 32 * p0, 32 * p1), d, -float(MT[t]), A_.is_lt)
             for p in range(p0, p1):
-                mm(K, sel(p), B(U, 32 * p, 32 * p + 32), False, p == 15)
+                mm(K, B("SEL", 15 - p, 143 - p), B(U, 32 * p, 32 * p + 32), False, p == 15)
 
         M2 = 32768.0 * MAGIC
         scan(B("K1"), B("THK%d" % s), K, -BIG, A_.max, A_.min)
         ts(B("RR"), B("K1", 15, 32, 16), M2, A_.add, M2, A_.subtract)
         for q in (0, 1):
-            ts(B("LW", q, 32, 2), B("B64", 0, 16), col("K1", 16 * q + 15), A_.add, col("RR", q), A_.subtract)
-        ts(B("LU"), B("LW"), 1.0 / 16, A_.mult, -0.47, A_.add)
+            ts(B("LW", 16 * q, 16 * q + 16), B("B64", 0, 16), col("K1", 16 * q + 15), A_.add, col("RR", q), A_.subtract)
+        ts(B("LU"), B("LW", 0, 32, 16), 1.0 / 16, A_.mult)
 
-        gat("v", B(O, 0, 32), B(IMT), B("LU", 0, 2))
-        mm(B("psS", 32, 64), IDN, B(O, 0, 32), True, True)
+        ts(B("UC"), B(U), 32768.0, A_.mult, off=B("LU"))
+        vput(B("ZU"), B("LZ"), B("UC"))
+        gat("v", B(O, 0, 32), B(IMT), B("LU"))
+        for h in (0, 1):
+            mms(B("psP", 16 * h, 16 * h + 16), [(move(h, q), B(O, 16 * q, 16 * q + 16)) for q in (0, 1)])
+        turn(B("NCT"), B("psP", 0, 32))
         mm(B("psS", 0, 32), IDN, B("KC"), True, False)
-        for x in (0, 1):
-            c0, c1 = 256 * x, 256 * x + 256
-            gat(P["ux"], B("UX", c0, c1), B(U), B("LU", 16 * x, 16 * x + 16), scale=-1.0)
-            if P["prs"]:
-                gat("s", B("WS", c0, c1), B(W), B("LW", 16 * x, 16 * x + 16))
-                scan(B("PR", c0, c1), B("WS", c0, c1), B("UX", c0, c1), 0.0, A_.max, A_.mult)
-            else:
-                ttg(B("PR", c0, c1), B(W), B("LW", 16 * x, 16 * x + 16), B("UX", c0, c1), A_.mult)
-            for k in range(8 * x, 8 * x + 8):
-                mm(B("psS", 0, 32), sel(k), B("PR", 32 * k, 32 * k + 32), False, k == 15)
-        turn(B("KT"), B("psS", 0, 64))
-        scan(B("K2"), B("TH2"), B("KT", 0, 32), BIG, A_.min, A_.max)
-        for h in (0, 1):
-            ts(B("XD", 16 * h, 16 * h + 16), B("KT", 16 * h, 16 * h + 16), col("K2", 16 * h + 15), A_.subtract)
+        for q in (0, 1):
+            gat(P["ws"][q], B("WS", 256 * q, 256 * q + 256), B(W), B("LW", 16 * q, 16 * q + 16))
+            for y in range(16 * q, 16 * q + 16):
+                mm(B("psS", 16 * q, 16 * q + 16), B("ZU", 128 * y, 128 * y + 128), B("WS", 240 * q + y, 256 * q + 256, 16), False, y == 31)
+        scan(B("K2"), B("TH2"), B("psS", 0, 32), BIG, A_.min, A_.max)
+        for q in (0, 1):
+            ts(B("XD", 16 * q, 16 * q + 16), B("psS", 16 * q, 16 * q + 16), col("K2", 16 * q + 15), A_.subtract)
         ts(B("AA"), B("K2", 15, 32, 16), 5000.0, A_.is_gt, -4096.0, A_.mult)
-        tt(B("XX", 1, 33), B("XD"), B("KT", 32, 64), A_.add)
+        tt(B("XX", 1, 33), B("XD"), B("NCT"), A_.add)
         tt(B("XX", 0, 34, 33), B(I, 64, 66), B("AA"), A_.add)
-        for h in (0, 1):
-            red(col(O, 64 + h), B("XX", 17 * h, 17 * h + 17), A_.max)
+        for q in (0, 1):
+            red(col(O, 64 + q), B("XX", 17 * q, 17 * q + 17), A_.max)
         pair_of(B(O, 64, 66), B(O, 66, 68), 2)
         if t < NR_ - 1:
             sent = op("g", lambda n=n: _send(g, T, topo, core, to, T["o%d" % n][:], "i%d" % (n + 2), "a%d" % (n + 2)), [B(O)[1]], [], 300.0,
@@ -428,12 +442,12 @@ def rank_program(g, core, T, topo):
 
         tt(B("EQ", 0, 130, 129), B("AA"), B("PC", 5, 7), A_.add)
         tt(B("PK"), B("PR2", 0, 2), B("EQ", 0, 130, 129), A_.max)
-        for h in (0, 1):
-            ts(B("XH", 32 * h, 32 * h + 32), B("OH"), col("PK", h), A_.mult)
-        for h in (0, 1):
-            mms(B("psP", 64 * h, 64 * h + 64), [(IDN, B("FAR", 64 * h, 64 * h + 64)), (B("B32"), B("XH"))])
-        for h in (0, 1):
-            ts(B("EQ", 64 * h + 1, 64 * h + 65), B("psP", 64 * h, 64 * h + 64), col("PK", h), A_.is_equal, col("PC", 5 + h), A_.mult)
+        for q in (0, 1):
+            ts(B("XH", 32 * q, 32 * q + 32), B("OH"), col("PK", q), A_.mult)
+        for q in (0, 1):
+            mms(B("psP", 64 * q, 64 * q + 64), [(IDN, B("FAR", 64 * q, 64 * q + 64)), (B("B32"), B("XH"))])
+        for q in (0, 1):
+            ts(B("EQ", 64 * q + 1, 64 * q + 65), B("psP", 64 * q, 64 * q + 64), col("PK", q), A_.is_equal, col("PC", 5 + q), A_.mult)
         scan(B("DV", 0, 130), B("MK2"), B("EQ"), 0.0, A_.mult, A_.max)
         ts(B("DV", 194, 260, 65), B("DV", 64, 130, 65), 1.0625, A_.mult)
         tt(B("EE"), B(O, 64, 68), B("DV", 64, 260, 65), A_.max)
@@ -442,14 +456,14 @@ def rank_program(g, core, T, topo):
         vcopy(B("EL"), B("psE", 0, 8))
         ts(B("ZE", 0, 64), val, 32.0, A_.add, 255.0, A_.min, B("EL", 0, 4))
         if P["down"] == "s" and n < 9:
-            gat("s", B("ZE", 64, 128), val, B("EL", 4, 8), F.Relu, 1.0, -32.0)
+            gat("s", B("ZE", 64, 128), val, B("EL", 4, 8), F.Relu, -32.0)
         else:
             ts(B("ZE", 64, 128), val, -32.0, A_.add, 0.0, A_.max, B("EL", 4, 8))
         vput(val, B("EL"), B("ZE"))
 
         if t < NR_ - 1:
             c = col("psE", 0)
-            mms(c, [(B("B32"), col("AA", h)) for h in (0, 1)])
+            mms(c, [(B("B32"), col("AA", q)) for q in (0, 1)])
             if P["par"] == "s":
                 act(col("TB", 0), c, -0.49994 / 4096, MAGIC)
                 act(col("TB", 1), col("TB", 0), 65536.0, -65536.0 * MAGIC)
@@ -472,9 +486,8 @@ def rank_program(g, core, T, topo):
     vput(B("YCD"), B("LC"), B("GU"))
     dmas("y", [(T.yc[:], T.YCD[:, 0:64])], [B("YCD")[1]], [], "stc")
     dmas("s", [(T.yd[:], T.YCD[:, 64:128])], [B("YCD")[1]], [], "std")
-    for q in (0, 1):
-        mms(B("psR", 2 * q, 2 * q + 2), [(move("IW", q, s), B("o%d" % (8 + s), 64, 66)) for s in (0, 1)])
-    for q in (0, 1):
-        vcopy(B("YL", q, 4, 2), B("psR", 2 * q, 2 * q + 2))
+    for h in (0, 1):
+        mms(B("psR", 2 * h, 2 * h + 2), [(move(h, s), B("o%d" % (8 + s), 64, 66)) for s in (0, 1)])
+    vcopy(B("YL"), B("psR", 0, 4))
     dmas("y", [(T.yl[:], T.YL[:])], [B("YL")[1]], [], "stl")
     issue()

@@ -4,24 +4,33 @@ A_ = AluOpType
 F = ActivationFunctionType
 X_ = AxisListType.X
 NR_ = 5
-PAR = dict(ch=(2, 2, 2, 2, 2, 2, 2, 1, 1), sunit=0, img="s", ws="vv", pt="ssssvvvv", pe=60, par="s", down="s", ic=(4, 12), vg=(), sc=512, i16=0,
-           cyc=1.0, gat=1.5, put=3.5, fix=10, wake=100, hop=4500, dma=4000, slack=30)
+PAR = dict(ch=(2, 2, 2, 2, 2, 2, 2, 1, 1), sunit=0, img="ss", vd=0, ws="vvss", pt="ssssvvvv", pe=60, down="v", ic=(4, 12), vg=(), sc=512, sl=256, i16=1,
+           xh="v", up="v", gli=4, gll=1, aa="v",
+           cyc=1.0, gat=1.5, put=3.5, fix=0, wake=100, xw=100, hop=4800, dma=4000, slack=30, it=1, gc=(4, 4, 4, 4, 4, 4, 4, 2, 2))
 VW = 2320
 BIG = 1.0e9
 MAGIC = 12582912.0
 
 SCRATCH = {}
-for _d, _names in (("int32", "GEN 1024 XCD 128 XL 4 PI 4 LC0 8 LZ0 2 TI 2 PR2 4"),
-                   ("float32", "PT0 2048 PT1 2048 IMG 512 IMT0 544 IMT1 544 PC 16 B64 64 IX0 32 KB 12 THK0 32 THK1 32 TH2 32 K1 32 RR 2 "
-                               "NCT 32 LN 64 K2 32 XD 32 XX 34 U4 4 PK 2 TB 4 GT 128 GU 128 YCD 128 YL 4"),
-                   ("bfloat16", "VAL0 %d VAL1 %d W0 8704 W1 8704 SB 8208 YB 8192 U0 544 U1 544 UC 32 WS 512 ZU 4096 MSK 2048 ONE 160 NEG 144 B1 128 "
-                                "BW 128 BP 128 BN 128 IW 160 IW0 160 IW1 160 SL1 144 SL2 144 SEL 144 R0 128 R1 128 RM0 128 RM1 128 "
-                                "B2 128 B32 128 OH 32 KC 32 FAR 128 XV 64 LE 32 ZE 128 ZC 64 MK2 130" % (VW, VW)),
-                   ("float16", "G16 1024 A16 1024 FX 128 FT 128 ML 8 IDX 32 AA 2 XH 64 EE 4 EQ 130 DV 260 CD 64 IH 512 IT 512"),
-                   ("uint16", "LC 8 LL 4 CU 32 LI0 512 LI1 512 LW 32 LU 2 LZ 2 EL 8")):
-    _w = _names.split()
+_POS = {}
+for _d, _names, _packed in (
+        ("int32", "GEN 1024 XCD 128 XL 4 TI 8", "PI 6 LC0 8 LZ0 2"),
+        ("float32", "PT0 2048 PT1 2048 IMG 512 IMT0 544 IMT1 544 THK0 64 THK1 64 K1 64 NCT 64 K2 64 XD 64 XX 66 U4 4 PK 2 EQ 130 TB 4 "
+                    "GT 128 GU 128 YCD 128 YL 4", "PC 16 B64 64 IX0 32 KB 20 TH2 64 LN 64 KE 64 KF 64"),
+        ("bfloat16", "VAL0 %d VAL1 %d W0 8704 W1 8704 SB 8208 YB 8192 U0 544 U1 544 UC 32 WS 512 ZU 2048 AA 2 DF 64 ZF 64 XV 64 LE 32 ZE 128" % (VW, VW),
+         "MSK 1024 ONE 160 NEG 144 B1 128 BW 128 BP 128 BN 128 IW 160 IW0 160 IW1 160 SL1 144 SL2 144 SEL 144 R0 128 R1 128 RM0 128 RM1 128 "
+         "RN0 128 RN1 128 RP0 128 RP1 128 TW0 128 TW1 128 B2 128 B32 128 OH 32 KC0 64 KC 64 FAR 128 ZC 64 MK2 130"),
+        ("float16", "G16 1024 A16 1024 FX 128 FT 128 ML 8 IDX 64 PR2 4 XH 64 DV 130 CD 64 IH 512 IT 512", ""),
+        ("uint16", "LC 8 LL 4 CU 32 LI0 512 LI1 512 LW 32 LU 2 LZ 2 EL 8", "")):
+    _w, _c = _names.split(), 0
     for _i in range(0, len(_w), 2):
         SCRATCH[_w[_i]] = ("sbuf", [128, int(_w[_i + 1])], _d)
+    _w = _packed.split()
+    for _i in range(0, len(_w), 2):
+        _POS[_w[_i]] = ("pk" + _d, _c, int(_w[_i + 1]))
+        _c += (int(_w[_i + 1]) + 31) // 32 * 32
+    if _c:
+        SCRATCH["pk" + _d] = ("sbuf", [128, _c], _d)
 for _n in "psD0 psD1 psK0 psK1 psS psR psP psE".split():
     SCRATCH[_n] = ("psum", [128, 512], "float32")
 SEMAPHORES = "vc sc tc gc ls ldg0 ldg1 ldc ldl ldv0 ldv1 stv0 stv1 stw1 stc std stl".split()
@@ -29,7 +38,8 @@ for _n in range(2 * NR_):
     SCRATCH["i%d" % _n] = ("sbuf", [128, 68], "float16")
     SCRATCH["o%d" % _n] = ("sbuf", [128, 68], "float16")
     if _n > 1:
-        SEMAPHORES.append("a%d" % _n)
+        SEMAPHORES += ["d%d" % _n, "a%d" % _n]
+PART = {"d": (0, 32), "a": (32, 68)}
 
 
 def _route(r, T, topo):
@@ -42,14 +52,14 @@ def _route(r, T, topo):
 
 
 def _mask(src, dst, topo):
-    e = topo.engines(src, dst)[:8]
-    return sum(1 << x for x in e), len(e)
+    return topo.mask(src, dst), len(topo.engines(src, dst))
 
 
-def _send(g, T, topo, core, dst, src_ap, name, sem):
+def _send(g, T, topo, core, dst, src, part, n):
     rid, pid = topo.addr(dst, core)
     m, k = _mask(core, dst, topo)
-    g.remote_dma(T[name][:], src_ap, T.sem[sem], T.sem["ls"], pid, rid, m)
+    c0, c1 = PART[part]
+    g.remote_dma(T["i%d" % n][:, c0:c1], T[src][:, c0:c1], T.sem["%s%d" % (part, n)], T.sem["ls"], pid, rid, m)
     return k
 
 
@@ -59,9 +69,11 @@ def _relay(g, core, T, topo):
         if h != core:
             continue
         tot = 0
-        for n in range(2, 2 * NR_):
-            g.wait_ge(T.sem["a%d" % n], _mask(s, h, topo)[1])
-            tot += _send(g, T, topo, core, d, T["i%d" % n][:], "i%d" % n, "a%d" % n)
+        for n in range(2, 2 * NR_ + 1):
+            for part, x in (("d", n), ("a", n - 1)):
+                if 2 <= x < 2 * NR_:
+                    g.wait_ge(T.sem["%s%d" % (part, x)], _mask(s, h, topo)[1])
+                    tot += _send(g, T, topo, core, d, "i%d" % x, part, x)
         g.wait_ge(T.sem["ls"], tot)
 
 
@@ -82,39 +94,42 @@ def _order(calls):
     if len(calls) in _DONE:
         return _DONE[len(calls)]
     P = PAR
-    users = [[] for c in calls]
+    deps, users = [c["deps"] for c in calls], [[] for c in calls]
     for i, c in enumerate(calls):
         for d in c["deps"]:
             users[d].append(i)
 
     def gap(i, u):
+        i, u = min(i, u), max(i, u)
         same = calls[i]["q"] == calls[u]["q"] and (calls[i]["q"] == "t" or i in calls[u]["free"])
-        return 0.0 if same else calls[i]["late"] + P["wake"]
+        return 0.0 if same else calls[i]["late"] + P["wake" if calls[i]["q"] == calls[u]["q"] else "xw"]
+
+    def run(pre, post, way):
+        left, at, end = [len(x) for x in pre], [0.0] * len(calls), [0.0] * len(calls)
+        ready = {c["q"]: [] for c in calls}
+        for i, c in enumerate(calls):
+            if not left[i]:
+                ready[c["q"]].append(i)
+        free, out = {q: 0.0 for q in ready}, []
+        while len(out) < len(calls):
+            now, q = min((max(free[q], min(at[i] for i in ready[q])), q) for q in ready if ready[q])
+            i = max((i for i in ready[q] if at[i] <= now + P["slack"]), key=lambda i: (way[i], -i))
+            ready[q].remove(i)
+            out.append(i)
+            end[i] = free[q] = max(now, at[i]) + calls[i]["busy"]
+            for u in post[i]:
+                at[u] = max(at[u], free[q] + gap(i, u))
+                left[u] -= 1
+                if not left[u]:
+                    ready[calls[u]["q"]].append(u)
+        return out, end
     way = [0.0] * len(calls)
     for i in reversed(range(len(calls))):
         way[i] = calls[i]["busy"] + max([way[u] + gap(i, u) for u in users[i]], default=calls[i]["late"])
-    left = [len(c["deps"]) for c in calls]
-    at = [0.0] * len(calls)
-    ready = {}
-    for i, c in enumerate(calls):
-        ready.setdefault(c["q"], [])
-        if not left[i]:
-            ready[c["q"]].append(i)
-    free = {q: 0.0 for q in ready}
-    out = []
-    while len(out) < len(calls):
-        now, q = min((max(free[q], min(at[i] for i in ready[q])), q) for q in ready if ready[q])
-        i = max((i for i in ready[q] if at[i] <= now + P["slack"]), key=lambda i: (way[i], -i))
-        ready[q].remove(i)
-        out.append(i)
-        free[q] = max(now, at[i]) + calls[i]["busy"]
-        for u in users[i]:
-            at[u] = max(at[u], free[q] + gap(i, u))
-            left[u] -= 1
-            if not left[u]:
-                ready[calls[u]["q"]].append(u)
-    _DONE[len(calls)] = out
-    return out
+    for x in range(P["it"]):
+        way = run(users, deps, run(deps, users, way)[1])[1]
+    _DONE[len(calls)] = run(deps, users, way)[0]
+    return _DONE[len(calls)]
 
 
 def rank_program(g, core, T, topo):
@@ -179,7 +194,8 @@ def rank_program(g, core, T, topo):
         return op(q, fn, reads, writes, 60.0 * len(pairs), late or P["dma"], (sem, 16 * len(pairs)), after)
 
     def B(name, c0=0, c1=None, st=1):
-        c1 = SCRATCH[name][1][1] if c1 is None else c1
+        name, off, w = _POS[name] if name in _POS else (name, 0, SCRATCH[name][1][1])
+        c0, c1 = off + c0, off + (w if c1 is None else c1)
         ap = T[name][:, c0:c1] if st == 1 else T[name][:, c0:c1:st]
         r = range(c0, c1, st)
         return ap, (name, range(512) if name[:2] == "ps" else r), len(r), 2 if "16" in SCRATCH[name][2] else 4
@@ -196,21 +212,22 @@ def rank_program(g, core, T, topo):
     def vcopy(o, i):
         op("v", lambda: V.tensor_copy(o[0], i[0]), [i[1]], [o[1]], cost(o, i))
 
-    def gat(q, o, win, off, f=F.Copy, bias=0.0, after=()):
+    def gat(q, o, win, off, f=F.Copy, bias=0.0, after=(), scale=1.0):
         if q == "s":
-            return op("s", lambda: S.activation(o[0], win[0].indirect(off[0]), f, bias=bias), [win[1], off[1]], [o[1]], picked(o[2]), after=after)
+            return op("s", lambda: S.activation(o[0], win[0].indirect(off[0]), f, bias=bias, scale=scale), [win[1], off[1]], [o[1]],
+                      picked(o[2]), after=after)
         op("v", lambda: V.tensor_copy(o[0], win[0].indirect(off[0])), [win[1], off[1]], [o[1]], picked(o[2]))
 
     def vput(win, off, i):
         op("v", lambda: V.tensor_copy(win[0].indirect(off[0]), i[0]), [off[1], i[1]], [win[1]], picked(i[2], "put"))
 
     def act(o, i, scale, bias, f=F.Copy):
-        c = isinstance(bias, tuple)
-        op("s", lambda: S.activation(o[0], i[0], f, bias=bias[0] if c else bias, scale=scale), [i[1]] + ([bias[1]] if c else []), [o[1]],
+        b, c = [x[0] if isinstance(x, tuple) else x for x in (bias, scale)]
+        op("s", lambda: S.activation(o[0], i[0], f, bias=b, scale=c), [x[1] for x in (i, bias, scale) if isinstance(x, tuple)], [o[1]],
            P["fix"] + P["cyc"] * max(64, o[2]))
 
     def tt(o, a, b, f):
-        op("v", lambda: V.tensor_tensor(o[0], a[0], b[0], f), [a[1], b[1]], [o[1]], P["fix"] + P["cyc"] * max(64, 2 * o[2]))
+        op("v", lambda: V.tensor_tensor(o[0], a[0], b[0], f), [a[1], b[1]], [o[1]], P["fix"] + P["cyc"] * max(64, o[2] * (1 if "ps" in (a[1][0][:2], b[1][0][:2]) else 2)))
 
     def ts(o, a, s1, f1, s2=None, f2=None, off=None):
         rd = [a[1]] + [s[1] for s in (s1, s2, off) if isinstance(s, tuple)]
@@ -245,6 +262,9 @@ def rank_program(g, core, T, topo):
     def asel(o, i, pat, f, base, ch):
         op("g", lambda: g.affine_select(o[0], i[0], pat, f, 0.0, base, ch), [i[1]], [o[1]], 200 + 2 * P["cyc"] * o[2])
 
+    def gcopy(o, i):
+        asel(o, i, [[0, o[2]]], A_.is_equal, 0, 0)
+
     def move(h, l):
         c = 16 + 16 * (h - l)
         return B("IW%d" % h, c, c + 128)
@@ -254,7 +274,7 @@ def rank_program(g, core, T, topo):
     x = [dmas("s", [(T.GEN[:, 0:512], T.gen[:, 0:512])], [], [B("GEN", 0, 512)[1]], "ldg0", P["dma"] - 800)]
     dmas("s", [(T.GEN[:, 512:1024], T.gen[:, 512:1024])], [], [B("GEN", 512, 1024)[1]], "ldg1", P["dma"] - 400, x)
     x = [dmas("y", [(T.XL[:], T.lit[:])], [], [B("XL")[1]], "ldl", P["dma"] - 800)]
-    x = [dmas("y", [(T.XCD[:, 0:64], T.cla[:]), (T.XCD[:, 64:128], T.par[:])], [], [B("XCD")[1]], "ldc", P["dma"] - 400, x)]
+    x = [dmas("y", [(T.XCD[:, 0:64], T.par[:]), (T.XCD[:, 64:128], T.cla[:])], [], [B("XCD")[1]], "ldc", P["dma"] - 400, x)]
     for s in (0, 1):
         x = [dmas("y", [(T["VAL%d" % s][16 * x:16 * x + 16, 0:2048], T.val[32 * (x // 2) + 16 * s:32 * (x // 2) + 16 * s + 16, :]) for x in range(8)],
                   [], [B("VAL%d" % s, 0, 2048)[1]], "ldv%d" % s, P["dma"] + 1000 + 2000 * s, x)]
@@ -266,34 +286,42 @@ def rank_program(g, core, T, topo):
     asel(B("B1"), B("ONE", 0, 128), [[-16, 8], [0, 16]], A_.is_ge, 0, 1)
     asel(B("BW"), B("B1"), [[16, 8], [0, 16]], A_.is_ge, 15, -1)
     ms(B("NEG"), -32768.0)
-    for c, m in ((1, 15), (2, 16), (3, 31)):
+    for c, m in ((1, 15), (2, 16), (3, 31), (4, 7), (5, 8)):
         ts(col("PI", c), col("PI", 0), m, A_.bitwise_and)
     vcopy(B("PC", 11, 13), B("PI", 2, 4))
+    vcopy(col("PC", 13), col("PI", 5))
     for h in (0, 1):
         ts(col("PC", 1 + h), col("PI", 2), 16.0 * h, A_.is_equal)
         ts(col("PC", 3 + h), col("PI", 3), col("PC", 11), A_.add, 16.0 * h, A_.add)
     ts(B("PC", 5, 7), B("PC", 3, 5), 2.0, A_.mult, 2048.0, A_.add)
-    for c, m in ((7, 4.0), (8, 512.0), (9, 16.0), (10, 128.0)):
+    for c, m in ((7, 4.0), (8, 512.0), (9, 16.0)):
         ts(col("PC", c), col("PI", 1), m, A_.mult)
     ts(B("LC"), B("LC0"), col("PC", 7), A_.add)
     for h in (0, 1):
         ts(B("IW%d" % h), B("IW"), col("PC", 1 + h), A_.mult)
         tt(B("R%d" % h), move(h, 0), move(h, 1), A_.add)
-        ts(B("RM%d" % h), B("R%d" % h), -0.25, A_.mult)
+        for x, m in (("RM", -0.25), ("RN", -2.0), ("RP", 2.0)):
+            ts(B("%s%d" % (x, h)), B("R%d" % h), m, A_.mult)
         ts(B(("BP", "BN")[h]), B("BW"), 4096.0 * (1 - 2 * h), A_.mult)
-        ms(B("ZC", 32 * h, 32 * h + 32), 8.5 * 4096.0 * (1 - 2 * h))
+        ms(B("ZC", 32 * h, 32 * h + 32), 8.5 * 4096.0 * (2 * h - 1))
     iota(B("B64"), [[1, 64]], 0, 0)
     iota(B("IX0"), [[16, 32]], 0, 0)
     iota(B("LN"), [[16, 2], [32, 2], [1, 16]], 0, 0)
-    iota(B("KC"), [[0, 2], [-2048, 16]], 0, 0)
-    iota(B("LZ0"), [[2048, 2]], 0, 1, True)
+    iota(B("KC0"), [[0, 2], [-2048, 16], [0, 2]], -2048, 0)
+    iota(B("KE"), [[0, 32], [8, 2]], 0, 0)
+    ts(B("KF"), B("KE"), col("PC", 13), A_.not_equal, -2.0 ** 30, A_.mult)
+    tt(B("KC"), B("KC0"), B("KF"), A_.add)
+    iota(B("LZ0"), [[1024, 2]], 0, 1, True)
+    ts(col("PC", 10), col("PI", 4), 128.0, A_.mult)
     ts(B("LZ"), B("LZ0"), col("PC", 10), A_.add)
+    for h in (0, 1):
+        asel(B("TW%d" % h), B("ONE", 0, 128), [[-32, 4], [-1, 16], [0, 2]], A_.is_equal, -16 * h, 1)
     asel(B("SL1"), B("NEG"), [[-16, 9], [0, 16]], A_.is_ge, 0, 1)
     asel(B("SL2"), B("SL1"), [[16, 9], [0, 16]], A_.is_ge, 15, -1)
     asel(B("SEL"), B("SL2"), [[0, 9], [1, 16]], A_.is_equal, -15, 0)
     asel(B("B2"), B("ONE", 0, 128), [[-32, 4], [0, 32]], A_.is_ge, 0, 1)
     asel(B("B32"), B("B2"), [[32, 4], [0, 32]], A_.is_ge, 31, -1)
-    for c in range(0, 4096, 1024):
+    for c in range(0, 2048, 1024):
         iota(B("ZU", c, c + 1024), [[0, 1024]], 0, 0)
     for s in (0, 1):
         iota(B("W%d" % s, 8192, 8704), [[0, 512]], 0, 0)
@@ -302,25 +330,26 @@ def rank_program(g, core, T, topo):
     ms(B("MSK", 0, P["sc"]), 1.0)
     ms(B("MSK", 15, P["sc"], 16), -1.0)
     ms(B("SB", 0, 1), 0.0)
-    ms(B("TH2"), BIG)
-    ms(B("TH2", 0, 32, 16), 4096.0)
+    ms(B("TH2"), 1.0)
+    ms(B("TH2", 0, 64, 32), 0.0)
     ms(B("MK2"), 1.0)
     ms(B("MK2", 0, 130, 65), 0.0)
-    ts(B("IDX"), B("IX0"), col("PC", 8), A_.add)
-    ts(B("KB", 0, 2), B("IX0", 0, 32, 16), 8192.0, A_.add, col("PC", 9), A_.add)
+    ts(B("IDX", 0, 32), B("IX0"), 0.0, A_.mult)
+    ts(B("IDX", 32, 64), B("IX0"), col("PC", 8), A_.add)
+    ms(B("KB", 0, 2), 0.0)
+    ts(B("KB", 2, 4), B("IX0", 0, 32, 16), 8192.0, A_.add, col("PC", 9), A_.add)
     ts(B("OH"), B("B64", 0, 32), col("PC", 12), A_.is_equal)
     for s in (0, 1):
         ms(B("VAL%d" % s, 2048, VW), 0.0)
         ms(B("THK%d" % s), -BIG)
         ts(B("FAR", 64 * s, 64 * s + 64), B("LN"), col("PC", 3 + s), A_.is_ge, 4096.0, A_.mult)
-        ts(B("THK%d" % s, 0, 32, 16), B("KB", 0, 2), -32768.0 * AT[0], A_.add)
-    if P["par"] == "s":
-        for t in range(1, NR_):
-            act(B("KB", 2 * t, 2 * t + 2), B("KB", 0, 2), 1.0, -32768.0 * AT[t])
+        ts(B("THK%d" % s, 0, 64, 16), B("KB", 0, 4), -32768.0 * AT[0], A_.add)
+    for t in range(1, NR_):
+        act(B("KB", 4 * t, 4 * t + 4), B("KB", 0, 4), 1.0, -32768.0 * AT[t])
 
     def pair_of(l, lp, n):
-        ts(B("PR2", 0, n), l, 0.5, A_.mult, -0.25, A_.add)
-        ts(B("U4", 0, n), B("PR2", 0, n), 4.0, A_.mult, 1.0, A_.add)
+        ts(B("PR2", 0, n), l, 0.5, A_.mult, 1023.8, A_.add)
+        ts(B("U4", 0, n), B("PR2", 0, n), 4.0, A_.mult, -4095.0, A_.add)
         tt(lp, B("U4", 0, n), l, A_.subtract)
 
     gat("v", B("FX"), B("XCD"), B("LC"))
@@ -358,103 +387,122 @@ def rank_program(g, core, T, topo):
     arr = _mask(into[1] if into[1] is not None else into[0], core, topo)[1]
     edge = [sum(P["ch"][:c]) for c in range(len(P["ch"]) + 1)]
 
+    def send(part, n):
+        if n + 2 < 2 * NR_:
+            x = op("g", lambda: _send(g, T, topo, core, to, "o%d" % n, part, n + 2), [B("o%d" % n, *PART[part])[1]], [], 300.0,
+                   ev=("ls", 4 * (NR_ - 1) * _mask(core, to, topo)[1]))
+            op(part + str(n), None, [], [B("i%d" % (n + 2), *PART[part])[1]], 0.0, P["hop"], ("%s%d" % (part, n + 2), arr), [x])
+
     before = []
     for n in range(2 * NR_):
         s, t, I, O = n % 2, n // 2, "i%d" % n, "o%d" % n
         val, W, U, IMT, LI = B("VAL%d" % s), "W%d" % s, "U%d" % s, "IMT%d" % s, "LI%d" % s
 
-        vcopy(B("LL"), B(I, 64, 68))
+        (gcopy if P["gll"] else vcopy)(B("LL"), B(I, 64, 68))
         gat("v", B("XV"), val, B("LL"))
         tt(B("LE"), B("XV", 0, 32), B("XV", 32, 64), A_.is_lt)
         mm(B("psR", 0, 64), IDN, B("ZC"), True, False)
-        mm(B("psR", 0, 32), B("BN"), B("LE"), False, False)
-        mm(B("psR", 32, 64), B("BP"), B("LE"), False, True)
+        mm(B("psR", 0, 32), B("BP"), B("LE"), False, False)
+        mm(B("psR", 32, 64), B("BN"), B("LE"), False, True)
         tt(B("CD"), B(I, 0, 64), B("psR", 0, 64), A_.min)
-        tt(B(O, 32, 64), B("CD", 0, 32), B("CD", 32, 64), A_.max)
+        tt(B(O, 0, 32), B("CD", 0, 32), B("CD", 32, 64), A_.max)
+        send("d", n)
         for l in (0, 1):
-            mms(B("psR", l, 32, 2), [(move(l, h), B(O, 32 + 16 * h, 48 + 16 * h)) for h in (0, 1)])
+            mms(B("psR", l, 32, 2), [(move(l, h), B(O, 16 * h, 16 * h + 16)) for h in (0, 1)])
         vcopy(B("CU"), B("psR", 0, 32))
-        mm(B("psR", 0, 32), IDN, B(I, 32, 64), True, True)
-        act(B(IMT, 512, 544), B("psR", 0, 32), 1.0, 0.0)
+        asel(B(IMT, 512, 544), B(I, 0, 32), [[0, 32]], A_.is_equal, 0, 0)
         p0 = 0
         for w in P["ic"]:
             c0, c1 = 32 * p0, 32 * (p0 + w)
             a, b = ("IH", "IT") if P["i16"] else ("IMG", IMT)
-            gat(P["img"], B(a, c0, c1), B("PT%d" % s), B("CU", 2 * p0, 2 * (p0 + w)))
+            gat(P["img"][p0 > 0], B(a, c0, c1), B("PT%d" % s), B("CU", 2 * p0, 2 * (p0 + w)))
             turn(B(b, c0, c1), B(a, c0, c1))
-            vcopy(B(LI, c0, c1), B(b, c0, c1))
+            (gcopy if p0 >= P["gli"] else vcopy)(B(LI, c0, c1), B(b, c0, c1))
             p0 += w
         if P["i16"]:
             asel(B(IMT, 0, 512), B("IT"), [[0, 512]], A_.is_equal, 0, 0)
 
-        K = B("psK%d" % s, 0, 32)
+        K = B("psK%d" % s, 0, 64)
         mm(K, IDN, B("IDX"), True, False)
-        for c in range(len(P["ch"])):
-            p0, p1 = edge[c], edge[c + 1]
-            c0, c1, d = 512 * p0, 512 * p1, B("psD%d" % (c & 1), 0, 32 * (p1 - p0))
-            x = gat("v" if (n, c) in P["vg"] or c in P["vg"] else "s", B(W, c0, c1), val, B(LI, 32 * p0, 32 * p1), after=before)
+        p0 = 0
+        for c, w in enumerate(P["gc"]):
+            x = gat("v" if (n, c) in P["vg"] or c in P["vg"] else "s", B(W, 256 * p0, 256 * (p0 + w)), val, B(LI, 16 * p0, 16 * (p0 + w)), after=before)
             before = before if x is None else [x]
             if n == c == 0:
                 maps(1, ("psS", "psP", "psE", "psK1"), before)
-            for x in range(c0, c1, P["sc"]):
-                y = min(x + P["sc"], c1)
-                scan(B("SB", x + 1, y + 1), B(W, x, y), B("MSK", 0, y - x), 0.0, A_.max, A_.mult)
+            p0 += w
+        for c in range(len(P["ch"])):
+            p0, p1 = edge[c], edge[c + 1]
+            c0, c1, d = 512 * p0, 512 * p1, B("psD%d" % (c & 1), 0, 32 * (p1 - p0))
+            w = P["sl"] if p1 == 16 else min(P["sc"], c1 - c0)
+            for x in range(c0, c1, w):
+                y = x + w
+                scan(B("SB", x + 1, y + 1), B(W, x, y), B("MSK", 0, w), 0.0, A_.max, A_.mult)
                 scan(B("YB", x, y), B(W, x, y), B("SB", x, y), 0.0, A_.max, A_.min)
-            mms(d, [(IDN, B("SB", c0 + 16, c1 + 1, 16)), (IDN, B("YB", c0 + 15, c1, 16))])
+            if c < len(P["ch"]) - P["vd"]:
+                mms(d, [(IDN, B("SB", c0 + 16, c1 + 1, 16)), (IDN, B("YB", c0 + 15, c1, 16))])
+            else:
+                d = B("DF", 0, 32 * (p1 - p0))
+                tt(d, B("SB", c0 + 16, c1 + 1, 16), B("YB", c0 + 15, c1, 16), A_.add)
             if c < P["sunit"]:
                 act(B(U, 32 * p0, 32 * p1), d, -1000.0, -1000.0 * (MT[t] + 0.5), F.Sigmoid)
             else:
                 ts(B(U, 32 * p0, 32 * p1), d, -float(MT[t]), A_.is_lt)
             for p in range(p0, p1):
-                mm(K, B("SEL", 15 - p, 143 - p), B(U, 32 * p, 32 * p + 32), False, p == 15)
+                for x in (0, 32):
+                    mm(B("psK%d" % s, x, x + 32), B("SEL", 15 - p, 143 - p), B(U, 32 * p, 32 * p + 32), False, p == 15 and x == 32)
 
-        M2 = 32768.0 * MAGIC
         scan(B("K1"), B("THK%d" % s), K, -BIG, A_.max, A_.min)
-        ts(B("RR"), B("K1", 15, 32, 16), M2, A_.add, M2, A_.subtract)
         for q in (0, 1):
-            ts(B("LW", 16 * q, 16 * q + 16), B("B64", 0, 16), col("K1", 16 * q + 15), A_.add, col("RR", q), A_.subtract)
-        ts(B("LU"), B("LW", 0, 32, 16), 1.0 / 16, A_.mult)
+            ts(col("LU", q), col("K1", 16 * q + 47), col("K1", 16 * q + 15), A_.subtract, 1.0 / 16, A_.mult)
+        for q in (0, 1):
+            ts(B("LW", 16 * q, 16 * q + 16), B("B64", 0, 16), col("K1", 16 * q + 47), A_.add, col("K1", 16 * q + 15), A_.subtract)
 
         ts(B("UC"), B(U), 32768.0, A_.mult, off=B("LU"))
         vput(B("ZU"), B("LZ"), B("UC"))
-        gat("v", B(O, 0, 32), B(IMT), B("LU"))
-        for h in (0, 1):
-            mms(B("psP", 16 * h, 16 * h + 16), [(move(h, q), B(O, 16 * q, 16 * q + 16)) for q in (0, 1)])
-        turn(B("NCT"), B("psP", 0, 32))
-        mm(B("psS", 0, 32), IDN, B("KC"), True, False)
+        gat("v", B(O, 32, 64), B(IMT), B("LU"))
+        for x in range(4):
+            mm(B("psP", 16 * x, 16 * x + 16), B("TW%d" % (x % 2)), B(O, 32 + 16 * (x // 2), 48 + 16 * (x // 2)), True, True)
+        turn(B("psP", 64, 128), B("psP", 0, 64))
+        mm(B("psS", 0, 64), IDN, B("KC"), True, False)
         for q in (0, 1):
-            gat(P["ws"][q], B("WS", 256 * q, 256 * q + 256), B(W), B("LW", 16 * q, 16 * q + 16))
-            for y in range(16 * q, 16 * q + 16):
-                mm(B("psS", 16 * q, 16 * q + 16), B("ZU", 128 * y, 128 * y + 128), B("WS", 240 * q + y, 256 * q + 256, 16), False, y == 31)
-        scan(B("K2"), B("TH2"), B("psS", 0, 32), BIG, A_.min, A_.max)
+            gat(P["ws"][q + 2 * (n == 9)], B("WS", 256 * q, 256 * q + 256), B(W), B("LW", 16 * q, 16 * q + 16))
+            for y in range(8 * q, 8 * q + 8):
+                mm(B("psS", 32 * q, 32 * q + 32), B("ZU", 128 * y, 128 * y + 128), B("WS", 248 * q + y, 256 * q + 256, 8), False, y == 15)
+        scan(B("K2"), B("TH2"), B("psS", 0, 64), 0.0, A_.mult, A_.max)
+        top = B("K2", 31, 64, 32)
         for q in (0, 1):
-            ts(B("XD", 16 * q, 16 * q + 16), B("psS", 16 * q, 16 * q + 16), col("K2", 16 * q + 15), A_.subtract)
-        ts(B("AA"), B("K2", 15, 32, 16), 5000.0, A_.is_gt, -4096.0, A_.mult)
-        tt(B("XX", 1, 33), B("XD"), B("NCT"), A_.add)
-        tt(B("XX", 0, 34, 33), B(I, 64, 66), B("AA"), A_.add)
+            ts(B("XD", 32 * q, 32 * q + 32), B("psS", 32 * q, 32 * q + 32), col("K2", 32 * q + 31), A_.subtract)
+        tt(B("XX", 1, 65), B("XD"), B("psP", 64, 128), A_.add)
+        tt(B("XX", 0, 66, 65), B(I, 64, 66), top, A_.subtract)
         for q in (0, 1):
-            red(col(O, 64 + q), B("XX", 17 * q, 17 * q + 17), A_.max)
+            red(col(O, 64 + q), B("XX", 33 * q, 33 * q + 33), A_.max)
         pair_of(B(O, 64, 66), B(O, 66, 68), 2)
-        if t < NR_ - 1:
-            sent = op("g", lambda n=n: _send(g, T, topo, core, to, T["o%d" % n][:], "i%d" % (n + 2), "a%d" % (n + 2)), [B(O)[1]], [], 300.0,
-                      ev=("ls", (n + 1) * _mask(core, to, topo)[1]))
-            op("in%d" % n, None, [], [B("i%d" % (n + 2))[1]], 0.0, P["hop"], ("a%d" % (n + 2), arr), [sent])
+        send("a", n)
 
-        tt(B("EQ", 0, 130, 129), B("AA"), B("PC", 5, 7), A_.add)
-        tt(B("PK"), B("PR2", 0, 2), B("EQ", 0, 130, 129), A_.max)
+        tt(B("PK"), B("PC", 5, 7), top, A_.subtract)
+        tt(B("EQ", 0, 130, 129), B("PR2", 0, 2), B("PK"), A_.max)
         for q in (0, 1):
-            ts(B("XH", 32 * q, 32 * q + 32), B("OH"), col("PK", q), A_.mult)
+            if P["xh"] == "s" and n < 9:
+                act(B("XH", 32 * q, 32 * q + 32), B("OH"), col("EQ", 129 * q), 0.0)
+            else:
+                ts(B("XH", 32 * q, 32 * q + 32), B("OH"), col("EQ", 129 * q), A_.mult)
         for q in (0, 1):
             mms(B("psP", 64 * q, 64 * q + 64), [(IDN, B("FAR", 64 * q, 64 * q + 64)), (B("B32"), B("XH"))])
         for q in (0, 1):
-            ts(B("EQ", 64 * q + 1, 64 * q + 65), B("psP", 64 * q, 64 * q + 64), col("PK", q), A_.is_equal, col("PC", 5 + q), A_.mult)
-        scan(B("DV", 0, 130), B("MK2"), B("EQ"), 0.0, A_.mult, A_.max)
-        ts(B("DV", 194, 260, 65), B("DV", 64, 130, 65), 1.0625, A_.mult)
-        tt(B("EE"), B(O, 64, 68), B("DV", 64, 260, 65), A_.max)
-        for x in range(4):
-            mm(B("psE", 2 * x, 2 * x + 2), B("R%d" % (x % 2)), B("EE", x // 2 * 2, x // 2 * 2 + 2), True, True)
+            ts(B("EQ", 64 * q + 1, 64 * q + 65), B("psP", 64 * q, 64 * q + 64), col("EQ", 129 * q), A_.is_equal, col("PC", 5 + q), A_.mult)
+        scan(B("DV"), B("MK2"), B("EQ"), 0.0, A_.mult, A_.max)
+        mm(B("psE", 0, 8), IDN, B(U, 512, 520), True, False)
+        for w in range(3):
+            for x in range(4):
+                r = (B(O, 64 + x // 2 * 2, 66 + x // 2 * 2), B("PR2", 0, 2), B("DV", 64, 130, 65))[w]
+                mm(B("psE", 2 * x, 2 * x + 2), B(("R%d", "RN%d", "RP%d")[w] % (x % 2)), r, False, w == 2 and x == 3)
         vcopy(B("EL"), B("psE", 0, 8))
-        ts(B("ZE", 0, 64), val, 32.0, A_.add, 255.0, A_.min, B("EL", 0, 4))
+        if P["up"] == "s" and n < 9:
+            gat("s", B("ZF"), val, B("EL", 0, 4), F.Relu, 223.0, scale=-1.0)
+            act(B("ZE", 0, 64), B("ZF"), -1.0, 255.0)
+        else:
+            ts(B("ZE", 0, 64), val, 32.0, A_.add, 255.0, A_.min, B("EL", 0, 4))
         if P["down"] == "s" and n < 9:
             gat("s", B("ZE", 64, 128), val, B("EL", 4, 8), F.Relu, -32.0)
         else:
@@ -462,18 +510,15 @@ def rank_program(g, core, T, topo):
         vput(val, B("EL"), B("ZE"))
 
         if t < NR_ - 1:
-            c = col("psE", 0)
-            mms(c, [(B("B32"), col("AA", q)) for q in (0, 1)])
-            if P["par"] == "s":
-                act(col("TB", 0), c, -0.49994 / 4096, MAGIC)
-                act(col("TB", 1), col("TB", 0), 65536.0, -65536.0 * MAGIC)
-                act(col("TB", 2), c, 8.0, col("TB", 1), F.Identity)
-                act(B("THK%d" % s, 0, 32, 16), B("KB", 2 * t + 2, 2 * t + 4), 1.0, col("TB", 2), F.Identity)
+            if P["aa"] == "s":
+                act(B("AA"), top, 1.0, 0.0, F.Sign)
             else:
-                ts(col("TI", 0), c, -1.0 / 4096, A_.mult)
-                ts(col("TI", 1), col("TI", 0), 1, A_.bitwise_and)
-                ts(col("TB", 0), col("TI", 1), float(AT[t + 1]), A_.add, -32768.0, A_.mult)
-                ts(B("THK%d" % s, 0, 32, 16), B("KB", 0, 2), col("TB", 0), A_.add)
+                ts(B("AA"), top, 1.0, A_.min)
+            for x in range(4):
+                mms(col("psE", x), [(B("B32"), col("AA", q)) for q in (0, 1)])
+            ts(B("TI", 0, 4), B("psE", 0, 4), 32768.0, A_.mult)
+            ts(B("TI", 4, 8), B("TI", 0, 4), 32768, A_.bitwise_and)
+            tt(B("THK%d" % s, 0, 64, 16), B("KB", 4 * t + 4, 4 * t + 8), B("TI", 4, 8), A_.subtract)
         else:
             rows = [(T.yv[32 * a + 16 * s:32 * a + 16 * s + 16, :], T["VAL%d" % s][32 * a:32 * a + 16, 0:2048]) for a in range(4)]
             dmas("y", rows[:4 - 2 * s], [val[1]], [], "stv%d" % s)
@@ -484,8 +529,8 @@ def rank_program(g, core, T, topo):
 
     turn(B("GU"), B("GT"))
     vput(B("YCD"), B("LC"), B("GU"))
-    dmas("y", [(T.yc[:], T.YCD[:, 0:64])], [B("YCD")[1]], [], "stc")
-    dmas("s", [(T.yd[:], T.YCD[:, 64:128])], [B("YCD")[1]], [], "std")
+    dmas("y", [(T.yc[:], T.YCD[:, 64:128])], [B("YCD")[1]], [], "stc")
+    dmas("s", [(T.yd[:], T.YCD[:, 0:64])], [B("YCD")[1]], [], "std")
     for h in (0, 1):
         mms(B("psR", 2 * h, 2 * h + 2), [(move(h, s), B("o%d" % (8 + s), 64, 66)) for s in (0, 1)])
     vcopy(B("YL"), B("psR", 0, 4))

from concourse.mybir import dt, AluOpType, AxisListType, ActivationFunctionType

A_ = AluOpType
F = ActivationFunctionType
X_ = AxisListType.X
NR_ = 5
PAR = dict(ch=(2, 2, 2, 2, 2, 2, 2, 1, 1), sunit=0, img="ss", vd=0, ws="vvss", pt="ssssvvvv", pe=60, down="v", ic=(4, 12), vg=(), sc=512, sl=256, i16=1,
           xh="v", up="v", gli=4, gll=1, aa="v",
           cyc=1.0, gat=1.5, put=3.5, fix=0, wake=100, xw=100, hop=4800, dma=4000, slack=30, it=1, gc=(4, 4, 4, 4, 4, 4, 4, 2, 2))
VW = 2320
BIG = 1.0e9
MAGIC = 12582912.0

SCRATCH = {}
_POS = {}
for _d, _names, _packed in (
        ("int32", "GEN 1024 XCD 128 XL 4 TI 8", "PI 6 LC0 8 LZ0 2"),
        ("float32", "PT0 2048 PT1 2048 IMG 512 IMT0 544 IMT1 544 THK0 64 THK1 64 K1 64 NCT 64 K2 64 XD 64 XX 66 U4 4 PK 2 EQ 130 TB 4 "
                    "GT 128 GU 128 YCD 128 YL 4", "PC 16 B64 64 IX0 32 KB 20 TH2 64 LN 64 KE 64 KF 64"),
        ("bfloat16", "VAL0 %d VAL1 %d W0 8704 W1 8704 SB 8208 YB 8192 U0 544 U1 544 UC 32 WS 512 ZU 2048 AA 2 DF 64 ZF 64 XV 64 LE 32 ZE 128" % (VW, VW),
         "MSK 1024 ONE 160 NEG 144 B1 128 BW 128 BP 128 BN 128 IW 160 IW0 160 IW1 160 SL1 144 SL2 144 SEL 144 R0 128 R1 128 RM0 128 RM1 128 "
         "RN0 128 RN1 128 RP0 128 RP1 128 TW0 128 TW1 128 B2 128 B32 128 OH 32 KC0 64 KC 64 FAR 128 ZC 64 MK2 130"),
        ("float16", "G16 1024 A16 1024 FX 128 FT 128 ML 8 IDX 64 PR2 4 XH 64 DV 130 CD 64 IH 512 IT 512", ""),
        ("uint16", "LC 8 LL 4 CU 32 LI0 512 LI1 512 LW 32 LU 2 LZ 2 EL 8", "")):
    _w, _c = _names.split(), 0
    for _i in range(0, len(_w), 2):
        SCRATCH[_w[_i]] = ("sbuf", [128, int(_w[_i + 1])], _d)
    _w = _packed.split()
    for _i in range(0, len(_w), 2):
        _POS[_w[_i]] = ("pk" + _d, _c, int(_w[_i + 1]))
        _c += (int(_w[_i + 1]) + 31) // 32 * 32
    if _c:
        SCRATCH["pk" + _d] = ("sbuf", [128, _c], _d)
for _n in "psD0 psD1 psK0 psK1 psS psR psP psE".split():
    SCRATCH[_n] = ("psum", [128, 512], "float32")
SEMAPHORES = "vc sc tc gc ls ldg0 ldg1 ldc ldl ldv0 ldv1 stv0 stv1 stw1 stc std stl".split()
for _n in range(2 * NR_):
    SCRATCH["i%d" % _n] = ("sbuf", [128, 68], "float16")
    SCRATCH["o%d" % _n] = ("sbuf", [128, 68], "float16")
    if _n > 1:
        SEMAPHORES += ["d%d" % _n, "a%d" % _n]
PART = {"d": (0, 32), "a": (32, 68)}


def _route(r, T, topo):
    s, d = T.cores[r], T.cores[(r + 3) % len(T.cores)]
    if topo.may_write(s, d):
        return s, None, d
    own = [c for c in topo.cores_of(s) if c not in T.cores and topo.may_write(c, d)]
    own.sort(key=lambda c: (topo.die(c) != topo.die(s), c))
    return s, own[0], d


def _mask(src, dst, topo):
    return topo.mask(src, dst), len(topo.engines(src, dst))


def _send(g, T, topo, core, dst, src, part, n):
    rid, pid = topo.addr(dst, core)
    m, k = _mask(core, dst, topo)
    c0, c1 = PART[part]
    g.remote_dma(T["i%d" % n][:, c0:c1], T[src][:, c0:c1], T.sem["%s%d" % (part, n)], T.sem["ls"], pid, rid, m)
    return k


def _relay(g, core, T, topo):
    for r in range(len(T.cores)):
        s, h, d = _route(r, T, topo)
        if h != core:
            continue
        tot = 0
        for n in range(2, 2 * NR_ + 1):
            for part, x in (("d", n), ("a", n - 1)):
                if 2 <= x < 2 * NR_:
                    g.wait_ge(T.sem["%s%d" % (part, x)], _mask(s, h, topo)[1])
                    tot += _send(g, T, topo, core, d, "i%d" % x, part, x)
        g.wait_ge(T.sem["ls"], tot)


def _meet(a, b):
    if a[0] > b[-1] or b[0] > a[-1]:
        return False
    return (a.step == 1 and b.step == 1) or any(x in b for x in a)


def _inside(a, b):
    return a == b or (b.step == 1 and b[0] <= a[0] and a[-1] <= b[-1])


_DONE = {}


def _order(calls):
    if len(calls) in _DONE:
        return _DONE[len(calls)]
    P = PAR
    deps, users = [c["deps"] for c in calls], [[] for c in calls]
    for i, c in enumerate(calls):
        for d in c["deps"]:
            users[d].append(i)

    def gap(i, u):
        i, u = min(i, u), max(i, u)
        same = calls[i]["q"] == calls[u]["q"] and (calls[i]["q"] == "t" or i in calls[u]["free"])
        return 0.0 if same else calls[i]["late"] + P["wake" if calls[i]["q"] == calls[u]["q"] else "xw"]

    def run(pre, post, way):
        left, at, end = [len(x) for x in pre], [0.0] * len(calls), [0.0] * len(calls)
        ready = {c["q"]: [] for c in calls}
        for i, c in enumerate(calls):
            if not left[i]:
                ready[c["q"]].append(i)
        free, out = {q: 0.0 for q in ready}, []
        while len(out) < len(calls):
            now, q = min((max(free[q], min(at[i] for i in ready[q])), q) for q in ready if ready[q])
            i = max((i for i in ready[q] if at[i] <= now + P["slack"]), key=lambda i: (way[i], -i))
            ready[q].remove(i)
            out.append(i)
            end[i] = free[q] = max(now, at[i]) + calls[i]["busy"]
            for u in post[i]:
                at[u] = max(at[u], free[q] + gap(i, u))
                left[u] -= 1
                if not left[u]:
                    ready[calls[u]["q"]].append(u)
        return out, end
    way = [0.0] * len(calls)
    for i in reversed(range(len(calls))):
        way[i] = calls[i]["busy"] + max([way[u] + gap(i, u) for u in users[i]], default=calls[i]["late"])
    for x in range(P["it"]):
        way = run(users, deps, run(deps, users, way)[1])[1]
    _DONE[len(calls)] = run(deps, users, way)[0]
    return _DONE[len(calls)]


def rank_program(g, core, T, topo):
    rank = T.rank_of(core)
    if rank is None:
        return _relay(g, core, T, topo)
    MT, AT = (12, 18, 14, 22, 16), (10, 8, 9, 6, 8)
    P = PAR
    eng = {"v": g.vector, "s": g.scalar, "t": g.tensor, "g": g, "y": g.sync}
    V, S, TE = g.vector, g.scalar, g.tensor
    calls, hist = [], {}

    def op(q, fn, reads, writes, busy, late=0.0, ev=None, after=()):
        me, deps = len(calls), set(after)
        for keys, wr in ((reads, False), (writes, True)):
            for key, r in keys:
                for h in hist.get(key, ()):
                    if (wr or h[1] or (key[:2] == "ps" and h[3] != q)) and _meet(r, h[0]):
                        deps.add(h[2])
        for keys, wr in ((reads, False), (writes, True)):
            for key, r in keys:
                L = hist.setdefault(key, [])
                if wr:
                    L[:] = [h for h in L if not _inside(h[0], r)]
                L.append((r, wr, me, q))
        deps.discard(me)
        calls.append(dict(q=q, fn=fn, deps=deps, free=set(after), busy=busy, late=late, ev=ev))
        return me

    def issue():
        cnt, total, known, clock = {}, {}, {q: {} for q in eng}, {}
        for i in _order(calls):
            c = calls[i]
            q = c["q"]
            if q in eng:
                for d in sorted(c["deps"], key=lambda d: -calls[d]["at"]):
                    if calls[d]["q"] == q == "t" or d in c["free"]:
                        continue
                    s, n = calls[d]["ev"]
                    if known[q].get(s, 0) < n:
                        eng[q].wait_ge(T.sem[s], n)
                        for x, m in list(clock[d].items()) + [(s, n)]:
                            known[q][x] = max(known[q].get(x, 0), m)
                clock[i] = dict(known[q])
                if c["ev"] is None:
                    cnt[q] = cnt.get(q, 0) + 1
                    c["ev"] = (q + "c", cnt[q])
                    c["fn"]().then_inc(T.sem[q + "c"], 1)
                else:
                    c["fn"]()
            else:
                clock[i] = {}
            c["at"] = len(clock)
            total[c["ev"][0]] = max(total.get(c["ev"][0], 0), c["ev"][1])
        for s in total:
            g.wait_ge(T.sem[s], total[s])

    def dmas(q, pairs, reads, writes, sem, late=None, after=()):
        def fn():
            for o, s in pairs:
                eng[q].dma_start(o, s).then_inc(T.sem[sem], 16)
        return op(q, fn, reads, writes, 60.0 * len(pairs), late or P["dma"], (sem, 16 * len(pairs)), after)

    def B(name, c0=0, c1=None, st=1):
        name, off, w = _POS[name] if name in _POS else (name, 0, SCRATCH[name][1][1])
        c0, c1 = off + c0, off + (w if c1 is None else c1)
        ap = T[name][:, c0:c1] if st == 1 else T[name][:, c0:c1:st]
        r = range(c0, c1, st)
        return ap, (name, range(512) if name[:2] == "ps" else r), len(r), 2 if "16" in SCRATCH[name][2] else 4

    def col(name, c):
        return B(name, c, c + 1)

    def cost(o, *ins):
        return P["fix"] + P["cyc"] * max(64, o[2] * (0.5 if max(x[3] for x in (o,) + ins) == 2 else 1.0))

    def picked(n, rate="gat"):
        return 60 + P["cyc"] * n * P[rate]

    def vcopy(o, i):
        op("v", lambda: V.tensor_copy(o[0], i[0]), [i[1]], [o[1]], cost(o, i))

    def gat(q, o, win, off, f=F.Copy, bias=0.0, after=(), scale=1.0):
        if q == "s":
            return op("s", lambda: S.activation(o[0], win[0].indirect(off[0]), f, bias=bias, scale=scale), [win[1], off[1]], [o[1]],
                      picked(o[2]), after=after)
        op("v", lambda: V.tensor_copy(o[0], win[0].indirect(off[0])), [win[1], off[1]], [o[1]], picked(o[2]))

    def vput(win, off, i):
        op("v", lambda: V.tensor_copy(win[0].indirect(off[0]), i[0]), [off[1], i[1]], [win[1]], picked(i[2], "put"))

    def act(o, i, scale, bias, f=F.Copy):
        b, c = [x[0] if isinstance(x, tuple) else x for x in (bias, scale)]
        op("s", lambda: S.activation(o[0], i[0], f, bias=b, scale=c), [x[1] for x in (i, bias, scale) if isinstance(x, tuple)], [o[1]],
           P["fix"] + P["cyc"] * max(64, o[2]))

    def tt(o, a, b, f):
        op("v", lambda: V.tensor_tensor(o[0], a[0], b[0], f), [a[1], b[1]], [o[1]], P["fix"] + P["cyc"] * max(64, o[2] * (1 if "ps" in (a[1][0][:2], b[1][0][:2]) else 2)))

    def ts(o, a, s1, f1, s2=None, f2=None, off=None):
        rd = [a[1]] + [s[1] for s in (s1, s2, off) if isinstance(s, tuple)]
        x1 = s1[0] if isinstance(s1, tuple) else s1
        x2 = s2[0] if isinstance(s2, tuple) else s2
        args = (x1, None, f1) if f2 is None else (x1, x2, f1, f2)
        op("v", lambda: V.tensor_scalar(o[0], a[0].indirect(off[0]) if off else a[0], *args), rd, [o[1]], picked(o[2]) if off else cost(o, a))

    def red(o, a, f):
        op("v", lambda: V.tensor_reduce(o[0], a[0], X_, f), [a[1]], [o[1]], cost(o))

    def scan(o, a, b, init, f0, f1):
        op("v", lambda: V.tensor_tensor_scan(o[0], a[0], b[0], init, f0, f1), [a[1], b[1]], [o[1]], cost(o, a, b))

    def turn(o, i):
        op("v", lambda: V.transpose(o[0], i[0]), [i[1]], [o[1]], cost(o))

    def ms(o, c):
        op("v", lambda: V.memset(o[0], c), [], [o[1]], cost(o))

    def mm(o, l, r, st, sp, after=()):
        op("t", lambda: TE.matmul(o[0], l[0], r[0], st, sp), [l[1], r[1]], [o[1]], P["cyc"] * max(64, r[2]), P["pe"], after=after)

    def mms(o, pairs):
        for i, (l, r) in enumerate(pairs):
            mm(o, l, r, i == 0, i == len(pairs) - 1)

    def iota(o, pat, base, ch, whole=False):
        kw = {} if whole else dict(allow_small_or_imprecise_dtypes=True)
        op("g", lambda: g.iota(o[0], pat, base, ch, **kw), [], [o[1]], 150 + 2 * P["cyc"] * o[2])

    def asel(o, i, pat, f, base, ch):
        op("g", lambda: g.affine_select(o[0], i[0], pat, f, 0.0, base, ch), [i[1]], [o[1]], 200 + 2 * P["cyc"] * o[2])

    def gcopy(o, i):
        asel(o, i, [[0, o[2]]], A_.is_equal, 0, 0)

    def move(h, l):
        c = 16 + 16 * (h - l)
        return B("IW%d" % h, c, c + 128)

    IDN = B("IW", 16, 144)

    x = [dmas("s", [(T.GEN[:, 0:512], T.gen[:, 0:512])], [], [B("GEN", 0, 512)[1]], "ldg0", P["dma"] - 800)]
    dmas("s", [(T.GEN[:, 512:1024], T.gen[:, 512:1024])], [], [B("GEN", 512, 1024)[1]], "ldg1", P["dma"] - 400, x)
    x = [dmas("y", [(T.XL[:], T.lit[:])], [], [B("XL")[1]], "ldl", P["dma"] - 800)]
    x = [dmas("y", [(T.XCD[:, 0:64], T.par[:]), (T.XCD[:, 64:128], T.cla[:])], [], [B("XCD")[1]], "ldc", P["dma"] - 400, x)]
    for s in (0, 1):
        x = [dmas("y", [(T["VAL%d" % s][16 * x:16 * x + 16, 0:2048], T.val[32 * (x // 2) + 16 * s:32 * (x // 2) + 16 * s + 16, :]) for x in range(8)],
                  [], [B("VAL%d" % s, 0, 2048)[1]], "ldv%d" % s, P["dma"] + 1000 + 2000 * s, x)]

    iota(col("PI", 0), [[1, 1]], 0, 1, True)
    ms(B("ONE"), 1.0)
    asel(B("IW"), B("ONE"), [[-1, 160]], A_.is_equal, 16, 1)
    iota(B("LC0"), [[64, 2], [1, 2], [2, 2]], 0, 0, True)
    asel(B("B1"), B("ONE", 0, 128), [[-16, 8], [0, 16]], A_.is_ge, 0, 1)
    asel(B("BW"), B("B1"), [[16, 8], [0, 16]], A_.is_ge, 15, -1)
    ms(B("NEG"), -32768.0)
    for c, m in ((1, 15), (2, 16), (3, 31), (4, 7), (5, 8)):
        ts(col("PI", c), col("PI", 0), m, A_.bitwise_and)
    vcopy(B("PC", 11, 13), B("PI", 2, 4))
    vcopy(col("PC", 13), col("PI", 5))
    for h in (0, 1):
        ts(col("PC", 1 + h), col("PI", 2), 16.0 * h, A_.is_equal)
        ts(col("PC", 3 + h), col("PI", 3), col("PC", 11), A_.add, 16.0 * h, A_.add)
    ts(B("PC", 5, 7), B("PC", 3, 5), 2.0, A_.mult, 2048.0, A_.add)
    for c, m in ((7, 4.0), (8, 512.0), (9, 16.0)):
        ts(col("PC", c), col("PI", 1), m, A_.mult)
    ts(B("LC"), B("LC0"), col("PC", 7), A_.add)
    for h in (0, 1):
        ts(B("IW%d" % h), B("IW"), col("PC", 1 + h), A_.mult)
        tt(B("R%d" % h), move(h, 0), move(h, 1), A_.add)
        for x, m in (("RM", -0.25), ("RN", -2.0), ("RP", 2.0)):
            ts(B("%s%d" % (x, h)), B("R%d" % h), m, A_.mult)
        ts(B(("BP", "BN")[h]), B("BW"), 4096.0 * (1 - 2 * h), A_.mult)
        ms(B("ZC", 32 * h, 32 * h + 32), 8.5 * 4096.0 * (2 * h - 1))
    iota(B("B64"), [[1, 64]], 0, 0)
    iota(B("IX0"), [[16, 32]], 0, 0)
    iota(B("LN"), [[16, 2], [32, 2], [1, 16]], 0, 0)
    iota(B("KC0"), [[0, 2], [-2048, 16], [0, 2]], -2048, 0)
    iota(B("KE"), [[0, 32], [8, 2]], 0, 0)
    ts(B("KF"), B("KE"), col("PC", 13), A_.not_equal, -2.0 ** 30, A_.mult)
    tt(B("KC"), B("KC0"), B("KF"), A_.add)
    iota(B("LZ0"), [[1024, 2]], 0, 1, True)
    ts(col("PC", 10), col("PI", 4), 128.0, A_.mult)
    ts(B("LZ"), B("LZ0"), col("PC", 10), A_.add)
    for h in (0, 1):
        asel(B("TW%d" % h), B("ONE", 0, 128), [[-32, 4], [-1, 16], [0, 2]], A_.is_equal, -16 * h, 1)
    asel(B("SL1"), B("NEG"), [[-16, 9], [0, 16]], A_.is_ge, 0, 1)
    asel(B("SL2"), B("SL1"), [[16, 9], [0, 16]], A_.is_ge, 15, -1)
    asel(B("SEL"), B("SL2"), [[0, 9], [1, 16]], A_.is_equal, -15, 0)
    asel(B("B2"), B("ONE", 0, 128), [[-32, 4], [0, 32]], A_.is_ge, 0, 1)
    asel(B("B32"), B("B2"), [[32, 4], [0, 32]], A_.is_ge, 31, -1)
    for c in range(0, 2048, 1024):
        iota(B("ZU", c, c + 1024), [[0, 1024]], 0, 0)
    for s in (0, 1):
        iota(B("W%d" % s, 8192, 8704), [[0, 512]], 0, 0)
        iota(B("U%d" % s, 512, 544), [[0, 32]], 0, 0)
    iota(B("YCD"), [[0, 128]], 0, 0)
    ms(B("MSK", 0, P["sc"]), 1.0)
    ms(B("MSK", 15, P["sc"], 16), -1.0)
    ms(B("SB", 0, 1), 0.0)
    ms(B("TH2"), 1.0)
    ms(B("TH2", 0, 64, 32), 0.0)
    ms(B("MK2"), 1.0)
    ms(B("MK2", 0, 130, 65), 0.0)
    ts(B("IDX", 0, 32), B("IX0"), 0.0, A_.mult)
    ts(B("IDX", 32, 64), B("IX0"), col("PC", 8), A_.add)
    ms(B("KB", 0, 2), 0.0)
    ts(B("KB", 2, 4), B("IX0", 0, 32, 16), 8192.0, A_.add, col("PC", 9), A_.add)
    ts(B("OH"), B("B64", 0, 32), col("PC", 12), A_.is_equal)
    for s in (0, 1):
        ms(B("VAL%d" % s, 2048, VW), 0.0)
        ms(B("THK%d" % s), -BIG)
        ts(B("FAR", 64 * s, 64 * s + 64), B("LN"), col("PC", 3 + s), A_.is_ge, 4096.0, A_.mult)
        ts(B("THK%d" % s, 0, 64, 16), B("KB", 0, 4), -32768.0 * AT[0], A_.add)
    for t in range(1, NR_):
        act(B("KB", 4 * t, 4 * t + 4), B("KB", 0, 4), 1.0, -32768.0 * AT[t])

    def pair_of(l, lp, n):
        ts(B("PR2", 0, n), l, 0.5, A_.mult, 1023.8, A_.add)
        ts(B("U4", 0, n), B("PR2", 0, n), 4.0, A_.mult, -4095.0, A_.add)
        tt(lp, B("U4", 0, n), l, A_.subtract)

    gat("v", B("FX"), B("XCD"), B("LC"))
    turn(B("FT"), B("FX"))
    vcopy(B("ML", 0, 4), B("XL"))
    pair_of(B("ML", 0, 4), B("ML", 4, 8), 4)
    for x in range(4):
        c = 4 * (x % 2)
        mms(B("psE", 2 * x, 2 * x + 2), [(move(x // 2, h), B("ML", c + 2 * h, c + 2 * h + 2)) for h in (0, 1)])
    for s in (0, 1):
        vcopy(B("i%d" % s, 64, 68), B("psE", 4 * s, 4 * s + 4))
        for x in range(4):
            vcopy(B("i%d" % s, 16 * x, 16 * x + 16), B("FT", 32 * x + 16 * s, 32 * x + 16 * s + 16))
    for c in (0, 512):
        vcopy(B("G16", c, c + 512), B("GEN", c, c + 512))
        ts(B("A16", c, c + 512), B("G16", c, c + 512), 0.5, A_.mult, 1023.8, A_.add)

    def maps(s, banks, after):
        for c in (0, 1):
            c0, c1, ev, od = 512 * c, 512 * c + 512, B(banks[2 * c]), B(banks[2 * c + 1])
            mm(ev, B("R%d" % s), B("G16", c0, c1), True, True, after)
            mm(od, B("RM%d" % s), B("G16", c0, c1), True, False, after)
            mm(od, B("R%d" % s), B("A16", c0, c1), False, True)
            for x, (i, a, b) in enumerate(((ev, 1.0, 0.0), (od, 4.0, -4095.0))):
                o = B("PT%d" % s, 2 * c0 + x, 2 * c1, 2)
                if P["pt"][4 * s + 2 * c + x] == "v":
                    ts(o, i, a, A_.mult, b, A_.add)
                else:
                    act(o, i, a, b)
    maps(0, ("psS", "psP", "psD1", "psK1"), ())

    src, hand, dst = _route(rank, T, topo)
    to = hand if hand is not None else dst
    into = _route((rank - 3) % len(T.cores), T, topo)
    arr = _mask(into[1] if into[1] is not None else into[0], core, topo)[1]
    edge = [sum(P["ch"][:c]) for c in range(len(P["ch"]) + 1)]

    def send(part, n):
        if n + 2 < 2 * NR_:
            x = op("g", lambda: _send(g, T, topo, core, to, "o%d" % n, part, n + 2), [B("o%d" % n, *PART[part])[1]], [], 300.0,
                   ev=("ls", 4 * (NR_ - 1) * _mask(core, to, topo)[1]))
            op(part + str(n), None, [], [B("i%d" % (n + 2), *PART[part])[1]], 0.0, P["hop"], ("%s%d" % (part, n + 2), arr), [x])

    before = []
    for n in range(2 * NR_):
        s, t, I, O = n % 2, n // 2, "i%d" % n, "o%d" % n
        val, W, U, IMT, LI = B("VAL%d" % s), "W%d" % s, "U%d" % s, "IMT%d" % s, "LI%d" % s

        (gcopy if P["gll"] else vcopy)(B("LL"), B(I, 64, 68))
        gat("v", B("XV"), val, B("LL"))
        tt(B("LE"), B("XV", 0, 32), B("XV", 32, 64), A_.is_lt)
        mm(B("psR", 0, 64), IDN, B("ZC"), True, False)
        mm(B("psR", 0, 32), B("BP"), B("LE"), False, False)
        mm(B("psR", 32, 64), B("BN"), B("LE"), False, True)
        tt(B("CD"), B(I, 0, 64), B("psR", 0, 64), A_.min)
        tt(B(O, 0, 32), B("CD", 0, 32), B("CD", 32, 64), A_.max)
        send("d", n)
        for l in (0, 1):
            mms(B("psR", l, 32, 2), [(move(l, h), B(O, 16 * h, 16 * h + 16)) for h in (0, 1)])
        vcopy(B("CU"), B("psR", 0, 32))
        asel(B(IMT, 512, 544), B(I, 0, 32), [[0, 32]], A_.is_equal, 0, 0)
        p0 = 0
        for w in P["ic"]:
            c0, c1 = 32 * p0, 32 * (p0 + w)
            a, b = ("IH", "IT") if P["i16"] else ("IMG", IMT)
            gat(P["img"][p0 > 0], B(a, c0, c1), B("PT%d" % s), B("CU", 2 * p0, 2 * (p0 + w)))
            turn(B(b, c0, c1), B(a, c0, c1))
            (gcopy if p0 >= P["gli"] else vcopy)(B(LI, c0, c1), B(b, c0, c1))
            p0 += w
        if P["i16"]:
            asel(B(IMT, 0, 512), B("IT"), [[0, 512]], A_.is_equal, 0, 0)

        K = B("psK%d" % s, 0, 64)
        mm(K, IDN, B("IDX"), True, False)
        p0 = 0
        for c, w in enumerate(P["gc"]):
            x = gat("v" if (n, c) in P["vg"] or c in P["vg"] else "s", B(W, 256 * p0, 256 * (p0 + w)), val, B(LI, 16 * p0, 16 * (p0 + w)), after=before)
            before = before if x is None else [x]
            if n == c == 0:
                maps(1, ("psS", "psP", "psE", "psK1"), before)
            p0 += w
        for c in range(len(P["ch"])):
            p0, p1 = edge[c], edge[c + 1]
            c0, c1, d = 512 * p0, 512 * p1, B("psD%d" % (c & 1), 0, 32 * (p1 - p0))
            w = P["sl"] if p1 == 16 else min(P["sc"], c1 - c0)
            for x in range(c0, c1, w):
                y = x + w
                scan(B("SB", x + 1, y + 1), B(W, x, y), B("MSK", 0, w), 0.0, A_.max, A_.mult)
                scan(B("YB", x, y), B(W, x, y), B("SB", x, y), 0.0, A_.max, A_.min)
            if c < len(P["ch"]) - P["vd"]:
                mms(d, [(IDN, B("SB", c0 + 16, c1 + 1, 16)), (IDN, B("YB", c0 + 15, c1, 16))])
            else:
                d = B("DF", 0, 32 * (p1 - p0))
                tt(d, B("SB", c0 + 16, c1 + 1, 16), B("YB", c0 + 15, c1, 16), A_.add)
            if c < P["sunit"]:
                act(B(U, 32 * p0, 32 * p1), d, -1000.0, -1000.0 * (MT[t] + 0.5), F.Sigmoid)
            else:
                ts(B(U, 32 * p0, 32 * p1), d, -float(MT[t]), A_.is_lt)
            for p in range(p0, p1):
                for x in (0, 32):
                    mm(B("psK%d" % s, x, x + 32), B("SEL", 15 - p, 143 - p), B(U, 32 * p, 32 * p + 32), False, p == 15 and x == 32)

        scan(B("K1"), B("THK%d" % s), K, -BIG, A_.max, A_.min)
        for q in (0, 1):
            ts(col("LU", q), col("K1", 16 * q + 47), col("K1", 16 * q + 15), A_.subtract, 1.0 / 16, A_.mult)
        for q in (0, 1):
            ts(B("LW", 16 * q, 16 * q + 16), B("B64", 0, 16), col("K1", 16 * q + 47), A_.add, col("K1", 16 * q + 15), A_.subtract)

        ts(B("UC"), B(U), 32768.0, A_.mult, off=B("LU"))
        vput(B("ZU"), B("LZ"), B("UC"))
        gat("v", B(O, 32, 64), B(IMT), B("LU"))
        for x in range(4):
            mm(B("psP", 16 * x, 16 * x + 16), B("TW%d" % (x % 2)), B(O, 32 + 16 * (x // 2), 48 + 16 * (x // 2)), True, True)
        turn(B("psP", 64, 128), B("psP", 0, 64))
        mm(B("psS", 0, 64), IDN, B("KC"), True, False)
        for q in (0, 1):
            gat(P["ws"][q + 2 * (n == 9)], B("WS", 256 * q, 256 * q + 256), B(W), B("LW", 16 * q, 16 * q + 16))
            for y in range(8 * q, 8 * q + 8):
                mm(B("psS", 32 * q, 32 * q + 32), B("ZU", 128 * y, 128 * y + 128), B("WS", 248 * q + y, 256 * q + 256, 8), False, y == 15)
        scan(B("K2"), B("TH2"), B("psS", 0, 64), 0.0, A_.mult, A_.max)
        top = B("K2", 31, 64, 32)
        for q in (0, 1):
            ts(B("XD", 32 * q, 32 * q + 32), B("psS", 32 * q, 32 * q + 32), col("K2", 32 * q + 31), A_.subtract)
        tt(B("XX", 1, 65), B("XD"), B("psP", 64, 128), A_.add)
        tt(B("XX", 0, 66, 65), B(I, 64, 66), top, A_.subtract)
        for q in (0, 1):
            red(col(O, 64 + q), B("XX", 33 * q, 33 * q + 33), A_.max)
        pair_of(B(O, 64, 66), B(O, 66, 68), 2)
        send("a", n)

        tt(B("PK"), B("PC", 5, 7), top, A_.subtract)
        tt(B("EQ", 0, 130, 129), B("PR2", 0, 2), B("PK"), A_.max)
        for q in (0, 1):
            if P["xh"] == "s" and n < 9:
                act(B("XH", 32 * q, 32 * q + 32), B("OH"), col("EQ", 129 * q), 0.0)
            else:
                ts(B("XH", 32 * q, 32 * q + 32), B("OH"), col("EQ", 129 * q), A_.mult)
        for q in (0, 1):
            mms(B("psP", 64 * q, 64 * q + 64), [(IDN, B("FAR", 64 * q, 64 * q + 64)), (B("B32"), B("XH"))])
        for q in (0, 1):
            ts(B("EQ", 64 * q + 1, 64 * q + 65), B("psP", 64 * q, 64 * q + 64), col("EQ", 129 * q), A_.is_equal, col("PC", 5 + q), A_.mult)
        scan(B("DV"), B("MK2"), B("EQ"), 0.0, A_.mult, A_.max)
        mm(B("psE", 0, 8), IDN, B(U, 512, 520), True, False)
        for w in range(3):
            for x in range(4):
                r = (B(O, 64 + x // 2 * 2, 66 + x // 2 * 2), B("PR2", 0, 2), B("DV", 64, 130, 65))[w]
                mm(B("psE", 2 * x, 2 * x + 2), B(("R%d", "RN%d", "RP%d")[w] % (x % 2)), r, False, w == 2 and x == 3)
        vcopy(B("EL"), B("psE", 0, 8))
        if P["up"] == "s" and n < 9:
            gat("s", B("ZF"), val, B("EL", 0, 4), F.Relu, 223.0, scale=-1.0)
            act(B("ZE", 0, 64), B("ZF"), -1.0, 255.0)
        else:
            ts(B("ZE", 0, 64), val, 32.0, A_.add, 255.0, A_.min, B("EL", 0, 4))
        if P["down"] == "s" and n < 9:
            gat("s", B("ZE", 64, 128), val, B("EL", 4, 8), F.Relu, -32.0)
        else:
            ts(B("ZE", 64, 128), val, -32.0, A_.add, 0.0, A_.max, B("EL", 4, 8))
        vput(val, B("EL"), B("ZE"))

        if t < NR_ - 1:
            if P["aa"] == "s":
                act(B("AA"), top, 1.0, 0.0, F.Sign)
            else:
                ts(B("AA"), top, 1.0, A_.min)
            for x in range(4):
                mms(col("psE", x), [(B("B32"), col("AA", q)) for q in (0, 1)])
            ts(B("TI", 0, 4), B("psE", 0, 4), 32768.0, A_.mult)
            ts(B("TI", 4, 8), B("TI", 0, 4), 32768, A_.bitwise_and)
            tt(B("THK%d" % s, 0, 64, 16), B("KB", 4 * t + 4, 4 * t + 8), B("TI", 4, 8), A_.subtract)
        else:
            rows = [(T.yv[32 * a + 16 * s:32 * a + 16 * s + 16, :], T["VAL%d" % s][32 * a:32 * a + 16, 0:2048]) for a in range(4)]
            dmas("y", rows[:4 - 2 * s], [val[1]], [], "stv%d" % s)
            if s:
                dmas("s", rows[2:], [val[1]], [], "stw1")
            for x in range(4):
                vcopy(B("GT", 32 * x + 16 * s, 32 * x + 16 * s + 16), B(O, 16 * x, 16 * x + 16))

    turn(B("GU"), B("GT"))
    vput(B("YCD"), B("LC"), B("GU"))
    dmas("y", [(T.yc[:], T.YCD[:, 64:128])], [B("YCD")[1]], [], "stc")
    dmas("s", [(T.yd[:], T.YCD[:, 0:64])], [B("YCD")[1]], [], "std")
    for h in (0, 1):
        mms(B("psR", 2 * h, 2 * h + 2), [(move(h, s), B("o%d" % (8 + s), 64, 66)) for s in (0, 1)])
    vcopy(B("YL"), B("psR", 0, 4))
    dmas("y", [(T.yl[:], T.YL[:])], [B("YL")[1]], [], "stl")
    issue()
